import numpy as np, ml_dtypes
CORES = [3,7,11,15,131,135,139,143]
N = 8
import mx_ref
BF = ml_dtypes.bfloat16
def gentries(a):
    return np.ascontiguousarray(a.reshape(8, 16, -1).transpose(0, 2, 1)).reshape(8, -1)
def gtable(e):
    e = np.asarray(e); return np.ascontiguousarray(e.reshape(8, -1, 16).transpose(0, 2, 1)).reshape(128, -1).astype(np.int32)
def gcols(t, e):
    v = np.concatenate([t.reshape(8, 16, -1, 4), np.zeros((8, 16, 1, 4), BF)], axis=2)
    return np.ascontiguousarray(np.stack([v[g][:, e[g]] for g in range(8)])).reshape(128, -1)
def tile(rs):
    return np.stack(rs, axis=2).reshape(128, -1).astype(BF)
def cut(t, i, w=512):
    return t[:, w * i:w * i + w]
def pick(q, e):
    c = np.concatenate([q[0].reshape(128, -1, 4), np.zeros((128, 1, 4), np.uint8)], axis=1); s = np.concatenate([q[1], np.ones((16, 1), np.uint8)], axis=1)
    return (np.ascontiguousarray(c[:, e].reshape(128, -1)), np.ascontiguousarray(s[:, e]))
def join(*qs):
    return (np.concatenate([q[0] for q in qs], axis=1), np.concatenate([q[1] for q in qs], axis=1))
def put(q, e, v):
    c, s = q[0].reshape(128, -1, 4).copy(), q[1].copy(); c[:, e] = v[0].reshape(128, -1, 4); s[:, e] = v[1]
    return (c.reshape(128, -1), s)
def pk(c, s):
    return (np.ascontiguousarray(c), mx_ref.live(s))
def emit(q):
    return q[0], q[1]
def packed(v, rng):
    q = [mx_ref.quantize(np.ascontiguousarray(v[r])) for r in range(N)]
    return np.stack([a for a, b in q]), np.stack([mx_ref.plane(b, rng) for a, b in q])
def values_of_codes():
    e, c = np.zeros((128, 128, 4), np.float32), np.zeros((128, 2, 4), np.uint8)
    e[np.arange(128), np.arange(128), 0] = 1
    c[:127, :, 0] = np.arange(256).reshape(2, 128).T[:127]
    return mx_ref.matmul(mx_ref.quantize(e.reshape(128, 512).astype(BF)), (c.reshape(128, 8), np.full((16, 2), 127, np.uint8))).T.reshape(-1).astype(np.float64)
CODE_VALUE, SCALE_VALUE = values_of_codes(), 2.0 ** (np.arange(256) - 127.0)
def decode(q):
    return (CODE_VALUE[q[0]].reshape(16, 8, -1, 4) * SCALE_VALUE[q[1]][:, None, :, None] + 0.0).reshape(128, -1).astype(np.float32)
def f(rng, *shape):
    return mx_ref.flush((rng.standard_normal(shape, dtype=np.float32) * np.exp2(rng.integers(-2, 3, shape[:-1] + (1,)))).astype(BF))
def wide(rng, *shape, cols=0):
    v = rng.standard_normal(shape, dtype=np.float32) * np.exp2(rng.integers(-12, 13, shape)).astype(np.float32)
    if cols: v *= np.repeat(np.exp2(rng.integers(-cols, cols + 1, shape[:-2] + (1, shape[-1] // 4))) * (rng.random(shape[:-2] + (1, shape[-1] // 4)) > 0.0625), 4, axis=-1).astype(np.float32)
    return mx_ref.flush(v.astype(BF))
C, B, R = 256, 16, 3
STEP = [3, 6, 4]
def slides(s):
    n = 8 * B
    i = np.arange(n)
    who = np.full((n, 5, 5), -9)
    key = np.full((n, 5, 5), -np.inf, np.float32)
    who[:, :4, :4] = np.arange(16).reshape(4, 4)
    key[:, :4, :4] = s.reshape(n, 4, 4)
    left = np.zeros((4, n), np.int64)
    for k in range(4):
        left[k] = who[:, 0, 0]
        y, c = np.zeros(n, np.int64), np.zeros(n, np.int64)
        for m in range(6):
            right = key[i, y, c + 1] >= key[i, y + 1, c]
            y2, c2 = np.where(right, y, y + 1), np.where(right, c + 1, c)
            go = who[i, y2, c2] >= 0
            j = i[go]
            who[j, y[go], c[go]] = who[j, y2[go], c2[go]]
            key[j, y[go], c[go]] = key[j, y2[go], c2[go]]
            y, c = np.where(go, y2, y), np.where(go, c2, c)
        who[i, y, c] = -1 - k
        key[i, y, c] = -np.inf
    b = np.arange(B)
    w = who[:, :4, :4].reshape(8, B, 16)
    stand = np.where(w >= 0, 16 * b[:, None] + w, C + B * (-1 - w) + b[:, None]).reshape(8, C)
    return (left.reshape(4, 8, B) + 16 * b).transpose(1, 0, 2).reshape(8, 4 * B), stand
def big(v):
    v = v.astype(np.float32)
    v[np.abs(v) < np.float32(2.0 ** -16)] = 0
    return v.astype(BF)
def seats(rng):
    return np.argsort(rng.random((N, 8, C)), axis=2)
def seated(e, a):
    s = np.zeros_like(a)
    np.put_along_axis(s, e, a, axis=2)
    return s
def digits(s):
    return ((s[..., None] >> np.arange(4)) & 1) * np.exp2(np.arange(4.0))
def numbers_of(rng, e):
    return {"x": big(f(rng, N, 128, 4 * C)), "p": np.stack([gtable(e[r]) for r in range(N)]), "u": np.array(f(rng, N, 128, 512)), "v": np.array(f(rng, N, 128, 512))}
def layers(rng, still=()):
    w = big(f(rng, N, 128, 2048)).reshape(N, 8, 16, 4, 8, 16, 4)
    for i in still:
        w[:, :, i] = 0
        w[:, :, :, :, :, i] = 0
    return w.reshape(N, 128, 2048)
def weights(rng, w):
    c, s = packed(np.ascontiguousarray(w).reshape(N, 128, 2048), rng)
    return {"wc": c, "ws": s}
def signs(rng):
    return np.stack([rng.permutation(8) % 2 * 2.0 - 1.0 for r in range(N)])
def setup_inputs(rng):
    return {**numbers_of(rng, seats(rng)), **weights(rng, layers(rng))}
def setup_inputs_ties(rng):
    d = numbers_of(rng, seats(rng))
    e = rng.permutation(N)
    x = d["x"].reshape(N, 8, 16, C, 4)
    for r in range(N):
        k = np.zeros(C, int) if r == e[0] else rng.permutation(C) % 3
        a = x[r][:, :8, :3].copy()
        a[:, :, 2] = 0
        x[r][:, :8] = a[:, :, k]
    x[e[1]] = 0
    u = d["u"].reshape(N, 8, 16, 8, 16, 4)
    k = u.copy()
    u[:, :, :, :, 0] = 0
    for g in range(8): u[:, g, :8, g, 0] = k[:, g, :8, g, 0]
    return {"x": x.reshape(N, 128, 4 * C), "p": d["p"], "u": u.reshape(N, 128, 512), "v": d["v"], **weights(rng, layers(rng, range(8)))}
def setup_inputs_near(rng):
    e = seats(rng)
    d = numbers_of(rng, e)
    x = d["x"].astype(np.float32).reshape(N, 8, 16, C, 4)
    u = d["u"].reshape(N, 128, 128, 4)
    u[:, :, ::16] = 0
    o, c = rng.permutation(N) % 4, signs(rng)
    s = seated(e, np.argsort(rng.random((N, 8, B, 16)), axis=3).reshape(N, 8, C))
    x[:, :, 0] = 0
    x[:, :, 9] = 0
    for r in range(N):
        size = 2.0 ** -23 if o[r] < 2 else 2.0 ** -30
        if o[r] < 2:
            x[r, :, 0, :, 0] = c[r][:, None]
            x[r, :, 9, :, 0] = c[r][:, None] * 2.0 ** -12
            for i in rng.permutation(8)[:4]: x[r, i, 0, rng.integers(C), 0] *= np.float32(2.0 ** 30)
        x[r, :, 8] = digits(s[r]) * (-size if o[r] == 3 else size) + 0.0
        x[r, :, 10:] = rng.integers(4, 8, (8, 6, C, 4)) * rng.choice([-1.0, 1.0], (8, 6, C, 4)) * size
        k = 1.0 if o[r] == 0 else 2.0 ** -30
        for h in range(0, 128, 16):
            u[r, h, h, 0] = k
            u[r, h + 8, h] = k
            u[r, h + 9, h, 0] = k
    return {"x": x.reshape(N, 128, 4 * C).astype(BF), "p": d["p"], "u": u.reshape(N, 128, 512), "v": d["v"], **weights(rng, layers(rng, [0, 8, 9, 10, 11, 12, 13, 14, 15]))}
def setup_inputs_huge(rng):
    d = numbers_of(rng, seats(rng))
    c = np.stack([rng.permutation(C) % 2 * 2.0 - 1.0 for r in range(N)])
    c[rng.permutation(N) < N // 2] = -1
    x = 2.0 ** 30 * (1 - 0.0625 * (rng.random((N, 128, C, 4)) < 0.25)) * c[:, None, :, None]
    u = d["u"].reshape(N, 128, 128, 4)
    a = 2.0 ** 30 * (1 - 0.0625 * (rng.random((N, 128, 8, 4)) < 0.25)) * signs(rng)[:, None, :, None]
    u[:, :, ::16] = a.astype(np.float32).astype(BF)
    w = np.zeros((N, 128, 4, 128, 4), np.float32)
    i = np.arange(128)
    for b in range(4): w[:, i, b, i, b] = -32
    return {"x": x.astype(np.float32).reshape(N, 128, 4 * C).astype(BF), "p": d["p"], "u": u.reshape(N, 128, 512), "v": d["v"], **weights(rng, w.astype(BF))}
def setup_inputs_moves(rng):
    e = seats(rng)
    i = rng.permutation(N)
    e[i[2]] = np.arange(C)
    d = numbers_of(rng, e)
    a = np.arange(16)
    s = np.argsort(rng.random((N, 8, B, 16)), axis=3)
    k = np.argsort(rng.random((N, 8, B)), axis=2) % 4
    k[i[0]], k[i[1]] = 0, 1
    s[k == 0] = a % 4 * 4 + a // 4
    s[k == 1] = a
    x = d["x"].reshape(N, 8, 16, C, 4)
    x[:, :, 8] = digits(seated(e, s.reshape(N, 8, C))).astype(np.float32).astype(BF)
    u = d["u"].reshape(N, 128, 128, 4)
    u[:, :, ::16] = 0
    for h in range(0, 128, 16): u[:, h + 8, h] = 1
    return {"x": x.reshape(N, 128, 4 * C), "p": d["p"], "u": u.reshape(N, 128, 512), "v": d["v"], **weights(rng, layers(rng, range(8, 16)))}
def setup_inputs_spread(rng):
    d = setup_inputs(rng)
    d["x"] = big(wide(rng, N, 128, 4 * C, cols=6))
    return d
def check_inputs(d):
    b = []
    for k in ("x", "u", "v"):
        a = np.abs(d[k].astype(np.float32))
        if not (np.isfinite(a).all() and ((a == 0) | (a >= 2.0 ** -30) & (a <= 2.0 ** 30)).all()): b.append("a value of " + k)
    none, least, most = [emit(mx_ref.quantize(np.full((128, 16), k, np.float32).astype(BF)))[1][0, 0] for k in (0.0, 2.0 ** -30, 2.0 ** 30)]
    for r in range(N):
        if not (np.sort(gentries(d["p"][r]), axis=1) == np.arange(C)).all(): b.append("p: a group's entries aren't all columns, each once")
        if ((d["wc"][r] == 0x7F) | (d["wc"][r] == 0xFF)).any(): b.append("wc: a code that is no number")
        s = mx_ref.live(d["ws"][r])
        if ((s != none) & ((s < least) | (s > most))).any(): b.append("ws: a scale out of range")
    return b
def reference(x, p, u, v, wc, ws):
    qu = [mx_ref.quantize(u[r]) for r in range(N)]
    lay = [pk(wc[r], ws[r]) for r in range(N)]
    seat = [gentries(p[r]) for r in range(N)]
    slots = np.tile(C + np.arange(4 * B), (8, 1))
    now = [x[r] for r in range(N)]
    for t in range(R):
        sent, fill = [], []
        for r in range(N):
            s = mx_ref.matmul(qu[r], mx_ref.quantize(now[r]))
            left, stand = slides(np.take_along_axis(s[::16], seat[r], axis=1))
            sent.append(mx_ref.quantize(gcols(now[r], np.take_along_axis(seat[r], left, axis=1))))
            fill.append(np.take_along_axis(np.concatenate([seat[r], slots], axis=1), stand, axis=1))
        came = decode(join(*sent)).astype(BF)
        made = []
        for r in range(N):
            z = gcols(np.concatenate([now[r], cut(came, (r - STEP[t]) % N, 16 * B)], axis=1), fill[r])
            q = mx_ref.quantize(z)
            made.append(tile([np.maximum(mx_ref.matmul(pick(lay[r], np.arange(128 * b, 128 * b + 128)), q), np.float32(0.0)) * np.float32(0.015625) + z[:, b::4].astype(np.float32) for b in range(4)]))
        now = made
    y, ol = np.zeros((N, 128, C), np.float32), np.zeros((N, 8, C), np.float32)
    oc, osc = np.zeros((N, 128, 4 * C), np.uint8), np.zeros((N, 16, C), np.uint8)
    for r in range(N):
        q = mx_ref.quantize(now[r])
        y[r] = mx_ref.matmul(mx_ref.quantize(v[r]), q)
        ol[r] = fill[r]
        oc[r], osc[r] = emit(q)
    return {"y": y, "ol": ol, "oc": oc, "osc": osc}

@@ -1,0 +1,512 @@
+from concourse.mybir import dt, AluOpType, AxisListType, ActivationFunctionType
+
+ALU = AluOpType
+ACT = ActivationFunctionType
+R = 3
+STEP = [3, 6, 4]
+LOW = -9.0e29
+MARK = 4000.0
+RUNS = [(0, 3, 0), (3, 3, 4), (6, 2, 8), (8, 1, 3), (9, 1, 7), (10, 6, 10)]
+CYCLE, LOAD, FLIGHT, FAR, ISSUE, FIRST, ROW, NEAR_RATE, FAR_RATE = 0.001, 1.5, 1.5, 0.2, 0.5, 1.5, 0.03, 20000.0, 10000.0
+CASES = [(0.1, 1.0), (0.05, 0.8), (0.22, 1.4)]
+STEPS, HEAT, SEED = 60000, 0.4, 1
+PLAN = []
+PICK_F, PICK_V = "vvaa", ["vvaa", "vaaa"]
+
+CODES = "float8_e4m3fn_x4"
+SCRATCH = {}
+
+
+def _buf(name, n, dtype, where="sbuf"):
+    SCRATCH[name] = (where, [128, n], dtype)
+
+
+for _r in range(R):
+    _buf("tw%d" % _r, 1280, "bfloat16")
+    _buf("vv%d" % _r, 1024, "bfloat16")
+    _buf("dd%d" % _r, 1024, "bfloat16")
+    _buf("qvc%d" % _r, 256, CODES)
+    _buf("qvs%d" % _r, 256, "uint8")
+    _buf("ldc%d" % _r, 256, CODES)
+    _buf("lds%d" % _r, 256, "uint8")
+    _buf("lso%d" % _r, 4, "uint16")
+    _buf("lsi%d" % _r, 4, "uint16")
+    _buf("ar%d" % _r, 1024, "float32")
+_buf("tw3", 1024, "bfloat16")
+for _r in range(R + 1):
+    _buf("qtc%d" % _r, 256, CODES)
+    _buf("qts%d" % _r, 256, "uint8")
+for _n, _w, _d in [
+    ("ub", 512, "bfloat16"), ("vb", 512, "bfloat16"), ("pi", 16, "int32"),
+    ("quc", 128, CODES), ("qus", 128, "uint8"), ("qpc", 128, CODES), ("qps", 128, "uint8"),
+    ("qyc", 128, CODES), ("qys", 128, "uint8"), ("wqc", 512, CODES), ("wqs", 512, "uint8"),
+    ("eb", 1032, "bfloat16"), ("qec", 512, CODES), ("qes", 512, "uint8"),
+    ("qnc", 256, CODES), ("qns", 256, "uint8"), ("ys", 256, "float32"), ("yi", 256, "float32"),
+    ("pc", 8, "int32"), ("cf", 24, "float32"), ("i16", 256, "float32"), ("i128", 128, "float32"),
+    ("mask", 256, "float32"), ("rst", 256, "float32"), ("inv", 320, "float32"),
+    ("tmp", 64, "float32"), ("c0", 16, "float32"), ("si", 51, "int32"), ("sf", 255, "float32"),
+    ("oz0", 4, "uint16"), ("oz1", 4, "uint16"), ("ox", 4, "uint16"), ("oc4", 4, "uint16"), ("ou", 8, "uint16"), ("om", 2, "uint16"),
+    ("on", 16, "uint16"), ("oka", 16, "uint16"), ("okb", 16, "uint16"), ("ov", 64, "uint16"), ("ot", 16, "uint16"),
+    ("pa", 32, "float32"), ("pb", 32, "float32"),
+    ("sk", 256, "float32"), ("km", 256, "float32"), ("kl", 560, "float32"), ("il", 400, "float32"),
+    ("xx", 128, "float32"), ("dn", 64, "float32"), ("zk", 192, "float32"), ("zi", 320, "float32"), ("nx", 256, "float32"),
+    ("pk", 192, "float32"), ("pj", 256, "float32"), ("gg", 64, "float32"), ("l3", 2, "float32"),
+    ("o1", 256, "float32"), ("o2", 256, "float32"),
+]:
+    _buf(_n, _w, _d)
+for _n in ["pr0", "pr1", "pr2", "pr3", "pk0", "pk1", "pd0", "pd1"]:
+    _buf(_n, 512, "float32", "psum")
+
+DMAS = ["x0", "x1", "u", "p", "wc", "ws", "v", "y0", "y1", "ol", "oc", "os0", "os1", "os2", "os3"]
+SEMAPHORES = (["sv", "sa", "st", "sg", "sent"] + ["m_" + n for n in DMAS]
+              + ["in%d_%d" % (r, k) for r in range(R) for k in range(3)])
+QUEUES = [None, "g", "v", "a", "t", "s"]
+GRAIN = 32
+
+
+def times(ops, seq, wake, slow, first=0, old=None):
+    k0 = first // GRAIN * GRAIN if old else 0
+    if old:
+        end, by, marks = list(old[0]), list(old[1]), old[2][:k0 // GRAIN + 1]
+        free, last, busy = list(marks[-1][0]), list(marks[-1][1]), marks[-1][2]
+    else:
+        end, by, marks = [0.0] * len(ops), [-1] * len(ops), []
+        free, last, busy = [0.0] * len(QUEUES), [-1] * len(QUEUES), 0.0
+    for k in range(k0, len(seq)):
+        if k % GRAIN == 0 and len(marks) == k // GRAIN:
+            marks.append((list(free), list(last), busy))
+        i = seq[k]
+        q, deps, hold, lat, move = ops[i]
+        t, b = free[q], last[q]
+        w = wake if q else FAR * slow
+        for d in deps:
+            if end[d] + w > t:
+                t, b = end[d] + w, d
+        by[i] = b
+        if move:
+            busy = max(busy, t + lat * slow) + move * slow
+            end[i] = busy
+        else:
+            end[i] = t + lat
+        if q:
+            free[q], last[q] = t + hold, i
+    return end, by, marks
+
+
+def order(calls):
+    n = len(calls)
+    ops = [(QUEUES.index(c[0]),) + c[1:5] for c in calls]
+    tied = [set(c[1]) | set(c[5]) for c in calls]
+    later = [set() for _ in calls]
+    tail = [o[3] + o[4] for o in ops]
+    for i in range(n - 1, -1, -1):
+        for d in tied[i]:
+            later[d].add(i)
+            tail[d] = max(tail[d], ops[d][3] + ops[d][4] + CASES[0][0] + tail[i])
+    start, lines = [0.0] * n, {}
+    for i in sorted(range(n), key=lambda i: (-tail[i], i)):
+        t = max([start[d] + ops[d][3] + ops[d][4] + CASES[0][0] for d in ops[i][1]] + [start[d] + ops[d][2] for d in calls[i][5]] + [0.0])
+        line, at = lines.setdefault(ops[i][0], []), 0
+        for a, b in line:
+            if t + ops[i][2] <= a + 1e-9:
+                break
+            t, at = max(t, b), at + 1
+        line.insert(at, (t, t + ops[i][2]))
+        start[i] = t
+    seq = sorted(range(n), key=lambda i: (start[i], i))
+    seed = [SEED]
+
+    def rnd(m):
+        seed[0] = (seed[0] * 1103515245 + 12345) % 2147483648
+        return (seed[0] >> 8) % m
+
+    def carry(run, links):
+        took, want = [run[0]], set(links[run[0]])
+        for i in run[1:]:
+            if i in want:
+                took.append(i)
+                want |= links[i]
+        if took[-1] == run[-1]:
+            return None
+        gone = set(took)
+        return [i for i in run if i not in gone] + took
+    runs = [times(ops, seq, w, f) for w, f in CASES]
+    cur = sum(max(r[0]) for r in runs)
+    best, keep = cur, seq
+    for turn in range(STEPS):
+        end, by = runs[rnd(len(CASES))][:2]
+        i = end.index(max(end))
+        pairs = []
+        while by[i] >= 0:
+            if by[i] not in tied[i]:
+                pairs.append((by[i], i))
+            i = by[i]
+        if not pairs:
+            continue
+        a, b = pairs[rnd(len(pairs))]
+        q, a, b, how = ops[a][0], seq.index(a), seq.index(b), rnd(4)
+        if how == 0:
+            same = [k for k in range(max(0, a - 40), a + 1) if ops[seq[k]][0] == q]
+            a = same[rnd(len(same))]
+        if how == 1:
+            same = [k for k in range(b, min(n, b + 40)) if ops[seq[k]][0] == q]
+            b = same[rnd(len(same))]
+        mid = carry(seq[a:b + 1], later) if how % 2 else carry(seq[a:b + 1][::-1], tied)
+        if mid is None:
+            continue
+        new = seq[:a] + (mid if how % 2 else mid[::-1]) + seq[b + 1:]
+        seen = [times(ops, new, w, f, a, r) for (w, f), r in zip(CASES, runs)]
+        score = sum(max(r[0]) for r in seen)
+        if score <= cur + HEAT * (1.0 - turn / STEPS) * rnd(1000) / 1000.0:
+            seq, cur, runs = new, score, seen
+            if score < best:
+                best, keep = score, new
+    PLAN.append(best / len(CASES))
+    return keep
+
+
+def rank_program(g, core, T, topo):
+    rank = T.rank_of(core)
+    if rank is None:
+        return
+    n = len(T.cores)
+    queues = {"g": g, "v": g.vector, "a": g.scalar, "t": g.tensor, "s": g.sync}
+    own = {"g": "sg", "v": "sv", "a": "sa", "t": "st"}
+    ops = []
+    log = {}
+
+    def A(name, lo=0, hi=None, step=1):
+        if hi is None:
+            hi = SCRATCH[name][1][1]
+        ap = T[name][:, lo:hi:step] if step > 1 else T[name][:, lo:hi]
+        if SCRATCH[name][0] == "psum":
+            return (ap, [(name, 0, 512, 1)], hi - lo, "p")
+        return (ap, [(name, lo, hi, step)], (hi - lo + step - 1) // step, "s")
+
+    def G(win, off, words=False):
+        ap = win[0].bitcast(dt.uint32) if words else win[0]
+        return (ap.indirect(off[0]), win[1] + off[1], 16 * off[2], "g")
+
+    def regs(xs):
+        return [r for x in xs if isinstance(x, tuple) for r in x[1]]
+
+    def raw(x):
+        return x[0] if isinstance(x, tuple) else x
+
+    def note(q, outs, ins, call, sem, inc, hold, lat, move=0.0, more=(), behind=()):
+        reads, writes, deps = regs(ins), regs(outs), set(more)
+        for rs, wr in ((reads, False), (writes, True)):
+            for (name, lo, hi, st) in rs:
+                excl = wr or SCRATCH[name][0] == "psum"
+                for (l2, h2, s2, w2, i) in log.get(name, []):
+                    if l2 < hi and lo < h2 and (excl or w2) and not (st == s2 and (lo - l2) % st):
+                        deps.add(i)
+        for rs, wr in ((reads, False), (writes, True)):
+            for (name, lo, hi, st) in rs:
+                w = wr or SCRATCH[name][0] == "psum"
+                old = log.get(name, [])
+                if w:
+                    old = [e for e in old if not (lo <= e[0] and e[1] <= hi and (st == 1 or (st == e[2] and (lo - e[0]) % st == 0)))]
+                log[name] = old + [(lo, hi, st, w, len(ops))]
+        ops.append((q, sorted(deps), hold, lat, move, list(behind), call, sem, inc))
+        return len(ops) - 1
+
+    def run(q, outs, ins, call, rate=1.0, fixed=0.0):
+        w = outs[0][2]
+        if any(isinstance(x, tuple) and x[3] == "g" for x in ins):
+            c = (0.05 if q == "v" else 0.065) + 1.5 * w * CYCLE
+        else:
+            c = max(64.0, rate * w) * CYCLE if not fixed else fixed + rate * w * CYCLE
+        note(q, outs, ins, lambda: call().then_inc(T.sem[own[q]], 1), own[q], 1, c, c)
+
+    V, S = g.vector, g.scalar
+
+    def ts(out, a, s1, op0, s2=None, op1=None):
+        if op1 is None:
+            run("v", [out], [a, s1], lambda: V.tensor_scalar(out[0], a[0], raw(s1), None, op0))
+        else:
+            run("v", [out], [a, s1, s2], lambda: V.tensor_scalar(out[0], a[0], raw(s1), raw(s2), op0, op1))
+
+    def tt(out, a, b, op):
+        run("v", [out], [a, b], lambda: V.tensor_tensor(out[0], a[0], b[0], op), 2.0)
+
+    def cp(q, out, a):
+        if q == "v":
+            run("v", [out], [a], lambda: V.tensor_copy(out[0], a[0]))
+        else:
+            run("a", [out], [a], lambda: S.activation(out[0], a[0], ACT.Copy))
+
+    def act(out, a, func, bias, scale):
+        run("a", [out], [a, bias], lambda: S.activation(out[0], a[0], func, bias=raw(bias), scale=scale))
+
+    def scan(out, d0, d1, op0, op1):
+        run("v", [out], [d0, d1], lambda: V.tensor_tensor_scan(out[0], d0[0], d1[0], 0.0, op0, op1))
+
+    def fill(out, c):
+        run("v", [out], [], lambda: V.memset(out[0], c))
+
+    def quant(c, s, lo, a):
+        oc, osc = A(c, lo, lo + a[2] // 4), A(s, lo, lo + a[2] // 4)
+        run("v", [oc, osc], [a], lambda: V.quantize_mx(oc[0], osc[0], a[0]), 1.06, 0.015)
+
+    def mm(bank, wc, ws, wl, c, s, lo, w):
+        o, a, b, x, y = A(bank, 0, w), A(wc, wl, wl + 128), A(ws, wl, wl + 128), A(c, lo, lo + w), A(s, lo, lo + w)
+        run("t", [o], [a, b, x, y], lambda: g.tensor.matmul_mx(o[0], a[0], b[0], x[0], y[0], True, True), 1.5, 0.024)
+
+    def iota(out, pattern, base, mult, flag=True):
+        if flag:
+            run("g", [out], [], lambda: g.iota(out[0], pattern, base, mult, allow_small_or_imprecise_dtypes=True), 2.0, 0.13)
+        else:
+            run("g", [out], [], lambda: g.iota(out[0], pattern, base, mult), 2.0, 0.13)
+
+    loads = []
+
+    def dma(q, name, out, a, rows, width, first=False):
+        i = note(q, [out], [a], lambda: queues[q].dma_start(raw(out), raw(a)).then_inc(T.sem["m_" + name], 16),
+                 "m_" + name, 16, 0.1, LOAD, max(1, rows // 16) * (ROW + width / NEAR_RATE), (), loads[-1:] if first else ())
+        loads.append(i)
+
+    def u8(x):
+        return (x[0].bitcast(dt.uint8),) + x[1:]
+
+    def u32(x):
+        return (x[0].bitcast(dt.uint32),) + x[1:]
+
+    sent = []
+
+    def send(r, k, pairs):
+        dst = T.cores[(rank + STEP[r]) % n]
+        src = T.cores[(rank - STEP[r]) % n]
+        rid, pid = topo.addr(dst, core)
+        sem = "in%d_%d" % (r, k)
+        mine = []
+        for out, a, width in pairs:
+            more = 0.0 if sent else FIRST
+            mine.append(note("g", [], [a], lambda out=out, a=a: g.remote_dma(out[0], a[0], T.sem[sem], T.sem["sent"], pid, rid, topo.mask(core, dst)),
+                             "sent", len(topo.engines(core, dst)), ISSUE + more, FLIGHT + more, 16 * (ROW + width / FAR_RATE), (), sent[:1]))
+            sent.append(mine[-1])
+        note(None, [p[0] for p in pairs], [], None, sem, len(pairs) * len(topo.engines(src, core)), 0.0, 0.0, 0.0, mine)
+
+    def send_state(r, h):
+        lo, hi = 128 * h, 128 * h + 128
+        send(r, h, [(u8(A("ldc%d" % r, lo, hi)), u8(A("qtc%d" % r, lo, hi)), 512), (A("lds%d" % r, lo, hi), A("qts%d" % r, lo, hi), 128)])
+
+    def col(j):
+        return A("cf", j, j + 1)
+
+    dma("s", "x0", A("tw0", 0, 512), T.x[:, 0:512], 128, 1024, True)
+    dma("a", "u", A("ub"), T.u[:], 128, 1024, True)
+    dma("s", "x1", A("tw0", 512, 1024), T.x[:, 512:1024], 128, 1024, True)
+    dma("a", "p", A("pi"), T.p[:], 128, 64, True)
+    dma("s", "wc", u8(A("wqc")), T.wc[:], 128, 2048, True)
+    dma("s", "ws", A("wqs"), T.ws[:], 128, 512, True)
+    dma("s", "v", A("vb"), T.v[:], 128, 1024, True)
+
+    iota(A("pc", 0, 1), [[0, 1]], 0, 1, False)
+    iota(A("i16"), [[0, 16], [1, 16]], 0, 0)
+    iota(A("i128"), [[1, 128]], 0, 0)
+    for pos, cnt, place in RUNS:
+        iota(A("inv", 16 * pos, 16 * (pos + cnt)), [[1, cnt], [16, 16]], place, 0)
+    iota(A("inv", 256, 320), [[1, 64]], 256, 0)
+    fill(A("xx"), 0.0)
+    for k in range(4):
+        fill(A("xx", 32 * k + 1, 32 * k + 4), 1.0)
+        fill(A("xx", 32 * k + 4, 32 * k + 20, 5), 1.0)
+    fill(A("sf", 119, 136), 0.0)
+    pcol = A("pc", 0, 1)
+    ts(A("pc", 1, 2), pcol, 15, ALU.bitwise_and)
+    ts(A("pc", 2, 3), pcol, 4, ALU.logical_shift_right, 1, ALU.bitwise_and)
+    ts(A("pc", 3, 4), pcol, 3, ALU.bitwise_and)
+    ts(A("pc", 4, 5), pcol, 2, ALU.logical_shift_right, 3, ALU.bitwise_and)
+    cp("v", A("cf", 0, 5), A("pc", 0, 5))
+    cp("v", A("si", 16, 17), A("pc", 1, 2))
+    P_, RR, ODD, SL, FI = [col(j) for j in range(5)]
+    i4 = A("i16", 0, 4)
+    ts(col(5), ODD, -1.0, ALU.mult, 1.0, ALU.add)
+    ts(col(19), RR, 256.0, ALU.add)
+    ts(A("ou"), A("i16", 0, 8), 16.0, ALU.mult)
+    ts(A("cf", 8, 12), i4, SL, ALU.is_equal)
+    ts(A("mask"), A("i16"), RR, ALU.is_equal)
+    ts(col(12), col(10), 4.0, ALU.mult, col(9), ALU.add)
+    ts(col(13), col(10), 5.0, ALU.mult, FI, ALU.add)
+    ts(col(14), col(8), -1.0, ALU.mult, 1.0, ALU.add)
+    ts(A("tmp", 16, 32), A("i16", 0, 16), 15.0, ALU.is_lt, 16.0, ALU.mult)
+    ts(col(15), col(12), FI, ALU.add)
+    ts(col(16), col(11), 4.0, ALU.mult, col(13), ALU.add)
+    ts(col(17), col(14), 5.0, ALU.mult)
+    ts(A("c0"), A("tmp", 16, 32), col(19), ALU.add)
+    ts(A("tmp", 0, 4), i4, 4.0, ALU.mult, col(15), ALU.add)
+    ts(col(18), col(16), col(14), ALU.mult, 1.0, ALU.add)
+    ts(A("oz1"), A("tmp", 0, 4), 4.0, ALU.mult, 3.0, ALU.add)
+    ts(A("oz0"), A("tmp", 0, 4), 16.0, ALU.mult, 15.0, ALU.add)
+    ts(A("ox"), i4, col(17), ALU.mult, col(18), ALU.add)
+    ts(A("oc4"), i4, 4.0, ALU.mult, FI, ALU.add)
+    act(A("rst"), A("i16"), ACT.Sign, 0.0, 1.0)
+    act(A("il", 0, 200), A("i16", 0, 200), ACT.Identity, MARK, 0.0)
+    act(A("il", 200, 400), A("i16", 0, 200), ACT.Identity, MARK, 0.0)
+    act(A("kl", 256, 512), A("i16"), ACT.Identity, LOW, 0.0)
+    act(A("kl", 512, 560), A("i16", 0, 48), ACT.Identity, LOW, 0.0)
+    for j in range(0, 1032, 256):
+        w = min(256, 1032 - j)
+        act(A("eb", j, j + w), A("i16", 0, w), ACT.Copy, 0.0, 0.0)
+    ts(A("eb", 2, 514, 4), A("i128"), P_, ALU.is_equal)
+    ts(A("eb", 519, 1031, 4), A("i128"), P_, ALU.is_equal)
+    for b, o in enumerate((2, 518, 0, 516)):
+        quant("qec", "qes", 128 * b, A("eb", o, o + 512))
+    tt(A("tmp", 32, 48), A("inv", 0, 256, 16), A("mask", 0, 16), ALU.mult)
+    run("v", [col(6)], [A("tmp", 32, 48)], lambda: V.tensor_reduce(T.cf[:, 6:7], T.tmp[:, 32:48], AxisListType.X, ALU.add))
+    ts(A("om", 0, 1), col(6), 4.0, ALU.mult, 3.0, ALU.add)
+
+    quant("quc", "qus", 0, A("ub"))
+    quant("qyc", "qys", 0, A("vb"))
+    cp("v", u32(A("qpc")), G(A("quc"), A("ou"), True))
+    cp("a", A("qps"), G(A("qus"), A("ou")))
+    for h in range(2):
+        quant("qtc0", "qts0", 128 * h, A("tw0", 512 * h, 512 * h + 512))
+        mm("pk%d" % h, "qpc", "qps", 0, "qtc0", "qts0", 128 * h, 128)
+        cp("a", A("sk", 128 * h, 128 * h + 128), A("pk%d" % h, 0, 128))
+        send_state(0, h)
+    ts(A("pa", 0, 16), A("pi"), col(5), ALU.mult)
+    ts(A("pa", 16, 32), A("pi"), ODD, ALU.mult)
+    run("v", [A("pb")], [A("pa")], lambda: V.transpose(T.pb[:], T.pa[:]))
+    tt(A("il", 3, 64, 4), A("pb", 0, 16), A("pb", 16, 32), ALU.add)
+    cp("v", A("oka"), A("il", 3, 64, 4))
+    shift = sorted((place, pos - place) for pos, cnt, place in RUNS)
+    low = A("si", 17, 34)
+    cp("v", A("si", 0, 16), A("il", 3, 64, 4))
+    ts(low, A("si", 0, 17), 15, ALU.bitwise_and)
+    ts(A("si", 34, 51), A("si", 0, 17), 4, ALU.logical_shift_right)
+    ts(A("sf", 0, 17), low, 16.0, ALU.mult)
+    cp("v", A("sf", 17, 34), A("si", 34, 51))
+    for j, (a, b) in enumerate(zip(shift, shift[1:])):
+        ts(A("sf", 34 + 17 * j, 51 + 17 * j), low, float(b[0]), ALU.is_ge, 16.0 * (b[1] - a[1]), ALU.mult)
+    tt(A("sf", 136, 204), A("sf", 0, 68), A("sf", 68, 136), ALU.add)
+    tt(A("sf", 204, 238), A("sf", 136, 170), A("sf", 170, 204), ALU.add)
+    tt(A("sf", 238, 255), A("sf", 204, 221), A("sf", 221, 238), ALU.add)
+    cp("v", A("okb"), A("sf", 238, 254))
+    ts(A("on"), A("i16", 0, 16), A("sf", 254, 255), ALU.add)
+
+    for r in range(R):
+        tw, nxt, vv, ar = "tw%d" % r, "tw%d" % (r + 1), "vv%d" % r, "ar%d" % r
+        last = r == R - 1
+        kbase = [0, 320, 400, 480]
+
+        def ids(k, lo=0, hi=16):
+            return A("il", 80 * k + 4 * lo + 3, 80 * k + 4 * hi, 4)
+
+        def keys(k, lo, hi):
+            if k == 0:
+                return A("kl", 16 * lo + 15, 16 * hi, 16)
+            return A("kl", kbase[k] + 4 * lo + 3, kbase[k] + 4 * hi, 4)
+
+        for h in range(2):
+            half = (128 * h, 128 * h + 128)
+            tt(A("km", *half), G(A("sk"), A("oka" if r == 0 else "okb", 8 * h, 8 * h + 8)), A("mask", *half), ALU.mult)
+            scan(A("kl", *half), A("rst", *half), A("km", *half), ALU.mult, ALU.add)
+        for h in range(2):
+            for b, bank in enumerate([["pr0", "pr1", "pr2", "pr3"], ["pd0", "pd1", "pk0", "pk1"]][h]):
+                mm(bank, "qec", "qes", 128 * b, "ldc%d" % r, "lds%d" % r, 128 * h, 128)
+                cp("a", A("dd%d" % r, 256 * b + 128 * h, 256 * b + 128 * h + 128), A(bank, 0, 128))
+        for k in range(4):
+            x, d, z = 32 * k, 16 * k, 64 * k
+            if k == 0:
+                tt(A("dn", 0, 11), keys(0, 4, 15), keys(0, 1, 12), ALU.is_gt)
+                cp("a", A("zk", 0, 64), G(A("kl", 0, 320), A("oz0")))
+            else:
+                tt(A("dn", d, d + 3), keys(k, 4, 7), keys(k, 1, 4), ALU.is_gt)
+                tt(A("dn", d + 4, d + 11), keys(k, 8, 15), keys(k, 5, 12), ALU.is_gt)
+                if k < 3:
+                    cp("a", A("zk", z, z + 64), G(A("kl", kbase[k], kbase[k] + 80), A("oz1")))
+            cp("a", A("zi", z, z + 64), G(A("il", 80 * k, 80 * k + 80), A("oz1")))
+            if k == 2:
+                cp("v", A("lso%d" % r, 0, 3), A("il", 3, 164, 80))
+                act(A("l3", 0, 1), ids(2, 1, 2), ACT.Identity, ids(2, 4, 5), -1.0)
+                ts(A("lso%d" % r, 3, 4), A("dn", d, d + 1), A("l3", 0, 1), ALU.mult, ids(2, 1, 2), ALU.add)
+                send(r, 2, [(A("lsi%d" % r), A("lso%d" % r), 8)])
+                act(A("gg", 0, 16), keys(2, 0, 16), ACT.Relu, 16.0, -32.0 / LOW)
+                tt(A("gg", 32, 48), A("gg", 0, 16), A("c0"), ALU.add)
+            zi = A("zi", z, z + 64)
+            if k == 3:
+                act(A("gg", 16, 32), keys(3, 0, 16), ACT.Relu, 16.0, -32.0 / LOW)
+                tt(A("gg", 48, 64), A("gg", 32, 48), A("gg", 16, 32), ALU.add)
+                tt(A("zi", 256, 320), G(A("gg", 48, 64), A("oc4")), zi, ALU.min)
+                zi = A("zi", 256, 320)
+            for i in range(3):
+                scan(A("xx", x + 5 * i + 6, x + 5 * i + 9), A("dn", d + 4 * i, d + 4 * i + 3), A("xx", x + 5 * i + 1, x + 5 * i + 4),
+                     ALU.max, ALU.min)
+            if k < 3:
+                for h in range(2):
+                    path = G(A("xx", x, x + 16 * h + 16), A("ox", 2 * h, 2 * h + 2))
+                    lo, hi = z + 32 * h, z + 32 * h + 32
+                    act(A("nx", lo, hi), path, ACT.Identity, 1.0, -1.0)
+                    tt(A("pk", lo, hi), path, A("zk", lo, hi), ALU.mult)
+                    scan(A("kl", kbase[k + 1] + 32 * h, kbase[k + 1] + 32 * h + 32), A("nx", lo, hi), A("pk", lo, hi), ALU.mult, ALU.add)
+            else:
+                act(A("nx", z, z + 64), G(A("xx", x, x + 32), A("ox")), ACT.Identity, 1.0, -1.0)
+            tt(A("pj", z, z + 64), G(A("xx", x, x + 32), A("ox")), zi, ALU.mult)
+            scan(A("il", 80 * k + 80, 80 * k + 144), A("nx", z, z + 64), A("pj", z, z + 64), ALU.mult, ALU.add)
+        where = G(A("il", 320, 384), A("om", 0, 1))
+        for t in range(4):
+            ts(A("ov", 16 * t, 16 * t + 16), where, 4.0, ALU.mult, float(t), ALU.add)
+        if r == 0:
+            cp("a", ids(0), A("sf", 238, 254))
+        if last:
+            cp("v", A("ot"), where)
+            cp("a", A("o1"), G(A("inv"), A("ot")))
+            cp("a", A("o2"), G(A("o1"), A("on")))
+            dma("s", "ol", T.ol[:], (T.o2[0:128:16, :],) + A("o2")[1:], 8, 1024)
+        for b in range(4):
+            cp(PICK_F[b], A(tw, 1024 + b, 1280, 4), G(A("dd%d" % r, 256 * b, 256 * b + 256), A("lsi%d" % r)))
+        for h in range(2):
+            for t in range(4):
+                cp(PICK_V[h][t], A(vv, 512 * h + t, 512 * h + 512, 4),
+                   G(A(tw, 0, 1024 + 256 * h), A("ov", 16 * t + 8 * h, 16 * t + 8 * h + 8)))
+            quant("qvc%d" % r, "qvs%d" % r, 128 * h, A(vv, 512 * h, 512 * h + 512))
+            for b in range(4):
+                mm("pr%d" % b, "wqc", "wqs", 128 * b, "qvc%d" % r, "qvs%d" % r, 128 * h, 128)
+                act(A(ar, 512 * h + 128 * b, 512 * h + 128 * b + 128), A("pr%d" % b, 0, 128), ACT.Relu, 0.0, 0.015625)
+                tt(A(nxt, 512 * h + b, 512 * h + 512, 4), A(ar, 512 * h + 128 * b, 512 * h + 128 * b + 128),
+                   A(vv, 512 * h + b, 512 * h + 512, 4), ALU.add)
+            quant("qtc%d" % (r + 1), "qts%d" % (r + 1), 128 * h, A(nxt, 512 * h, 512 * h + 512))
+            if not last:
+                send_state(r + 1, h)
+                mm("pk%d" % h, "qpc", "qps", 0, "qtc%d" % (r + 1), "qts%d" % (r + 1), 128 * h, 128)
+                cp("a", A("sk", 128 * h, 128 * h + 128), A("pk%d" % h, 0, 128))
+
+    cp("v", u32(A("qnc")), G(A("qtc3"), A("on"), True))
+    cp("a", A("qns"), G(A("qts3"), A("on")))
+    dma("s", "oc", T.oc[:], u8(A("qnc")), 128, 1024)
+    for k in range(4):
+        dma("ssaa"[k], "os%d" % k, T.osc[4 * k:4 * k + 4, :], (T.qns[32 * k:32 * k + 4, :],) + A("qns")[1:], 4, 256)
+    for h in range(2):
+        mm("pk%d" % h, "qyc", "qys", 0, "qtc3", "qts3", 128 * h, 128)
+        cp("av"[h], A("yi", 128 * h, 128 * h + 128), A("pk%d" % h, 0, 128))
+    for h in range(2):
+        cp("va"[h], A("ys", 128 * h, 128 * h + 128), G(A("yi"), A("on", 8 * h, 8 * h + 8)))
+        dma("sa"[h], "y%d" % h, T.y[:, 128 * h:128 * h + 128], A("ys", 128 * h, 128 * h + 128), 128, 512)
+
+    known = {q: {} for q in queues}
+    count, seen, token = {}, {}, {}
+    if not PLAN:
+        PLAN.append(order(ops))
+    for i in PLAN[-1]:
+        q, deps, call, sem, inc = ops[i][0], ops[i][1], ops[i][6], ops[i][7], ops[i][8]
+        if q:
+            want = {}
+            for d in deps:
+                s, v = token[d]
+                want[s] = max(want.get(s, 0), v)
+            todo = [(s, v) for s, v in want.items() if known[q].get(s, 0) < v]
+            for s, v in todo:
+                if not any(s2 != s and seen[(s2, v2)].get(s, 0) >= v for s2, v2 in todo):
+                    queues[q].wait_ge(T.sem[s], v)
+                    for s2, v2 in seen[(s, v)].items():
+                        known[q][s2] = max(known[q].get(s2, 0), v2)
+            call()
+        count[sem] = count.pop(sem, 0) + inc
+        token[i] = (sem, count[sem])
+        seen[token[i]] = dict(known[q]) if q else {}
+        seen[token[i]][sem] = count[sem]
+    for s, v in count.items():
+        if all(known[q].get(s, 0) < v for q in queues):
+            g.wait_ge(T.sem[s], v)

@@ -1,17 +1,31 @@
-from concourse.mybir import dt, AluOpType, AxisListType, ActivationFunctionType
+from concourse.mybir import dt, AluOpType, ActivationFunctionType
 
 ALU = AluOpType
 ACT = ActivationFunctionType
 R = 3
 STEP = [3, 6, 4]
 LOW = -9.0e29
-MARK = 4000.0
-RUNS = [(0, 3, 0), (3, 3, 4), (6, 2, 8), (8, 1, 3), (9, 1, 7), (10, 6, 10)]
-CYCLE, LOAD, FLIGHT, FAR, ISSUE, FIRST, ROW, NEAR_RATE, FAR_RATE = 0.001, 1.5, 1.5, 0.2, 0.5, 1.5, 0.03, 20000.0, 10000.0
-CASES = [(0.1, 1.0), (0.05, 0.8), (0.22, 1.4)]
-STEPS, HEAT, SEED = 60000, 0.4, 1
-PLAN = []
-PICK_F, PICK_V = "vvaa", ["vvaa", "vaaa"]
+SWAPS = [(3, 8), (7, 9)]
+PICK_F, PICK_V = "vvaa", ["vvaa", "vvaa"]
+HEAD = {
+    "s": "u p x1 ws wc",
+    "g": "x5 pc i16 i128 hs0 hs1",
+    "v": "six eb pc1 xz six0 cf xo mask e1 cf2 vam hq0 cf3 qe1 vas ou qu pa qe0 qp pb qe2 hq1 oz ob oka oza si",
+    "a": "x0 val val5 rst qp pad il0 hk0 hk1",
+    "t": "hk0 hk1",
+}
+ROUND = {
+    "s": "v ol oc os",
+    "g": "inv sl s0 s1",
+    "v": "qy km0 km1 kl0 kl1 d0a low d0b s00 e04 e02 e03 s01 e01 qe3 s02 p0a p0b o0a j0 o0b "
+         "s10 sf2 i0 sf0 s11 sf1 vam5 s12 p1a j1a p1b o1a i1a j1b o1b d2a la i1b d2b "
+         "s20 lb e21 e24 s21 e22 e23 vas5 em2 s22 vam6 p2a p2b vas6 o2a j2 o2b "
+         "s30 oz5 i2 s31 ox5 em3 s32 sh j3 om i3 a2 a0 a1 a3 "
+         "g00 g01 f1 f0 q0 g10 g11 ot okb q1 t00 t01 t02 t03 t10 qt0 t11 t12 t13 qt1 n1 n0 y0g",
+    "a": "y0s z0b z0a c0 inv1 n0a n0b m0 z1 y1 n1a n1b l3 u00 u01 c2 y2 n2a u02 n2b m2 u03 r2 y3 m3 u10 u11 u12 u13 "
+         "g02 g03 f3 f2 g12 g13 r00 r01 r02 r03 r10 r11 r12 r13 o1 k0 o2 n1 ilb k1 n0 y1g yd",
+    "t": "u00 u01 u02 u03 u10 u11 u12 u13 r00 r01 r02 r03 r10 r11 r12 r13 k0 k1",
+}
 
 CODES = "float8_e4m3fn_x4"
 SCRATCH = {}
@@ -42,127 +56,44 @@ for _n, _w, _d in [
     ("qyc", 128, CODES), ("qys", 128, "uint8"), ("wqc", 512, CODES), ("wqs", 512, "uint8"),
     ("eb", 1032, "bfloat16"), ("qec", 512, CODES), ("qes", 512, "uint8"),
     ("qnc", 256, CODES), ("qns", 256, "uint8"), ("ys", 256, "float32"), ("yi", 256, "float32"),
-    ("pc", 8, "int32"), ("cf", 24, "float32"), ("i16", 256, "float32"), ("i128", 128, "float32"),
-    ("mask", 256, "float32"), ("rst", 256, "float32"), ("inv", 320, "float32"),
-    ("tmp", 64, "float32"), ("c0", 16, "float32"), ("si", 51, "int32"), ("sf", 255, "float32"),
-    ("oz0", 4, "uint16"), ("oz1", 4, "uint16"), ("ox", 4, "uint16"), ("oc4", 4, "uint16"), ("ou", 8, "uint16"), ("om", 2, "uint16"),
-    ("on", 16, "uint16"), ("oka", 16, "uint16"), ("okb", 16, "uint16"), ("ov", 64, "uint16"), ("ot", 16, "uint16"),
+    ("pc", 4, "int32"), ("cf", 8, "float32"), ("i16", 256, "float32"), ("i128", 128, "float32"), ("x5", 16, "float32"),
+    ("mask", 256, "float32"), ("rst", 256, "float32"), ("six", 102, "float32"), ("inv", 320, "float32"),
+    ("val", 368, "float32"), ("vam", 368, "float32"), ("vas", 368, "float32"), ("tmp", 8, "float32"),
+    ("si", 51, "int32"), ("sf", 102, "float32"), ("sh", 102, "float32"),
+    ("oz0", 4, "uint16"), ("oza", 4, "uint16"), ("oz1", 4, "uint16"), ("ox", 4, "uint16"), ("ob", 10, "uint16"), ("ou", 8, "uint16"),
+    ("ox5", 6, "uint16"), ("oz5", 6, "uint16"),
+    ("om", 6, "uint16"), ("on", 16, "uint16"), ("oka", 16, "uint16"), ("okb", 16, "uint16"), ("ov", 64, "uint16"), ("ot", 16, "uint16"),
     ("pa", 32, "float32"), ("pb", 32, "float32"),
-    ("sk", 256, "float32"), ("km", 256, "float32"), ("kl", 560, "float32"), ("il", 400, "float32"),
-    ("xx", 128, "float32"), ("dn", 64, "float32"), ("zk", 192, "float32"), ("zi", 320, "float32"), ("nx", 256, "float32"),
-    ("pk", 192, "float32"), ("pj", 256, "float32"), ("gg", 64, "float32"), ("l3", 2, "float32"),
+    ("sk", 256, "float32"), ("km", 256, "float32"), ("kl", 320, "float32"), ("il", 416, "float32"), ("xx", 168, "float32"),
+    ("zz", 288, "float32"), ("nn", 288, "float32"), ("pp", 288, "float32"), ("oo", 320, "float32"),
+    ("zi", 272, "float32"), ("ni", 272, "float32"), ("pj", 272, "float32"), ("em", 16, "float32"), ("l3", 2, "float32"),
     ("o1", 256, "float32"), ("o2", 256, "float32"),
 ]:
     _buf(_n, _w, _d)
-for _n in ["pr0", "pr1", "pr2", "pr3", "pk0", "pk1", "pd0", "pd1"]:
+BANK = ["ps%d" % _b for _b in range(8)]
+for _n in BANK:
     _buf(_n, 512, "float32", "psum")
 
-DMAS = ["x0", "x1", "u", "p", "wc", "ws", "v", "y0", "y1", "ol", "oc", "os0", "os1", "os2", "os3"]
+DMAS = ["x0", "x1", "u", "p", "wc", "ws", "v", "y", "ol", "oc", "os0", "os1", "os2", "os3"]
 SEMAPHORES = (["sv", "sa", "st", "sg", "sent"] + ["m_" + n for n in DMAS]
               + ["in%d_%d" % (r, k) for r in range(R) for k in range(3)])
-QUEUES = [None, "g", "v", "a", "t", "s"]
-GRAIN = 32
 
 
-def times(ops, seq, wake, slow, first=0, old=None):
-    k0 = first // GRAIN * GRAIN if old else 0
-    if old:
-        end, by, marks = list(old[0]), list(old[1]), old[2][:k0 // GRAIN + 1]
-        free, last, busy = list(marks[-1][0]), list(marks[-1][1]), marks[-1][2]
-    else:
-        end, by, marks = [0.0] * len(ops), [-1] * len(ops), []
-        free, last, busy = [0.0] * len(QUEUES), [-1] * len(QUEUES), 0.0
-    for k in range(k0, len(seq)):
-        if k % GRAIN == 0 and len(marks) == k // GRAIN:
-            marks.append((list(free), list(last), busy))
-        i = seq[k]
-        q, deps, hold, lat, move = ops[i]
-        t, b = free[q], last[q]
-        w = wake if q else FAR * slow
-        for d in deps:
-            if end[d] + w > t:
-                t, b = end[d] + w, d
-        by[i] = b
-        if move:
-            busy = max(busy, t + lat * slow) + move * slow
-            end[i] = busy
-        else:
-            end[i] = t + lat
-        if q:
-            free[q], last[q] = t + hold, i
-    return end, by, marks
-
-
-def order(calls):
-    n = len(calls)
-    ops = [(QUEUES.index(c[0]),) + c[1:5] for c in calls]
-    tied = [set(c[1]) | set(c[5]) for c in calls]
-    later = [set() for _ in calls]
-    tail = [o[3] + o[4] for o in ops]
-    for i in range(n - 1, -1, -1):
-        for d in tied[i]:
-            later[d].add(i)
-            tail[d] = max(tail[d], ops[d][3] + ops[d][4] + CASES[0][0] + tail[i])
-    start, lines = [0.0] * n, {}
-    for i in sorted(range(n), key=lambda i: (-tail[i], i)):
-        t = max([start[d] + ops[d][3] + ops[d][4] + CASES[0][0] for d in ops[i][1]] + [start[d] + ops[d][2] for d in calls[i][5]] + [0.0])
-        line, at = lines.setdefault(ops[i][0], []), 0
-        for a, b in line:
-            if t + ops[i][2] <= a + 1e-9:
-                break
-            t, at = max(t, b), at + 1
-        line.insert(at, (t, t + ops[i][2]))
-        start[i] = t
-    seq = sorted(range(n), key=lambda i: (start[i], i))
-    seed = [SEED]
-
-    def rnd(m):
-        seed[0] = (seed[0] * 1103515245 + 12345) % 2147483648
-        return (seed[0] >> 8) % m
-
-    def carry(run, links):
-        took, want = [run[0]], set(links[run[0]])
-        for i in run[1:]:
-            if i in want:
-                took.append(i)
-                want |= links[i]
-        if took[-1] == run[-1]:
-            return None
-        gone = set(took)
-        return [i for i in run if i not in gone] + took
-    runs = [times(ops, seq, w, f) for w, f in CASES]
-    cur = sum(max(r[0]) for r in runs)
-    best, keep = cur, seq
-    for turn in range(STEPS):
-        end, by = runs[rnd(len(CASES))][:2]
-        i = end.index(max(end))
-        pairs = []
-        while by[i] >= 0:
-            if by[i] not in tied[i]:
-                pairs.append((by[i], i))
-            i = by[i]
-        if not pairs:
-            continue
-        a, b = pairs[rnd(len(pairs))]
-        q, a, b, how = ops[a][0], seq.index(a), seq.index(b), rnd(4)
-        if how == 0:
-            same = [k for k in range(max(0, a - 40), a + 1) if ops[seq[k]][0] == q]
-            a = same[rnd(len(same))]
-        if how == 1:
-            same = [k for k in range(b, min(n, b + 40)) if ops[seq[k]][0] == q]
-            b = same[rnd(len(same))]
-        mid = carry(seq[a:b + 1], later) if how % 2 else carry(seq[a:b + 1][::-1], tied)
-        if mid is None:
-            continue
-        new = seq[:a] + (mid if how % 2 else mid[::-1]) + seq[b + 1:]
-        seen = [times(ops, new, w, f, a, r) for (w, f), r in zip(CASES, runs)]
-        score = sum(max(r[0]) for r in seen)
-        if score <= cur + HEAT * (1.0 - turn / STEPS) * rnd(1000) / 1000.0:
-            seq, cur, runs = new, score, seen
-            if score < best:
-                best, keep = score, new
-    PLAN.append(best / len(CASES))
-    return keep
+def order(ops):
+    lines = {None: [i for i, o in enumerate(ops) if not o[0]]}
+    for q in HEAD:
+        head, body = HEAD[q].split(), ROUND[q].split()
+        mine = [i for i, o in enumerate(ops) if o[0] == q]
+        lines[q] = sorted(mine, key=lambda i: (-1, head.index(ops[i][2]), i) if ops[i][2] in head else (ops[i][3], body.index(ops[i][2]), i))
+    seq, done = [], set()
+    while len(seq) < len(ops):
+        before = len(seq)
+        for line in lines.values():
+            while line and done.issuperset(ops[line[0]][1]):
+                done.add(line[0])
+                seq.append(line.pop(0))
+        assert len(seq) > before, [ops[line[0]][2:4] for line in lines.values() if line]
+    return seq
 
 
 def rank_program(g, core, T, topo):
@@ -174,18 +105,20 @@ def rank_program(g, core, T, topo):
     own = {"g": "sg", "v": "sv", "a": "sa", "t": "st"}
     ops = []
     log = {}
+    now = [0]
 
     def A(name, lo=0, hi=None, step=1):
         if hi is None:
             hi = SCRATCH[name][1][1]
         ap = T[name][:, lo:hi:step] if step > 1 else T[name][:, lo:hi]
-        if SCRATCH[name][0] == "psum":
-            return (ap, [(name, 0, 512, 1)], hi - lo, "p")
-        return (ap, [(name, lo, hi, step)], (hi - lo + step - 1) // step, "s")
+        return (ap, [(name, 0, 512, 1) if SCRATCH[name][0] == "psum" else (name, lo, hi, step)], (hi - lo + step - 1) // step)
+
+    def N(name, lo, count, step):
+        return A(name, lo, lo + (count - 1) * step + 1, step)
 
     def G(win, off, words=False):
         ap = win[0].bitcast(dt.uint32) if words else win[0]
-        return (ap.indirect(off[0]), win[1] + off[1], 16 * off[2], "g")
+        return (ap.indirect(off[0]), win[1] + off[1], 16 * off[2])
 
     def regs(xs):
         return [r for x in xs if isinstance(x, tuple) for r in x[1]]
@@ -193,7 +126,7 @@ def rank_program(g, core, T, topo):
     def raw(x):
         return x[0] if isinstance(x, tuple) else x
 
-    def note(q, outs, ins, call, sem, inc, hold, lat, move=0.0, more=(), behind=()):
+    def note(nm, q, outs, ins, call, sem, inc, more=()):
         reads, writes, deps = regs(ins), regs(outs), set(more)
         for rs, wr in ((reads, False), (writes, True)):
             for (name, lo, hi, st) in rs:
@@ -208,63 +141,57 @@ def rank_program(g, core, T, topo):
                 if w:
                     old = [e for e in old if not (lo <= e[0] and e[1] <= hi and (st == 1 or (st == e[2] and (lo - e[0]) % st == 0)))]
                 log[name] = old + [(lo, hi, st, w, len(ops))]
-        ops.append((q, sorted(deps), hold, lat, move, list(behind), call, sem, inc))
+        ops.append((q, sorted(deps), nm, now[0], call, sem, inc))
         return len(ops) - 1
 
-    def run(q, outs, ins, call, rate=1.0, fixed=0.0):
-        w = outs[0][2]
-        if any(isinstance(x, tuple) and x[3] == "g" for x in ins):
-            c = (0.05 if q == "v" else 0.065) + 1.5 * w * CYCLE
-        else:
-            c = max(64.0, rate * w) * CYCLE if not fixed else fixed + rate * w * CYCLE
-        note(q, outs, ins, lambda: call().then_inc(T.sem[own[q]], 1), own[q], 1, c, c)
+    def run(nm, q, outs, ins, call):
+        note(nm, q, outs, ins, lambda: call().then_inc(T.sem[own[q]], 1), own[q], 1)
 
     V, S = g.vector, g.scalar
 
-    def ts(out, a, s1, op0, s2=None, op1=None):
+    def ts(nm, out, a, s1, op0, s2=None, op1=None):
         if op1 is None:
-            run("v", [out], [a, s1], lambda: V.tensor_scalar(out[0], a[0], raw(s1), None, op0))
+            run(nm, "v", [out], [a, s1], lambda: V.tensor_scalar(out[0], a[0], raw(s1), None, op0))
         else:
-            run("v", [out], [a, s1, s2], lambda: V.tensor_scalar(out[0], a[0], raw(s1), raw(s2), op0, op1))
+            run(nm, "v", [out], [a, s1, s2], lambda: V.tensor_scalar(out[0], a[0], raw(s1), raw(s2), op0, op1))
 
-    def tt(out, a, b, op):
-        run("v", [out], [a, b], lambda: V.tensor_tensor(out[0], a[0], b[0], op), 2.0)
+    def tt(nm, out, a, b, op):
+        run(nm, "v", [out], [a, b], lambda: V.tensor_tensor(out[0], a[0], b[0], op))
 
-    def cp(q, out, a):
+    def cp(nm, q, out, a):
         if q == "v":
-            run("v", [out], [a], lambda: V.tensor_copy(out[0], a[0]))
+            run(nm, "v", [out], [a], lambda: V.tensor_copy(out[0], a[0]))
         else:
-            run("a", [out], [a], lambda: S.activation(out[0], a[0], ACT.Copy))
+            run(nm, "a", [out], [a], lambda: S.activation(out[0], a[0], ACT.Copy))
 
-    def act(out, a, func, bias, scale):
-        run("a", [out], [a, bias], lambda: S.activation(out[0], a[0], func, bias=raw(bias), scale=scale))
+    def act(nm, out, a, func, bias, scale):
+        run(nm, "a", [out], [a, bias], lambda: S.activation(out[0], a[0], func, bias=raw(bias), scale=scale))
 
-    def scan(out, d0, d1, op0, op1):
-        run("v", [out], [d0, d1], lambda: V.tensor_tensor_scan(out[0], d0[0], d1[0], 0.0, op0, op1))
+    def scan(nm, out, d0, d1, op0, op1):
+        run(nm, "v", [out], [d0, d1], lambda: V.tensor_tensor_scan(out[0], d0[0], d1[0], 0.0, op0, op1))
 
-    def fill(out, c):
-        run("v", [out], [], lambda: V.memset(out[0], c))
+    def fill(nm, out, c):
+        run(nm, "v", [out], [], lambda: V.memset(out[0], c))
 
-    def quant(c, s, lo, a):
+    def const(nm, out, c):
+        act(nm, out, A("i16", 0, out[2]), ACT.Identity, c, 0.0)
+
+    def quant(nm, c, s, lo, a):
         oc, osc = A(c, lo, lo + a[2] // 4), A(s, lo, lo + a[2] // 4)
-        run("v", [oc, osc], [a], lambda: V.quantize_mx(oc[0], osc[0], a[0]), 1.06, 0.015)
+        run(nm, "v", [oc, osc], [a], lambda: V.quantize_mx(oc[0], osc[0], a[0]))
 
-    def mm(bank, wc, ws, wl, c, s, lo, w):
+    def mm(nm, bank, wc, ws, wl, c, s, lo, w):
         o, a, b, x, y = A(bank, 0, w), A(wc, wl, wl + 128), A(ws, wl, wl + 128), A(c, lo, lo + w), A(s, lo, lo + w)
-        run("t", [o], [a, b, x, y], lambda: g.tensor.matmul_mx(o[0], a[0], b[0], x[0], y[0], True, True), 1.5, 0.024)
+        run(nm, "t", [o], [a, b, x, y], lambda: g.tensor.matmul_mx(o[0], a[0], b[0], x[0], y[0], True, True))
 
-    def iota(out, pattern, base, mult, flag=True):
+    def iota(nm, out, pattern, base, mult, flag=True):
         if flag:
-            run("g", [out], [], lambda: g.iota(out[0], pattern, base, mult, allow_small_or_imprecise_dtypes=True), 2.0, 0.13)
+            run(nm, "g", [out], [], lambda: g.iota(out[0], pattern, base, mult, allow_small_or_imprecise_dtypes=True))
         else:
-            run("g", [out], [], lambda: g.iota(out[0], pattern, base, mult), 2.0, 0.13)
+            run(nm, "g", [out], [], lambda: g.iota(out[0], pattern, base, mult))
 
-    loads = []
-
-    def dma(q, name, out, a, rows, width, first=False):
-        i = note(q, [out], [a], lambda: queues[q].dma_start(raw(out), raw(a)).then_inc(T.sem["m_" + name], 16),
-                 "m_" + name, 16, 0.1, LOAD, max(1, rows // 16) * (ROW + width / NEAR_RATE), (), loads[-1:] if first else ())
-        loads.append(i)
+    def dma(nm, q, name, out, a, more=()):
+        note(nm, q, [out], [a], lambda: queues[q].dma_start(raw(out), raw(a)).then_inc(T.sem["m_" + name], 16), "m_" + name, 16, more)
 
     def u8(x):
         return (x[0].bitcast(dt.uint8),) + x[1:]
@@ -272,225 +199,239 @@ def rank_program(g, core, T, topo):
     def u32(x):
         return (x[0].bitcast(dt.uint32),) + x[1:]
 
-    sent = []
-
-    def send(r, k, pairs):
+    def send(nm, r, k, pairs):
         dst = T.cores[(rank + STEP[r]) % n]
         src = T.cores[(rank - STEP[r]) % n]
         rid, pid = topo.addr(dst, core)
         sem = "in%d_%d" % (r, k)
-        mine = []
-        for out, a, width in pairs:
-            more = 0.0 if sent else FIRST
-            mine.append(note("g", [], [a], lambda out=out, a=a: g.remote_dma(out[0], a[0], T.sem[sem], T.sem["sent"], pid, rid, topo.mask(core, dst)),
-                             "sent", len(topo.engines(core, dst)), ISSUE + more, FLIGHT + more, 16 * (ROW + width / FAR_RATE), (), sent[:1]))
-            sent.append(mine[-1])
-        note(None, [p[0] for p in pairs], [], None, sem, len(pairs) * len(topo.engines(src, core)), 0.0, 0.0, 0.0, mine)
+        mine = [note(nm, "g", [], [a], lambda out=out, a=a: g.remote_dma(out[0], a[0], T.sem[sem], T.sem["sent"], pid, rid, topo.mask(core, dst)),
+                     "sent", len(topo.engines(core, dst))) for out, a in pairs]
+        return note(nm, None, [p[0] for p in pairs], [], None, sem, len(pairs) * len(topo.engines(src, core)), mine)
 
-    def send_state(r, h):
+    def keys_and_send(nm, r, h):
         lo, hi = 128 * h, 128 * h + 128
-        send(r, h, [(u8(A("ldc%d" % r, lo, hi)), u8(A("qtc%d" % r, lo, hi)), 512), (A("lds%d" % r, lo, hi), A("qts%d" % r, lo, hi), 128)])
+        mm(nm + "k%d" % h, BANK[h], "qpc", "qps", 0, "qtc%d" % r, "qts%d" % r, lo, 128)
+        cp(nm + "k%d" % h, "a", A("sk", lo, hi), A(BANK[h], 0, 128))
+        return send(nm + "s%d" % h, r, h, [(u8(A("ldc%d" % r, lo, hi)), u8(A("qtc%d" % r, lo, hi))), (A("lds%d" % r, lo, hi), A("qts%d" % r, lo, hi))])
 
     def col(j):
         return A("cf", j, j + 1)
 
-    dma("s", "x0", A("tw0", 0, 512), T.x[:, 0:512], 128, 1024, True)
-    dma("a", "u", A("ub"), T.u[:], 128, 1024, True)
-    dma("s", "x1", A("tw0", 512, 1024), T.x[:, 512:1024], 128, 1024, True)
-    dma("a", "p", A("pi"), T.p[:], 128, 64, True)
-    dma("s", "wc", u8(A("wqc")), T.wc[:], 128, 2048, True)
-    dma("s", "ws", A("wqs"), T.ws[:], 128, 512, True)
-    dma("s", "v", A("vb"), T.v[:], 128, 1024, True)
+    dma("u", "s", "u", A("ub"), T.u[:])
+    dma("x0", "a", "x0", A("tw0", 0, 512), T.x[:, 0:512])
+    dma("x1", "s", "x1", A("tw0", 512, 1024), T.x[:, 512:1024])
+    dma("p", "s", "p", A("pi"), T.p[:])
+    dma("wc", "s", "wc", u8(A("wqc")), T.wc[:])
+    dma("ws", "s", "ws", A("wqs"), T.ws[:])
 
-    iota(A("pc", 0, 1), [[0, 1]], 0, 1, False)
-    iota(A("i16"), [[0, 16], [1, 16]], 0, 0)
-    iota(A("i128"), [[1, 128]], 0, 0)
-    for pos, cnt, place in RUNS:
-        iota(A("inv", 16 * pos, 16 * (pos + cnt)), [[1, cnt], [16, 16]], place, 0)
-    iota(A("inv", 256, 320), [[1, 64]], 256, 0)
-    fill(A("xx"), 0.0)
-    for k in range(4):
-        fill(A("xx", 32 * k + 1, 32 * k + 4), 1.0)
-        fill(A("xx", 32 * k + 4, 32 * k + 20, 5), 1.0)
-    fill(A("sf", 119, 136), 0.0)
-    pcol = A("pc", 0, 1)
-    ts(A("pc", 1, 2), pcol, 15, ALU.bitwise_and)
-    ts(A("pc", 2, 3), pcol, 4, ALU.logical_shift_right, 1, ALU.bitwise_and)
-    ts(A("pc", 3, 4), pcol, 3, ALU.bitwise_and)
-    ts(A("pc", 4, 5), pcol, 2, ALU.logical_shift_right, 3, ALU.bitwise_and)
-    cp("v", A("cf", 0, 5), A("pc", 0, 5))
-    cp("v", A("si", 16, 17), A("pc", 1, 2))
-    P_, RR, ODD, SL, FI = [col(j) for j in range(5)]
-    i4 = A("i16", 0, 4)
-    ts(col(5), ODD, -1.0, ALU.mult, 1.0, ALU.add)
-    ts(col(19), RR, 256.0, ALU.add)
-    ts(A("ou"), A("i16", 0, 8), 16.0, ALU.mult)
-    ts(A("cf", 8, 12), i4, SL, ALU.is_equal)
-    ts(A("mask"), A("i16"), RR, ALU.is_equal)
-    ts(col(12), col(10), 4.0, ALU.mult, col(9), ALU.add)
-    ts(col(13), col(10), 5.0, ALU.mult, FI, ALU.add)
-    ts(col(14), col(8), -1.0, ALU.mult, 1.0, ALU.add)
-    ts(A("tmp", 16, 32), A("i16", 0, 16), 15.0, ALU.is_lt, 16.0, ALU.mult)
-    ts(col(15), col(12), FI, ALU.add)
-    ts(col(16), col(11), 4.0, ALU.mult, col(13), ALU.add)
-    ts(col(17), col(14), 5.0, ALU.mult)
-    ts(A("c0"), A("tmp", 16, 32), col(19), ALU.add)
-    ts(A("tmp", 0, 4), i4, 4.0, ALU.mult, col(15), ALU.add)
-    ts(col(18), col(16), col(14), ALU.mult, 1.0, ALU.add)
-    ts(A("oz1"), A("tmp", 0, 4), 4.0, ALU.mult, 3.0, ALU.add)
-    ts(A("oz0"), A("tmp", 0, 4), 16.0, ALU.mult, 15.0, ALU.add)
-    ts(A("ox"), i4, col(17), ALU.mult, col(18), ALU.add)
-    ts(A("oc4"), i4, 4.0, ALU.mult, FI, ALU.add)
-    act(A("rst"), A("i16"), ACT.Sign, 0.0, 1.0)
-    act(A("il", 0, 200), A("i16", 0, 200), ACT.Identity, MARK, 0.0)
-    act(A("il", 200, 400), A("i16", 0, 200), ACT.Identity, MARK, 0.0)
-    act(A("kl", 256, 512), A("i16"), ACT.Identity, LOW, 0.0)
-    act(A("kl", 512, 560), A("i16", 0, 48), ACT.Identity, LOW, 0.0)
-    for j in range(0, 1032, 256):
-        w = min(256, 1032 - j)
-        act(A("eb", j, j + w), A("i16", 0, w), ACT.Copy, 0.0, 0.0)
-    ts(A("eb", 2, 514, 4), A("i128"), P_, ALU.is_equal)
-    ts(A("eb", 519, 1031, 4), A("i128"), P_, ALU.is_equal)
+    iota("pc", A("pc", 0, 1), [[0, 1]], 0, 1, False)
+    iota("x5", A("x5"), [[5, 4], [1, 4]], 0, 0)
+    iota("i16", A("i16"), [[0, 16], [1, 16]], 0, 0)
+    iota("i128", A("i128"), [[1, 128]], 0, 0)
+    fill("xz", A("xx"), 0.0)
+    fill("xo", A("xx", 4, 160, 5), 1.0)
+    for c in range(1, 4):
+        fill("xo", A("xx", c, 160, 40), 1.0)
+    fill("eb", A("eb"), 0.0)
+    fill("six", A("six"), 1.0)
+    fill("six0", A("six", 0, 102, 6), 0.0)
+    ts("pc1", A("pc", 1, 2), A("pc", 0, 1), 15, ALU.bitwise_and)
+    ts("pc1", A("pc", 2, 3), A("pc", 0, 1), 31, ALU.bitwise_and)
+    cp("cf", "v", A("cf", 0, 2), A("pc", 0, 2))
+    cp("cf", "v", A("om", 4, 5), A("pc", 2, 3))
+    cp("cf", "v", A("si", 16, 17), A("pc", 1, 2))
+    ts("mask", A("mask"), A("i16"), col(1), ALU.is_equal)
+    ts("ou", A("ou"), A("i16", 0, 8), 16.0, ALU.mult)
+    act("rst", A("rst"), A("i16"), ACT.Sign, 0.0, 1.0)
+    for s, c in enumerate((1.0, 1.0, 6.0, 5.0)):
+        act("val", A("val", s, 64, 4), A("x5"), ACT.Identity, c, 1.0 if s else 0.0)
+    act("val", A("val", 64, 72), A("x5", 0, 8), ACT.Identity, 0.0, 0.0)
+    for s, c in enumerate((1.0, 2.0, 7.0, 6.0, 11.0, 10.0)):
+        act("val", N("val", 72 + s, 12, 6), A("x5", 0, 12), ACT.Identity, c, 1.0 if s else 0.0)
+    for s, c in enumerate((0.0, 1.0, 4.0, 0.0)):
+        act("val", A("val", 144 + s, 208, 4), A("i16", 0, 16), ACT.Identity, c, 1.0)
+    for s, c in enumerate((1.0, 1.0, 6.0, 5.0)):
+        act("val5", A("val", 208 + s, 288, 5), A("x5"), ACT.Identity, c, 1.0 if s else 0.0)
+    act("val5", A("val", 212, 288, 5), A("i16", 0, 16), ACT.Identity, 32.0, 1.0)
+    for s, c in enumerate((0.0, 1.0, 4.0, 0.0)):
+        act("val5", A("val", 288 + s, 368, 5), A("i16", 0, 16), ACT.Identity, 4.0 * c + 3.0, 4.0)
+    act("val5", A("val", 292, 368, 5), A("i16", 0, 16), ACT.Identity, 80.0, 1.0)
+    for nm, lo, hi in (("", 0, 208), ("5", 208, 288), ("6", 288, 368)):
+        tt("vam" + nm, A("vam", lo, hi), A("val", lo, hi), A("mask", 0, hi - lo), ALU.mult)
+        scan("vas" + nm, A("vas", lo, hi), A("rst", 0, hi - lo), A("vam", lo, hi), ALU.mult, ALU.add)
+    cp("ox5", "v", A("ox5", 0, 5), N("vas", 223, 5, 16))
+    cp("oz5", "v", A("oz5", 0, 5), N("vas", 303, 5, 16))
+    place = N("vas", 159, 4, 16)
+    ts("oz", A("tmp", 0, 4), place, 8.0, ALU.is_ge, 20.0, ALU.mult)
+    ts("oz", A("oz0"), place, 16.0, ALU.mult, 15.0, ALU.add)
+    ts("oz", A("oz1"), place, 4.0, ALU.mult, 3.0, ALU.add)
+    cp("ob", "v", A("ox"), N("vas", 15, 4, 16))
+    cp("ob", "v", A("ob", 0, 2), N("vas", 15, 2, 16))
+    cp("ob", "v", A("ob", 2, 7), N("vas", 79, 5, 16))
+    cp("ob", "v", A("ob", 7, 9), N("vas", 47, 2, 16))
+    tt("oza", A("tmp", 4, 8), A("tmp", 0, 4), place, ALU.add)
+    ts("oza", A("oza"), A("tmp", 4, 8), 4.0, ALU.mult, 3.0, ALU.add)
+    ts("cf2", A("cf", 2, 6), A("i16", 0, 4), 16.0, ALU.mult, col(1), ALU.add)
+    ts("cf3", A("cf", 2, 6), A("cf", 2, 6), 256.0, ALU.add)
+    const("pad", A("kl", 256, 320), LOW)
+    const("pad", A("zz", 32, 112), 0.0)
+    const("pad", A("il", 0, 80), col(5))
+    const("pad", A("oo", 144, 240), LOW)
+    const("pad", A("zz", 208, 288), 0.0)
+    for k in range(1, 4):
+        const("pad", A("il", 80 * k + 64, 80 * k + 80), col(5))
+    const("pad", A("il", 335, 336), col(2))
+    ts("e1", A("eb", 2, 514, 4), A("i128"), col(0), ALU.is_equal)
+    ts("e1", A("eb", 519, 1031, 4), A("i128"), col(0), ALU.is_equal)
     for b, o in enumerate((2, 518, 0, 516)):
-        quant("qec", "qes", 128 * b, A("eb", o, o + 512))
-    tt(A("tmp", 32, 48), A("inv", 0, 256, 16), A("mask", 0, 16), ALU.mult)
-    run("v", [col(6)], [A("tmp", 32, 48)], lambda: V.tensor_reduce(T.cf[:, 6:7], T.tmp[:, 32:48], AxisListType.X, ALU.add))
-    ts(A("om", 0, 1), col(6), 4.0, ALU.mult, 3.0, ALU.add)
+        quant("qe%d" % b, "qec", "qes", 128 * b, A("eb", o, o + 512))
 
-    quant("quc", "qus", 0, A("ub"))
-    quant("qyc", "qys", 0, A("vb"))
-    cp("v", u32(A("qpc")), G(A("quc"), A("ou"), True))
-    cp("a", A("qps"), G(A("qus"), A("ou")))
+    quant("qu", "quc", "qus", 0, A("ub"))
+    cp("qp", "v", u32(A("qpc")), G(A("quc"), A("ou"), True))
+    cp("qp", "a", A("qps"), G(A("qus"), A("ou")))
     for h in range(2):
-        quant("qtc0", "qts0", 128 * h, A("tw0", 512 * h, 512 * h + 512))
-        mm("pk%d" % h, "qpc", "qps", 0, "qtc0", "qts0", 128 * h, 128)
-        cp("a", A("sk", 128 * h, 128 * h + 128), A("pk%d" % h, 0, 128))
-        send_state(0, h)
-    ts(A("pa", 0, 16), A("pi"), col(5), ALU.mult)
-    ts(A("pa", 16, 32), A("pi"), ODD, ALU.mult)
-    run("v", [A("pb")], [A("pa")], lambda: V.transpose(T.pb[:], T.pa[:]))
-    tt(A("il", 3, 64, 4), A("pb", 0, 16), A("pb", 16, 32), ALU.add)
-    cp("v", A("oka"), A("il", 3, 64, 4))
-    shift = sorted((place, pos - place) for pos, cnt, place in RUNS)
+        quant("hq%d" % h, "qtc0", "qts0", 128 * h, A("tw0", 512 * h, 512 * h + 512))
+        came = keys_and_send("h", 0, h)
+    dma("v", "s", "v", A("vb"), T.v[:], [came])
+    for h in range(2):
+        cp("pa", "v", A("pa", 16 * h, 16 * h + 16), A("pi"))
+    run("pb", "v", [A("pb")], [A("pa")], lambda: V.transpose(T.pb[:], T.pa[:]))
+    turned = G(A("pb"), A("om", 4, 5))
+    cp("oka", "v", A("oka"), turned)
+    cp("il0", "a", A("il", 3, 64, 4), turned)
+    cp("si", "v", A("si", 0, 16), turned)
     low = A("si", 17, 34)
-    cp("v", A("si", 0, 16), A("il", 3, 64, 4))
-    ts(low, A("si", 0, 17), 15, ALU.bitwise_and)
-    ts(A("si", 34, 51), A("si", 0, 17), 4, ALU.logical_shift_right)
-    ts(A("sf", 0, 17), low, 16.0, ALU.mult)
-    cp("v", A("sf", 17, 34), A("si", 34, 51))
-    for j, (a, b) in enumerate(zip(shift, shift[1:])):
-        ts(A("sf", 34 + 17 * j, 51 + 17 * j), low, float(b[0]), ALU.is_ge, 16.0 * (b[1] - a[1]), ALU.mult)
-    tt(A("sf", 136, 204), A("sf", 0, 68), A("sf", 68, 136), ALU.add)
-    tt(A("sf", 204, 238), A("sf", 136, 170), A("sf", 170, 204), ALU.add)
-    tt(A("sf", 238, 255), A("sf", 204, 221), A("sf", 221, 238), ALU.add)
-    cp("v", A("okb"), A("sf", 238, 254))
-    ts(A("on"), A("i16", 0, 16), A("sf", 254, 255), ALU.add)
+    ts("low", low, A("si", 0, 17), 15, ALU.bitwise_and)
+    ts("low", A("si", 34, 51), A("si", 0, 17), 4, ALU.logical_shift_right)
+    ts("sf0", A("sf", 0, 102, 6), low, 16.0, ALU.mult)
+    cp("sf0", "v", A("sf", 1, 102, 6), A("si", 34, 51))
+    for j, (a, b) in enumerate(SWAPS + [s[::-1] for s in SWAPS]):
+        ts("sf%d" % (1 + j // 2), A("sf", 2 + j, 102, 6), low, float(a), ALU.is_equal, 16.0 * (b - a), ALU.mult)
+    scan("sh", A("sh"), A("six"), A("sf"), ALU.mult, ALU.add)
+    ts("om", A("om", 0, 1), A("sh", 101, 102), 0.3125, ALU.mult, 4.0, ALU.add)
+    cp("okb", "v", A("okb"), N("sh", 5, 16, 6))
+    now[0] = 1
+    ts("sf0", A("on"), A("i16", 0, 16), A("sh", 101, 102), ALU.add)
+    quant("qy", "qyc", "qys", 0, A("vb"))
+    iota("inv", A("inv", 0, 256), [[1, 16], [16, 16]], 0, 0)
+    iota("inv", A("inv", 256, 320), [[1, 64]], 256, 0)
+    for a, b in SWAPS + [s[::-1] for s in SWAPS]:
+        act("inv1", A("inv", 16 * a, 16 * a + 16), A("inv", 16 * a, 16 * a + 16), ACT.Identity, float(b - a), 1.0)
+
+    DN = [("zz", 40), ("oo", 45), ("zz", 216), ("oo", 253)]
+    PARTS = [[(0, 64, "ob", 0, 0), (64, 144, "ob", 4, 64)],
+             [(144, 176, "ox", 0, 160), (176, 208, "ox", 2, 192)],
+             [(208, 240, "ob", 2, 240), (240, 288, "ob", 4, 272)]]
+
+    def dn(k, lo, count, slot=0):
+        return N(DN[k][0], DN[k][1] + 6 * lo + slot, count, 6)
+
+    def keys(k, lo, count):
+        return N("kl", 16 * lo + 15, count, 16) if k == 0 else N("oo", 163 + 4 * lo, count, 4)
+
+    def ids(k, lo=0, count=16):
+        return N("il", 80 * k + 4 * lo + 3, count, 4)
 
     for r in range(R):
+        now[0] = r
         tw, nxt, vv, ar = "tw%d" % r, "tw%d" % (r + 1), "vv%d" % r, "ar%d" % r
         last = r == R - 1
-        kbase = [0, 320, 400, 480]
-
-        def ids(k, lo=0, hi=16):
-            return A("il", 80 * k + 4 * lo + 3, 80 * k + 4 * hi, 4)
-
-        def keys(k, lo, hi):
-            if k == 0:
-                return A("kl", 16 * lo + 15, 16 * hi, 16)
-            return A("kl", kbase[k] + 4 * lo + 3, kbase[k] + 4 * hi, 4)
-
         for h in range(2):
             half = (128 * h, 128 * h + 128)
-            tt(A("km", *half), G(A("sk"), A("oka" if r == 0 else "okb", 8 * h, 8 * h + 8)), A("mask", *half), ALU.mult)
-            scan(A("kl", *half), A("rst", *half), A("km", *half), ALU.mult, ALU.add)
+            tt("km%d" % h, A("km", *half), G(A("sk"), A("oka" if r == 0 else "okb", 8 * h, 8 * h + 8)), A("mask", *half), ALU.mult)
+            scan("kl%d" % h, A("kl", *half), A("rst", *half), A("km", *half), ALU.mult, ALU.add)
         for h in range(2):
-            for b, bank in enumerate([["pr0", "pr1", "pr2", "pr3"], ["pd0", "pd1", "pk0", "pk1"]][h]):
-                mm(bank, "qec", "qes", 128 * b, "ldc%d" % r, "lds%d" % r, 128 * h, 128)
-                cp("a", A("dd%d" % r, 256 * b + 128 * h, 256 * b + 128 * h + 128), A(bank, 0, 128))
+            for b in range(4):
+                mm("u%d%d" % (h, b), BANK[4 * (1 - h) + b], "qec", "qes", 128 * b, "ldc%d" % r, "lds%d" % r, 128 * h, 128)
+                cp("u%d%d" % (h, b), "a", A("dd%d" % r, 256 * b + 128 * h, 256 * b + 128 * h + 128), A(BANK[4 * (1 - h) + b], 0, 128))
         for k in range(4):
-            x, d, z = 32 * k, 16 * k, 64 * k
+            x, z = 40 * k, 64 * k
+            if k % 2 == 0:
+                tt("d%da" % k, dn(k, 0, 3), keys(k, 4, 3), keys(k, 1, 3), ALU.is_gt)
+                tt("d%db" % k, dn(k, 4, 7), keys(k, 8, 7), keys(k, 5, 7), ALU.is_gt)
+                for s, (a, b) in enumerate(((4, 2), (4, 5), (5, 1), (8, 1))):
+                    tt("e%d%d" % (k, s + 1), dn(k, 0, 11, s + 1), keys(k, a, 11), keys(k, b, 11), ALU.is_gt)
+                cp("c%d" % k, "a", dn(k, 0, 11, 5), dn(k, 0, 11))
             if k == 0:
-                tt(A("dn", 0, 11), keys(0, 4, 15), keys(0, 1, 12), ALU.is_gt)
-                cp("a", A("zk", 0, 64), G(A("kl", 0, 320), A("oz0")))
-            else:
-                tt(A("dn", d, d + 3), keys(k, 4, 7), keys(k, 1, 4), ALU.is_gt)
-                tt(A("dn", d + 4, d + 11), keys(k, 8, 15), keys(k, 5, 12), ALU.is_gt)
-                if k < 3:
-                    cp("a", A("zk", z, z + 64), G(A("kl", kbase[k], kbase[k] + 80), A("oz1")))
-            cp("a", A("zi", z, z + 64), G(A("il", 80 * k, 80 * k + 80), A("oz1")))
-            if k == 2:
-                cp("v", A("lso%d" % r, 0, 3), A("il", 3, 164, 80))
-                act(A("l3", 0, 1), ids(2, 1, 2), ACT.Identity, ids(2, 4, 5), -1.0)
-                ts(A("lso%d" % r, 3, 4), A("dn", d, d + 1), A("l3", 0, 1), ALU.mult, ids(2, 1, 2), ALU.add)
-                send(r, 2, [(A("lsi%d" % r), A("lso%d" % r), 8)])
-                act(A("gg", 0, 16), keys(2, 0, 16), ACT.Relu, 16.0, -32.0 / LOW)
-                tt(A("gg", 32, 48), A("gg", 0, 16), A("c0"), ALU.add)
-            zi = A("zi", z, z + 64)
+                cp("z0a", "a", A("zz", 0, 32), G(A("kl"), A("oz0", 0, 2)))
+                cp("z0b", "a", A("zz", 112, 144), G(A("kl"), A("oz0", 2, 4)))
+            if k == 1:
+                cp("z1", "a", A("zz", 144, 208), G(A("oo", 0, 160), A("oza")))
             if k == 3:
-                act(A("gg", 16, 32), keys(3, 0, 16), ACT.Relu, 16.0, -32.0 / LOW)
-                tt(A("gg", 48, 64), A("gg", 32, 48), A("gg", 16, 32), ALU.add)
-                tt(A("zi", 256, 320), G(A("gg", 48, 64), A("oc4")), zi, ALU.min)
-                zi = A("zi", 256, 320)
+                cp("y3", "a", A("zi", z, z + 80), G(A("il", 240, 336), A("oz5", 0, 5)))
+                ts("em3", A("xx", x + 32, x + 48), ids(3), 256.0, ALU.is_ge)
+            elif k or r < 2:
+                cp("y%d" % k if k else "y0s", "a", A("zi", z, z + 64), G(A("il", 80 * k, 80 * k + 80), A("oz1")))
+            if k == 2:
+                cp("la", "v", A("lso%d" % r, 0, 3), A("il", 3, 164, 80))
+                act("l3", A("l3", 0, 1), ids(2, 1, 1), ACT.Identity, ids(2, 4, 1), -1.0)
+                ts("lb", A("lso%d" % r, 3, 4), dn(k, 0, 1), A("l3", 0, 1), ALU.mult, ids(2, 1, 1), ALU.add)
+                send("sl", r, 2, [(A("lsi%d" % r), A("lso%d" % r))])
+                ts("em2", A("em", 0, 15), ids(2, 0, 15), 256.0, ALU.is_ge)
+                act("r2", A("il", 320, 335), A("em", 0, 15), ACT.Identity, col(4), -16.0)
             for i in range(3):
-                scan(A("xx", x + 5 * i + 6, x + 5 * i + 9), A("dn", d + 4 * i, d + 4 * i + 3), A("xx", x + 5 * i + 1, x + 5 * i + 4),
-                     ALU.max, ALU.min)
+                scan("s%d%d" % (k, i), A("xx", x + 5 * i + 6, x + 5 * i + 9), dn(k, 4 * i, 3), A("xx", x + 5 * i + 1, x + 5 * i + 4), ALU.max, ALU.min)
             if k < 3:
+                for h, (lo, hi, lst, c, o) in enumerate(PARTS[k]):
+                    nm = "%d%s" % (k, "ab"[h])
+                    path = G(A("xx", x, x + 16 * h + 16), A(lst, c, c + (hi - lo) // 16))
+                    act("n" + nm, A("nn", lo, hi), path, ACT.Identity, 1.0, -1.0)
+                    tt("p" + nm, A("pp", lo, hi), path, A("zz", lo, hi), ALU.mult)
+                    scan("o" + nm, A("oo", o, o + hi - lo), A("nn", lo, hi), A("pp", lo, hi), ALU.mult, ALU.add)
+            if k == 1:
                 for h in range(2):
-                    path = G(A("xx", x, x + 16 * h + 16), A("ox", 2 * h, 2 * h + 2))
-                    lo, hi = z + 32 * h, z + 32 * h + 32
-                    act(A("nx", lo, hi), path, ACT.Identity, 1.0, -1.0)
-                    tt(A("pk", lo, hi), path, A("zk", lo, hi), ALU.mult)
-                    scan(A("kl", kbase[k + 1] + 32 * h, kbase[k + 1] + 32 * h + 32), A("nx", lo, hi), A("pk", lo, hi), ALU.mult, ALU.add)
-            else:
-                act(A("nx", z, z + 64), G(A("xx", x, x + 32), A("ox")), ACT.Identity, 1.0, -1.0)
-            tt(A("pj", z, z + 64), G(A("xx", x, x + 32), A("ox")), zi, ALU.mult)
-            scan(A("il", 80 * k + 80, 80 * k + 144), A("nx", z, z + 64), A("pj", z, z + 64), ALU.mult, ALU.add)
-        where = G(A("il", 320, 384), A("om", 0, 1))
+                    lo = z + 32 * h
+                    tt("j1" + "ab"[h], A("pj", lo, lo + 32), G(A("xx", x, x + 16 * h + 16), A("ox", 2 * h, 2 * h + 2)), A("zi", lo, lo + 32), ALU.mult)
+                    scan("i1" + "ab"[h], A("il", 160 + 32 * h, 192 + 32 * h), A("nn", 144 + 32 * h, 176 + 32 * h), A("pj", lo, lo + 32), ALU.mult, ALU.add)
+                continue
+            w, o = (80, 336) if k == 3 else (64, 80 * k + 80)
+            path = G(A("xx", x, x + 48), A("ox5", 0, 5)) if k == 3 else G(A("xx", x, x + 32), A("ox"))
+            act("m%d" % k, A("ni", z, z + w), path, ACT.Identity, 1.0, -1.0)
+            tt("j%d" % k, A("pj", z, z + w), path, A("zi", z, z + w), ALU.mult)
+            scan("i%d" % k, A("il", o, o + w), A("ni", z, z + w), A("pj", z, z + w), ALU.mult, ALU.add)
+        where = G(A("il", 336, 416), A("om", 0, 1))
         for t in range(4):
-            ts(A("ov", 16 * t, 16 * t + 16), where, 4.0, ALU.mult, float(t), ALU.add)
+            ts("a%d" % t, A("ov", 16 * t, 16 * t + 16), where, 4.0, ALU.mult, float(t), ALU.add)
         if r == 0:
-            cp("a", ids(0), A("sf", 238, 254))
+            cp("ilb", "a", ids(0), N("sh", 5, 16, 6))
         if last:
-            cp("v", A("ot"), where)
-            cp("a", A("o1"), G(A("inv"), A("ot")))
-            cp("a", A("o2"), G(A("o1"), A("on")))
-            dma("s", "ol", T.ol[:], (T.o2[0:128:16, :],) + A("o2")[1:], 8, 1024)
+            cp("ot", "v", A("ot"), where)
+            cp("o1", "a", A("o1"), G(A("inv"), A("ot")))
+            cp("o2", "a", A("o2"), G(A("o1"), A("on")))
+            dma("ol", "s", "ol", T.ol[:], (T.o2[0:128:16, :],) + A("o2")[1:])
         for b in range(4):
-            cp(PICK_F[b], A(tw, 1024 + b, 1280, 4), G(A("dd%d" % r, 256 * b, 256 * b + 256), A("lsi%d" % r)))
+            cp("f%d" % b, PICK_F[b], A(tw, 1024 + b, 1280, 4), G(A("dd%d" % r, 256 * b, 256 * b + 256), A("lsi%d" % r)))
         for h in range(2):
             for t in range(4):
-                cp(PICK_V[h][t], A(vv, 512 * h + t, 512 * h + 512, 4),
-                   G(A(tw, 0, 1024 + 256 * h), A("ov", 16 * t + 8 * h, 16 * t + 8 * h + 8)))
-            quant("qvc%d" % r, "qvs%d" % r, 128 * h, A(vv, 512 * h, 512 * h + 512))
+                cp("g%d%d" % (h, t), PICK_V[h][t], A(vv, 512 * h + t, 512 * h + 512, 4),
+                   G(A(tw, 0, 1024 + 256 * h), A("ov", 8 * h + 16 * t, 8 * h + 16 * t + 8)))
+            quant("q%d" % h, "qvc%d" % r, "qvs%d" % r, 128 * h, A(vv, 512 * h, 512 * h + 512))
             for b in range(4):
-                mm("pr%d" % b, "wqc", "wqs", 128 * b, "qvc%d" % r, "qvs%d" % r, 128 * h, 128)
-                act(A(ar, 512 * h + 128 * b, 512 * h + 128 * b + 128), A("pr%d" % b, 0, 128), ACT.Relu, 0.0, 0.015625)
-                tt(A(nxt, 512 * h + b, 512 * h + 512, 4), A(ar, 512 * h + 128 * b, 512 * h + 128 * b + 128),
-                   A(vv, 512 * h + b, 512 * h + 512, 4), ALU.add)
-            quant("qtc%d" % (r + 1), "qts%d" % (r + 1), 128 * h, A(nxt, 512 * h, 512 * h + 512))
-            if not last:
-                send_state(r + 1, h)
-                mm("pk%d" % h, "qpc", "qps", 0, "qtc%d" % (r + 1), "qts%d" % (r + 1), 128 * h, 128)
-                cp("a", A("sk", 128 * h, 128 * h + 128), A("pk%d" % h, 0, 128))
+                lo = 512 * h + 128 * b
+                mm("r%d%d" % (h, b), BANK[4 * h + b], "wqc", "wqs", 128 * b, "qvc%d" % r, "qvs%d" % r, 128 * h, 128)
+                act("r%d%d" % (h, b), A(ar, lo, lo + 128), A(BANK[4 * h + b], 0, 128), ACT.Relu, 0.0, 0.015625)
+                tt("t%d%d" % (h, b), A(nxt, 512 * h + b, 512 * h + 512, 4), A(ar, lo, lo + 128), A(vv, 512 * h + b, 512 * h + 512, 4), ALU.add)
+            quant("qt%d" % h, "qtc%d" % (r + 1), "qts%d" % (r + 1), 128 * h, A(nxt, 512 * h, 512 * h + 512))
+        if not last:
+            for h in range(2):
+                keys_and_send("", r + 1, h)
 
-    cp("v", u32(A("qnc")), G(A("qtc3"), A("on"), True))
-    cp("a", A("qns"), G(A("qts3"), A("on")))
-    dma("s", "oc", T.oc[:], u8(A("qnc")), 128, 1024)
+    for h in range(2):
+        mm("k%d" % h, BANK[h], "qyc", "qys", 0, "qtc3", "qts3", 128 * h, 128)
+        cp("k%d" % h, "a", A("yi", 128 * h, 128 * h + 128), A(BANK[h], 0, 128))
+        cp("n%d" % h, "v", u32(A("qnc", 128 * h, 128 * h + 128)), G(A("qtc3"), A("on", 8 * h, 8 * h + 8), True))
+        cp("n%d" % h, "a", A("qns", 128 * h, 128 * h + 128), G(A("qts3"), A("on", 8 * h, 8 * h + 8)))
+    dma("oc", "s", "oc", T.oc[:], u8(A("qnc")))
     for k in range(4):
-        dma("ssaa"[k], "os%d" % k, T.osc[4 * k:4 * k + 4, :], (T.qns[32 * k:32 * k + 4, :],) + A("qns")[1:], 4, 256)
+        dma("os", "s", "os%d" % k, T.osc[4 * k:4 * k + 4, :], (T.qns[32 * k:32 * k + 4, :],) + A("qns")[1:])
     for h in range(2):
-        mm("pk%d" % h, "qyc", "qys", 0, "qtc3", "qts3", 128 * h, 128)
-        cp("av"[h], A("yi", 128 * h, 128 * h + 128), A("pk%d" % h, 0, 128))
-    for h in range(2):
-        cp("va"[h], A("ys", 128 * h, 128 * h + 128), G(A("yi"), A("on", 8 * h, 8 * h + 8)))
-        dma("sa"[h], "y%d" % h, T.y[:, 128 * h:128 * h + 128], A("ys", 128 * h, 128 * h + 128), 128, 512)
+        cp("y%d" % h + "g", "va"[h], A("ys", 128 * h, 128 * h + 128), G(A("yi"), A("on", 8 * h, 8 * h + 8)))
+    dma("yd", "a", "y", T.y[:], A("ys"))
 
     known = {q: {} for q in queues}
     count, seen, token = {}, {}, {}
-    if not PLAN:
-        PLAN.append(order(ops))
-    for i in PLAN[-1]:
-        q, deps, call, sem, inc = ops[i][0], ops[i][1], ops[i][6], ops[i][7], ops[i][8]
+    for i in order(ops):
+        q, deps, call, sem, inc = ops[i][0], ops[i][1], ops[i][4], ops[i][5], ops[i][6]
         if q:
             want = {}
             for d in deps:

@@ -8,22 +8,24 @@ LOW = -9.0e29
 SWAPS = [(3, 8), (7, 9)]
 PICK_F, PICK_V = "vvaa", ["vvaa", "vvaa"]
 HEAD = {
-    "s": "u p x1 ws wc",
+    "s": "x0 u x1 p ws wc",
     "g": "x5 pc i16 i128 hs0 hs1",
-    "v": "six eb pc1 xz six0 cf xo mask e1 cf2 vam hq0 cf3 qe1 vas ou qu pa qe0 qp pb qe2 hq1 oz ob oka oza si",
-    "a": "x0 val val5 rst qp pad il0 hk0 hk1",
+    "v": "xz eb pc1 xf six cf xo ou mask e1 cf2 vam hq0 qu vas cf3 qp hq1 qe0 pa ob pb oz oka si qe2",
+    "a": "val val3 rst val4 qp pad hk0 hk1 il0",
     "t": "hk0 hk1",
 }
 ROUND = {
-    "s": "v ol oc os",
-    "g": "inv sl s0 s1",
-    "v": "qy km0 km1 kl0 kl1 d0a low d0b s00 e04 e02 e03 s01 e01 qe3 s02 p0a p0b o0a j0 o0b "
-         "s10 sf2 i0 sf0 s11 sf1 vam5 s12 p1a j1a p1b o1a i1a j1b o1b d2a la i1b d2b "
-         "s20 lb e21 e24 s21 e22 e23 vas5 em2 s22 vam6 p2a p2b vas6 o2a j2 o2b "
-         "s30 oz5 i2 s31 ox5 em3 s32 sh j3 om i3 a2 a0 a1 a3 "
-         "g00 g01 f1 f0 q0 g10 g11 ot okb q1 t00 t01 t02 t03 t10 qt0 t11 t12 t13 qt1 n1 n0 y0g",
-    "a": "y0s z0b z0a c0 inv1 n0a n0b m0 z1 y1 n1a n1b l3 u00 u01 c2 y2 n2a u02 n2b m2 u03 r2 y3 m3 u10 u11 u12 u13 "
-         "g02 g03 f3 f2 g12 g13 r00 r01 r02 r03 r10 r11 r12 r13 o1 k0 o2 n1 ilb k1 n0 y1g yd",
+    "s": "v ol oc0 oc1 os",
+    "g": "inv sl s1",
+    "v": "km0 km1 kl0 qe1 kl1 d0a qy oza low d0b s00 e03 e01 e04 s01 e02 qe3 s02 p0a ozb p0b o0a j0 o0b "
+         "s10 sf1 i0 s11 sf2 sf0 s12 p1a vam5 p1b o1a j1 o1b d2a vam6 i1 d2b "
+         "s20 e21 e22 e23 e24 s21 vas6 la lb s22 p2a em2 vas5 p2b o2a j2 o2b "
+         "s30 oz5 six0 i2 s31 ox5 sh em3 s32 om j3 i3 i4 "
+         "a2 a0 a3 a1 g00 g01 f1 f0 q0 g11 g10 q1 t00 t00b t01 t02 t03 t10 t11 t12 t13 qt0 okb qt1 "
+         "turn zf0 zf1 za0 za2 za1 za3 ot zg00 zg01 zg10 zq0 zg11 zq1 zt00 zt00b zt01 zt02 zt03 zt10 zqt0 zt11 zt12 zt13 zqt1",
+    "a": "y0s z0b c0 z0a inv1 n0a n0b m0 z1 y1 n1a n1b l3 c2 y2 n2a n2b r2 m2 u00 u01 y3 u02 m3 u03 u10 u11 u12 u13 "
+         "g02 g03 f2 f3 g13 g12 r00 r00b r01 r02 r03 r10 r11 r12 r13 k0 ilb k1 "
+         "zf2 zf3 zg02 zg03 zg13 zg12 o1 zr00 zr00b zr01 zr02 zr03 zr10 zr11 zr12 zr13 yp0 y0d yp1 y1d",
     "t": "u00 u01 u02 u03 u10 u11 u12 u13 r00 r01 r02 r03 r10 r11 r12 r13 k0 k1",
 }
 
@@ -55,26 +57,25 @@ for _n, _w, _d in [
     ("quc", 128, CODES), ("qus", 128, "uint8"), ("qpc", 128, CODES), ("qps", 128, "uint8"),
     ("qyc", 128, CODES), ("qys", 128, "uint8"), ("wqc", 512, CODES), ("wqs", 512, "uint8"),
     ("eb", 1032, "bfloat16"), ("qec", 512, CODES), ("qes", 512, "uint8"),
-    ("qnc", 256, CODES), ("qns", 256, "uint8"), ("ys", 256, "float32"), ("yi", 256, "float32"),
+    ("ys", 256, "float32"), ("o1", 256, "float32"),
     ("pc", 4, "int32"), ("cf", 8, "float32"), ("i16", 256, "float32"), ("i128", 128, "float32"), ("x5", 16, "float32"),
     ("mask", 256, "float32"), ("rst", 256, "float32"), ("six", 102, "float32"), ("inv", 320, "float32"),
-    ("val", 368, "float32"), ("vam", 368, "float32"), ("vas", 368, "float32"), ("tmp", 8, "float32"),
+    ("val", 336, "float32"), ("vam", 336, "float32"), ("vas", 336, "float32"), ("tmp", 8, "float32"),
     ("si", 51, "int32"), ("sf", 102, "float32"), ("sh", 102, "float32"),
     ("oz0", 4, "uint16"), ("oza", 4, "uint16"), ("oz1", 4, "uint16"), ("ox", 4, "uint16"), ("ob", 10, "uint16"), ("ou", 8, "uint16"),
-    ("ox5", 6, "uint16"), ("oz5", 6, "uint16"),
-    ("om", 6, "uint16"), ("on", 16, "uint16"), ("oka", 16, "uint16"), ("okb", 16, "uint16"), ("ov", 64, "uint16"), ("ot", 16, "uint16"),
+    ("ox3", 4, "uint16"), ("oz3", 4, "uint16"),
+    ("om", 6, "uint16"), ("oka", 16, "uint16"), ("okb", 16, "uint16"), ("ov", 64, "uint16"), ("ot", 16, "uint16"),
     ("pa", 32, "float32"), ("pb", 32, "float32"),
-    ("sk", 256, "float32"), ("km", 256, "float32"), ("kl", 320, "float32"), ("il", 416, "float32"), ("xx", 168, "float32"),
+    ("sk", 256, "float32"), ("km", 256, "float32"), ("kl", 320, "float32"), ("il", 464, "float32"), ("xx", 168, "float32"),
     ("zz", 288, "float32"), ("nn", 288, "float32"), ("pp", 288, "float32"), ("oo", 320, "float32"),
-    ("zi", 272, "float32"), ("ni", 272, "float32"), ("pj", 272, "float32"), ("em", 16, "float32"), ("l3", 2, "float32"),
-    ("o1", 256, "float32"), ("o2", 256, "float32"),
+    ("zi", 256, "float32"), ("ni", 256, "float32"), ("pj", 256, "float32"), ("em", 16, "float32"), ("l3", 2, "float32"),
 ]:
     _buf(_n, _w, _d)
 BANK = ["ps%d" % _b for _b in range(8)]
 for _n in BANK:
     _buf(_n, 512, "float32", "psum")
 
-DMAS = ["x0", "x1", "u", "p", "wc", "ws", "v", "y", "ol", "oc", "os0", "os1", "os2", "os3"]
+DMAS = ["x0", "x1", "u", "p", "wc", "ws", "v", "y0", "y1", "ol", "oc0", "oc1", "os0", "os1", "os2", "os3"]
 SEMAPHORES = (["sv", "sa", "st", "sg", "sent"] + ["m_" + n for n in DMAS]
               + ["in%d_%d" % (r, k) for r in range(R) for k in range(3)])
 
@@ -130,17 +131,16 @@ def rank_program(g, core, T, topo):
         reads, writes, deps = regs(ins), regs(outs), set(more)
         for rs, wr in ((reads, False), (writes, True)):
             for (name, lo, hi, st) in rs:
-                excl = wr or SCRATCH[name][0] == "psum"
+                bank = SCRATCH[name][0] == "psum"
                 for (l2, h2, s2, w2, i) in log.get(name, []):
-                    if l2 < hi and lo < h2 and (excl or w2) and not (st == s2 and (lo - l2) % st):
+                    if l2 < hi and lo < h2 and (wr or w2 or bank and ops[i][0] != q) and not (st == s2 and (lo - l2) % st):
                         deps.add(i)
         for rs, wr in ((reads, False), (writes, True)):
             for (name, lo, hi, st) in rs:
-                w = wr or SCRATCH[name][0] == "psum"
                 old = log.get(name, [])
-                if w:
+                if wr:
                     old = [e for e in old if not (lo <= e[0] and e[1] <= hi and (st == 1 or (st == e[2] and (lo - e[0]) % st == 0)))]
-                log[name] = old + [(lo, hi, st, w, len(ops))]
+                log[name] = old + [(lo, hi, st, wr, len(ops))]
         ops.append((q, sorted(deps), nm, now[0], call, sem, inc))
         return len(ops) - 1
 
@@ -212,13 +212,16 @@ def rank_program(g, core, T, topo):
         lo, hi = 128 * h, 128 * h + 128
         mm(nm + "k%d" % h, BANK[h], "qpc", "qps", 0, "qtc%d" % r, "qts%d" % r, lo, 128)
         cp(nm + "k%d" % h, "a", A("sk", lo, hi), A(BANK[h], 0, 128))
-        return send(nm + "s%d" % h, r, h, [(u8(A("ldc%d" % r, lo, hi)), u8(A("qtc%d" % r, lo, hi))), (A("lds%d" % r, lo, hi), A("qts%d" % r, lo, hi))])
+        if r:
+            lo = 0
+        if h or not r:
+            return send(nm + "s%d" % h, r, h, [(u8(A("ldc%d" % r, lo, hi)), u8(A("qtc%d" % r, lo, hi))), (A("lds%d" % r, lo, hi), A("qts%d" % r, lo, hi))])
 
     def col(j):
         return A("cf", j, j + 1)
 
     dma("u", "s", "u", A("ub"), T.u[:])
-    dma("x0", "a", "x0", A("tw0", 0, 512), T.x[:, 0:512])
+    dma("x0", "s", "x0", A("tw0", 0, 512), T.x[:, 0:512])
     dma("x1", "s", "x1", A("tw0", 512, 1024), T.x[:, 512:1024])
     dma("p", "s", "p", A("pi"), T.p[:])
     dma("wc", "s", "wc", u8(A("wqc")), T.wc[:])
@@ -229,7 +232,7 @@ def rank_program(g, core, T, topo):
     iota("i16", A("i16"), [[0, 16], [1, 16]], 0, 0)
     iota("i128", A("i128"), [[1, 128]], 0, 0)
     fill("xz", A("xx"), 0.0)
-    fill("xo", A("xx", 4, 160, 5), 1.0)
+    fill("xf", A("xx", 4, 160, 5), 1.0)
     for c in range(1, 4):
         fill("xo", A("xx", c, 160, 40), 1.0)
     fill("eb", A("eb"), 0.0)
@@ -250,17 +253,19 @@ def rank_program(g, core, T, topo):
         act("val", N("val", 72 + s, 12, 6), A("x5", 0, 12), ACT.Identity, c, 1.0 if s else 0.0)
     for s, c in enumerate((0.0, 1.0, 4.0, 0.0)):
         act("val", A("val", 144 + s, 208, 4), A("i16", 0, 16), ACT.Identity, c, 1.0)
-    for s, c in enumerate((1.0, 1.0, 6.0, 5.0)):
-        act("val5", A("val", 208 + s, 288, 5), A("x5"), ACT.Identity, c, 1.0 if s else 0.0)
-    act("val5", A("val", 212, 288, 5), A("i16", 0, 16), ACT.Identity, 32.0, 1.0)
-    for s, c in enumerate((0.0, 1.0, 4.0, 0.0)):
-        act("val5", A("val", 288 + s, 368, 5), A("i16", 0, 16), ACT.Identity, 4.0 * c + 3.0, 4.0)
-    act("val5", A("val", 292, 368, 5), A("i16", 0, 16), ACT.Identity, 80.0, 1.0)
-    for nm, lo, hi in (("", 0, 208), ("5", 208, 288), ("6", 288, 368)):
+    act("val3", A("val", 208, 272), A("val", 0, 64), ACT.Identity, 0.0, 1.0)
+    act("val3", A("val", 272, 336), A("val", 144, 208), ACT.Identity, 3.0, 4.0)
+    act("val4", N("val", 222, 3, 16), N("x5", 3, 3, 4), ACT.Identity, 5.0, 1.0)
+    for base, c in ((208, 32.0), (272, 80.0)):
+        act("val4", N("val", base + 15, 3, 16), N("i16", 3, 3, 4), ACT.Identity, c, 1.0)
+        act("val4", N("val", base + 50, 4, 4), A("i16", 12, 16), ACT.Identity, c, 1.0)
+    for s, c in ((1, 19.0), (2, 3.0)):
+        act("val4", N("val", 284 + s, 3, 16), N("i16", 3, 3, 4), ACT.Identity, c, 4.0)
+    for nm, lo, hi in (("", 0, 208), ("5", 208, 272), ("6", 272, 336)):
         tt("vam" + nm, A("vam", lo, hi), A("val", lo, hi), A("mask", 0, hi - lo), ALU.mult)
         scan("vas" + nm, A("vas", lo, hi), A("rst", 0, hi - lo), A("vam", lo, hi), ALU.mult, ALU.add)
-    cp("ox5", "v", A("ox5", 0, 5), N("vas", 223, 5, 16))
-    cp("oz5", "v", A("oz5", 0, 5), N("vas", 303, 5, 16))
+    cp("ox5", "v", A("ox3"), N("vas", 223, 4, 16))
+    cp("oz5", "v", A("oz3"), N("vas", 287, 4, 16))
     place = N("vas", 159, 4, 16)
     ts("oz", A("tmp", 0, 4), place, 8.0, ALU.is_ge, 20.0, ALU.mult)
     ts("oz", A("oz0"), place, 16.0, ALU.mult, 15.0, ALU.add)
@@ -270,7 +275,7 @@ def rank_program(g, core, T, topo):
     cp("ob", "v", A("ob", 2, 7), N("vas", 79, 5, 16))
     cp("ob", "v", A("ob", 7, 9), N("vas", 47, 2, 16))
     tt("oza", A("tmp", 4, 8), A("tmp", 0, 4), place, ALU.add)
-    ts("oza", A("oza"), A("tmp", 4, 8), 4.0, ALU.mult, 3.0, ALU.add)
+    ts("ozb", A("oza"), A("tmp", 4, 8), 4.0, ALU.mult, 3.0, ALU.add)
     ts("cf2", A("cf", 2, 6), A("i16", 0, 4), 16.0, ALU.mult, col(1), ALU.add)
     ts("cf3", A("cf", 2, 6), A("cf", 2, 6), 256.0, ALU.add)
     const("pad", A("kl", 256, 320), LOW)
@@ -308,10 +313,9 @@ def rank_program(g, core, T, topo):
     for j, (a, b) in enumerate(SWAPS + [s[::-1] for s in SWAPS]):
         ts("sf%d" % (1 + j // 2), A("sf", 2 + j, 102, 6), low, float(a), ALU.is_equal, 16.0 * (b - a), ALU.mult)
     scan("sh", A("sh"), A("six"), A("sf"), ALU.mult, ALU.add)
-    ts("om", A("om", 0, 1), A("sh", 101, 102), 0.3125, ALU.mult, 4.0, ALU.add)
+    ts("om", A("om", 0, 1), A("sh", 101, 102), 0.25, ALU.mult, 3.0, ALU.add)
     cp("okb", "v", A("okb"), N("sh", 5, 16, 6))
     now[0] = 1
-    ts("sf0", A("on"), A("i16", 0, 16), A("sh", 101, 102), ALU.add)
     quant("qy", "qyc", "qys", 0, A("vb"))
     iota("inv", A("inv", 0, 256), [[1, 16], [16, 16]], 0, 0)
     iota("inv", A("inv", 256, 320), [[1, 64]], 256, 0)
@@ -358,7 +362,7 @@ def rank_program(g, core, T, topo):
             if k == 1:
                 cp("z1", "a", A("zz", 144, 208), G(A("oo", 0, 160), A("oza")))
             if k == 3:
-                cp("y3", "a", A("zi", z, z + 80), G(A("il", 240, 336), A("oz5", 0, 5)))
+                cp("y3", "a", A("zi", z, z + 64), G(A("il", 240, 336), A("oz3")))
                 ts("em3", A("xx", x + 32, x + 48), ids(3), 256.0, ALU.is_ge)
             elif k or r < 2:
                 cp("y%d" % k if k else "y0s", "a", A("zi", z, z + 64), G(A("il", 80 * k, 80 * k + 80), A("oz1")))
@@ -378,55 +382,53 @@ def rank_program(g, core, T, topo):
                     act("n" + nm, A("nn", lo, hi), path, ACT.Identity, 1.0, -1.0)
                     tt("p" + nm, A("pp", lo, hi), path, A("zz", lo, hi), ALU.mult)
                     scan("o" + nm, A("oo", o, o + hi - lo), A("nn", lo, hi), A("pp", lo, hi), ALU.mult, ALU.add)
-            if k == 1:
-                for h in range(2):
-                    lo = z + 32 * h
-                    tt("j1" + "ab"[h], A("pj", lo, lo + 32), G(A("xx", x, x + 16 * h + 16), A("ox", 2 * h, 2 * h + 2)), A("zi", lo, lo + 32), ALU.mult)
-                    scan("i1" + "ab"[h], A("il", 160 + 32 * h, 192 + 32 * h), A("nn", 144 + 32 * h, 176 + 32 * h), A("pj", lo, lo + 32), ALU.mult, ALU.add)
-                continue
-            w, o = (80, 336) if k == 3 else (64, 80 * k + 80)
-            path = G(A("xx", x, x + 48), A("ox5", 0, 5)) if k == 3 else G(A("xx", x, x + 32), A("ox"))
-            act("m%d" % k, A("ni", z, z + w), path, ACT.Identity, 1.0, -1.0)
-            tt("j%d" % k, A("pj", z, z + w), path, A("zi", z, z + w), ALU.mult)
-            scan("i%d" % k, A("il", o, o + w), A("ni", z, z + w), A("pj", z, z + w), ALU.mult, ALU.add)
-        where = G(A("il", 336, 416), A("om", 0, 1))
-        for t in range(4):
-            ts("a%d" % t, A("ov", 16 * t, 16 * t + 16), where, 4.0, ALU.mult, float(t), ALU.add)
-        if r == 0:
-            cp("ilb", "a", ids(0), N("sh", 5, 16, 6))
+            path = G(A("xx", x, x + 48), A("ox3")) if k == 3 else G(A("xx", x, x + 32), A("ox"))
+            nx = A("nn", 144, 208)
+            if k != 1:
+                nx = A("ni", z, z + 64)
+                act("m%d" % k, nx, path, ACT.Identity, 1.0, -1.0)
+            tt("j%d" % k, A("pj", z, z + 64), path, A("zi", z, z + 64), ALU.mult)
+            o = 336 if k == 3 else 80 * k + 80
+            scan("i%d" % k, A("il", o, o + 64), nx, A("pj", z, z + 64), ALU.mult, ALU.add)
+        where, e = G(A("il", 336, 400), A("om", 0, 1)), ""
         if last:
+            scan("i4", A("il", 400, 464), nx, A("pj", z, z + 64), ALU.mult, ALU.add)
+            twice = N("il", 339, 32, 4)
+            run("turn", "v", [A("pb")], [twice], lambda: V.transpose(T.pb[:], twice[0]))
+            where, e = turned, "z"
             cp("ot", "v", A("ot"), where)
             cp("o1", "a", A("o1"), G(A("inv"), A("ot")))
-            cp("o2", "a", A("o2"), G(A("o1"), A("on")))
-            dma("ol", "s", "ol", T.ol[:], (T.o2[0:128:16, :],) + A("o2")[1:])
+            dma("ol", "s", "ol", T.ol[:], (T.o1[0:128:16, :],) + A("o1")[1:])
+        for t in range(4):
+            ts(e + "a%d" % t, A("ov", 16 * t, 16 * t + 16), where, 4.0, ALU.mult, float(t), ALU.add)
+        if r == 0:
+            cp("ilb", "a", ids(0), N("sh", 5, 16, 6))
         for b in range(4):
-            cp("f%d" % b, PICK_F[b], A(tw, 1024 + b, 1280, 4), G(A("dd%d" % r, 256 * b, 256 * b + 256), A("lsi%d" % r)))
+            cp(e + "f%d" % b, PICK_F[b], A(tw, 1024 + b, 1280, 4), G(A("dd%d" % r, 256 * b, 256 * b + 256), A("lsi%d" % r)))
         for h in range(2):
             for t in range(4):
-                cp("g%d%d" % (h, t), PICK_V[h][t], A(vv, 512 * h + t, 512 * h + 512, 4),
-                   G(A(tw, 0, 1024 + 256 * h), A("ov", 8 * h + 16 * t, 8 * h + 16 * t + 8)))
-            quant("q%d" % h, "qvc%d" % r, "qvs%d" % r, 128 * h, A(vv, 512 * h, 512 * h + 512))
+                cp(e + "g%d%d" % (h, t), PICK_V[h][t], A(vv, 512 * h + t, 512 * h + 512, 4),
+                   G(A(tw, 0, 1280 if h or last else 1024), A("ov", 8 * h + 16 * t, 8 * h + 16 * t + 8)))
+            quant(e + "q%d" % h, "qvc%d" % r, "qvs%d" % r, 128 * h, A(vv, 512 * h, 512 * h + 512))
             for b in range(4):
-                lo = 512 * h + 128 * b
                 mm("r%d%d" % (h, b), BANK[4 * h + b], "wqc", "wqs", 128 * b, "qvc%d" % r, "qvs%d" % r, 128 * h, 128)
-                act("r%d%d" % (h, b), A(ar, lo, lo + 128), A(BANK[4 * h + b], 0, 128), ACT.Relu, 0.0, 0.015625)
-                tt("t%d%d" % (h, b), A(nxt, 512 * h + b, 512 * h + 512, 4), A(ar, lo, lo + 128), A(vv, 512 * h + b, 512 * h + 512, 4), ALU.add)
-            quant("qt%d" % h, "qtc%d" % (r + 1), "qts%d" % (r + 1), 128 * h, A(nxt, 512 * h, 512 * h + 512))
+                for c, w in ((0, 64), (64, 64)) if h + b == 0 else ((0, 128),):
+                    nm, lo, at = "%d%d" % (h, b) + "b" * (c > 0), 512 * h + 128 * b + c, 512 * h + 4 * c + b
+                    act(e + "r" + nm, A(ar, lo, lo + w), A(BANK[4 * h + b], c, c + w), ACT.Relu, 0.0, 0.015625)
+                    tt(e + "t" + nm, N(nxt, at, w, 4), A(ar, lo, lo + w), N(vv, at, w, 4), ALU.add)
+            quant(e + "qt%d" % h, "qtc%d" % (r + 1), "qts%d" % (r + 1), 128 * h, A(nxt, 512 * h, 512 * h + 512))
         if not last:
             for h in range(2):
                 keys_and_send("", r + 1, h)
 
     for h in range(2):
-        mm("k%d" % h, BANK[h], "qyc", "qys", 0, "qtc3", "qts3", 128 * h, 128)
-        cp("k%d" % h, "a", A("yi", 128 * h, 128 * h + 128), A(BANK[h], 0, 128))
-        cp("n%d" % h, "v", u32(A("qnc", 128 * h, 128 * h + 128)), G(A("qtc3"), A("on", 8 * h, 8 * h + 8), True))
-        cp("n%d" % h, "a", A("qns", 128 * h, 128 * h + 128), G(A("qts3"), A("on", 8 * h, 8 * h + 8)))
-    dma("oc", "s", "oc", T.oc[:], u8(A("qnc")))
+        lo, hi = 128 * h, 128 * h + 128
+        dma("oc%d" % h, "s", "oc%d" % h, T.oc[:, 4 * lo:4 * hi], u8(A("qtc3", lo, hi)))
+        mm("k%d" % h, BANK[h], "qyc", "qys", 0, "qtc3", "qts3", lo, 128)
+        cp("yp%d" % h, "a", A("ys", lo, hi), A(BANK[h], 0, 128))
+        dma("y%d" % h + "d", "a", "y%d" % h, T.y[:, lo:hi], A("ys", lo, hi))
     for k in range(4):
-        dma("os", "s", "os%d" % k, T.osc[4 * k:4 * k + 4, :], (T.qns[32 * k:32 * k + 4, :],) + A("qns")[1:])
-    for h in range(2):
-        cp("y%d" % h + "g", "va"[h], A("ys", 128 * h, 128 * h + 128), G(A("yi"), A("on", 8 * h, 8 * h + 8)))
-    dma("yd", "a", "y", T.y[:], A("ys"))
+        dma("os", "s", "os%d" % k, T.osc[4 * k:4 * k + 4, :], (T.qts3[32 * k:32 * k + 4, :],) + A("qts3")[1:])
 
     known = {q: {} for q in queues}
     count, seen, token = {}, {}, {}

@@ -1,3 +1,4 @@
+import math
 from concourse.mybir import dt, AluOpType, ActivationFunctionType
 
 ALU = AluOpType
@@ -10,21 +11,22 @@ PICK_F, PICK_V = "vvaa", ["vvaa", "vvaa"]
 HEAD = {
     "s": "x0 u x1 p ws wc",
     "g": "x5 pc i16 i128 hs0 hs1",
-    "v": "xz eb pc1 xf six cf xo ou mask e1 cf2 vam hq0 qu vas cf3 qp hq1 qe0 pa ob pb oz oka si qe2",
-    "a": "val val3 rst val4 qp pad hk0 hk1 il0",
+    "v": "eb six pc1 six0 cf xz mask cf2 e1 cf3 ou hq0 qe3 vam qu qe1 vas qp hq1 pa qe0 oxr pb oz om oka si qe2",
+    "a": "val val2 rst pad qp xo hk0 hk1 xf il0",
     "t": "hk0 hk1",
 }
 ROUND = {
     "s": "v ol oc0 oc1 os",
     "g": "inv sl s1",
-    "v": "km0 km1 kl0 qe1 kl1 d0a qy oza low d0b s00 e03 e01 e04 s01 e02 qe3 s02 p0a ozb p0b o0a j0 o0b "
-         "s10 sf1 i0 s11 sf2 sf0 s12 p1a vam5 p1b o1a j1 o1b d2a vam6 i1 d2b "
-         "s20 e21 e22 e23 e24 s21 vas6 la lb s22 p2a em2 vas5 p2b o2a j2 o2b "
-         "s30 oz5 six0 i2 s31 ox5 sh em3 s32 om j3 i3 i4 "
-         "a2 a0 a3 a1 g00 g01 f1 f0 q0 g11 g10 q1 t00 t00b t01 t02 t03 t10 t11 t12 t13 qt0 okb qt1 "
-         "turn zf0 zf1 za0 za2 za1 za3 ot zg00 zg01 zg10 zq0 zg11 zq1 zt00 zt00b zt01 zt02 zt03 zt10 zqt0 zt11 zt12 zt13 zqt1",
-    "a": "y0s z0b c0 z0a inv1 n0a n0b m0 z1 y1 n1a n1b l3 c2 y2 n2a n2b r2 m2 u00 u01 y3 u02 m3 u03 u10 u11 u12 u13 "
-         "g02 g03 f2 f3 g13 g12 r00 r00b r01 r02 r03 r10 r11 r12 r13 k0 ilb k1 "
+    "v": "km0 km1 kl0 A00 kl1 d0a e01a e02a e03a d0b s00 e04 e01b e02b e03b s01 D0a S01 D0b s02 S02 H00 A01 A02 H01 "
+         "s10 p0 H02 s11 S11 T11 o0 s12 S12 T12 p1a i0 p1b o1a j1 o1b d2a i1 d2b "
+         "s20 e24 e21 e23 e22 s21 la S21 lb D2a s22 S22 D2b H20 A20 A21 A22 H21 "
+         "s30 low i2 H22 s31 A30 A31 A33 s32 S32 T32 A32 sf2 i3 i4 sf0 "
+         "a2 a0 a3 a1 g00 g01 f0 f1 q0 sf1 g11 g10 sh qy q1 t00 t00b t01 t02 t03 t10 t11 t12 t13 qt0 qt1 okb "
+         "turn zf0 zf1 za2 za0 za1 za3 zg00 zg01 ot zq0 zg11 zg10 zq1 zt00 zt00b zt01 zt02 zt03 zt10 zqt0 zt11 zt12 zt13 zqt1",
+    "a": "c0a c0b x001 x000 z0 x011 x010 x012 x020 x021 n0 m0 x102 x101 n1a n1b c2a l3 c2b em2 x200 x201 x210 x211 x212 x220 m2 x221 "
+         "u00 r2 u01 x302 u02 x301 x312 x311 u03 u10 u11 u12 u13 "
+         "g02 g03 f3 f2 g13 g12 r00 r00b r01 ilb r02 r03 r10 r11 r12 r13 inv1 k0 k1 "
          "zf2 zf3 zg02 zg03 zg13 zg12 o1 zr00 zr00b zr01 zr02 zr03 zr10 zr11 zr12 zr13 yp0 y0d yp1 y1d",
     "t": "u00 u01 u02 u03 u10 u11 u12 u13 r00 r01 r02 r03 r10 r11 r12 r13 k0 k1",
 }
@@ -59,16 +61,16 @@ for _n, _w, _d in [
     ("eb", 1032, "bfloat16"), ("qec", 512, CODES), ("qes", 512, "uint8"),
     ("ys", 256, "float32"), ("o1", 256, "float32"),
     ("pc", 4, "int32"), ("cf", 8, "float32"), ("i16", 256, "float32"), ("i128", 128, "float32"), ("x5", 16, "float32"),
-    ("mask", 256, "float32"), ("rst", 256, "float32"), ("six", 102, "float32"), ("inv", 320, "float32"),
-    ("val", 336, "float32"), ("vam", 336, "float32"), ("vas", 336, "float32"), ("tmp", 8, "float32"),
-    ("si", 51, "int32"), ("sf", 102, "float32"), ("sh", 102, "float32"),
-    ("oz0", 4, "uint16"), ("oza", 4, "uint16"), ("oz1", 4, "uint16"), ("ox", 4, "uint16"), ("ob", 10, "uint16"), ("ou", 8, "uint16"),
-    ("ox3", 4, "uint16"), ("oz3", 4, "uint16"),
+    ("mask", 256, "float32"), ("rst", 256, "float32"), ("six", 96, "float32"), ("inv", 320, "float32"),
+    ("val", 208, "float32"), ("vam", 208, "float32"), ("vas", 208, "float32"),
+    ("si", 48, "int32"), ("sf", 96, "float32"), ("sh", 96, "float32"),
+    ("oz0", 4, "uint16"), ("oz1", 4, "uint16"), ("ox", 8, "uint16"), ("ou", 8, "uint16"),
     ("om", 6, "uint16"), ("oka", 16, "uint16"), ("okb", 16, "uint16"), ("ov", 64, "uint16"), ("ot", 16, "uint16"),
     ("pa", 32, "float32"), ("pb", 32, "float32"),
-    ("sk", 256, "float32"), ("km", 256, "float32"), ("kl", 320, "float32"), ("il", 464, "float32"), ("xx", 168, "float32"),
-    ("zz", 288, "float32"), ("nn", 288, "float32"), ("pp", 288, "float32"), ("oo", 320, "float32"),
-    ("zi", 256, "float32"), ("ni", 256, "float32"), ("pj", 256, "float32"), ("em", 16, "float32"), ("l3", 2, "float32"),
+    ("sk", 256, "float32"), ("km", 256, "float32"), ("kl", 320, "float32"), ("il", 464, "float32"),
+    ("hb", 224, "float32"), ("he", 224, "float32"), ("hd", 224, "float32"), ("ho", 224, "float32"), ("hk", 128, "float32"), ("hy", 64, "float32"),
+    ("zz", 64, "float32"), ("nn", 256, "float32"), ("pp", 128, "float32"), ("oo", 160, "float32"),
+    ("pj", 64, "float32"), ("em", 16, "float32"), ("l3", 2, "float32"),
 ]:
     _buf(_n, _w, _d)
 BANK = ["ps%d" % _b for _b in range(8)]
@@ -133,7 +135,8 @@ def rank_program(g, core, T, topo):
             for (name, lo, hi, st) in rs:
                 bank = SCRATCH[name][0] == "psum"
                 for (l2, h2, s2, w2, i) in log.get(name, []):
-                    if l2 < hi and lo < h2 and (wr or w2 or bank and ops[i][0] != q) and not (st == s2 and (lo - l2) % st):
+                    if (l2 < hi and lo < h2 and (wr or w2 or bank and ops[i][0] != q)
+                            and (lo - l2) % max(1, math.gcd(st * (hi - lo > 1), s2 * (h2 - l2 > 1))) == 0):
                         deps.add(i)
         for rs, wr in ((reads, False), (writes, True)):
             for (name, lo, hi, st) in rs:
@@ -167,14 +170,14 @@ def rank_program(g, core, T, topo):
     def act(nm, out, a, func, bias, scale):
         run(nm, "a", [out], [a, bias], lambda: S.activation(out[0], a[0], func, bias=raw(bias), scale=scale))
 
-    def scan(nm, out, d0, d1, op0, op1):
+    def scan(nm, out, d0, d1, op0=ALU.mult, op1=ALU.add):
         run(nm, "v", [out], [d0, d1], lambda: V.tensor_tensor_scan(out[0], d0[0], d1[0], 0.0, op0, op1))
 
     def fill(nm, out, c):
         run(nm, "v", [out], [], lambda: V.memset(out[0], c))
 
     def const(nm, out, c):
-        act(nm, out, A("i16", 0, out[2]), ACT.Identity, c, 0.0)
+        act(nm, out, A("i16" if out[2] > 16 else "x5", 0, out[2]), ACT.Identity, c, 0.0)
 
     def quant(nm, c, s, lo, a):
         oc, osc = A(c, lo, lo + a[2] // 4), A(s, lo, lo + a[2] // 4)
@@ -215,7 +218,7 @@ def rank_program(g, core, T, topo):
         if r:
             lo = 0
         if h or not r:
-            return send(nm + "s%d" % h, r, h, [(u8(A("ldc%d" % r, lo, hi)), u8(A("qtc%d" % r, lo, hi))), (A("lds%d" % r, lo, hi), A("qts%d" % r, lo, hi))])
+            send(nm + "s%d" % h, r, h, [(u8(A("ldc%d" % r, lo, hi)), u8(A("qtc%d" % r, lo, hi))), (A("lds%d" % r, lo, hi), A("qts%d" % r, lo, hi))])
 
     def col(j):
         return A("cf", j, j + 1)
@@ -228,61 +231,54 @@ def rank_program(g, core, T, topo):
     dma("ws", "s", "ws", A("wqs"), T.ws[:])
 
     iota("pc", A("pc", 0, 1), [[0, 1]], 0, 1, False)
-    iota("x5", A("x5"), [[5, 4], [1, 4]], 0, 0)
+    iota("x5", A("x5"), [[1, 16]], 0, 0)
     iota("i16", A("i16"), [[0, 16], [1, 16]], 0, 0)
     iota("i128", A("i128"), [[1, 128]], 0, 0)
-    fill("xz", A("xx"), 0.0)
-    fill("xf", A("xx", 4, 160, 5), 1.0)
-    for c in range(1, 4):
-        fill("xo", A("xx", c, 160, 40), 1.0)
+    fill("xz", A("hb"), 0.0)
+    fill("xz", A("hk"), 0.0)
+    for lo, step in ((12, 28), (19, 28), (25, 28), (26, 28), (30, 28), (31, 112)):
+        const("xo", A("hb", lo, 224, step), 1.0)
+    for lo, hi, step in ((0, 64, 4), (1, 64, 4), (67, 128, 4), (14, 47, 16), (78, 111, 16)):
+        const("xf", A("hk", lo, hi, step), 1.0)
     fill("eb", A("eb"), 0.0)
     fill("six", A("six"), 1.0)
-    fill("six0", A("six", 0, 102, 6), 0.0)
+    fill("six0", A("six", 0, 96, 6), 0.0)
     ts("pc1", A("pc", 1, 2), A("pc", 0, 1), 15, ALU.bitwise_and)
     ts("pc1", A("pc", 2, 3), A("pc", 0, 1), 31, ALU.bitwise_and)
     cp("cf", "v", A("cf", 0, 2), A("pc", 0, 2))
     cp("cf", "v", A("om", 4, 5), A("pc", 2, 3))
-    cp("cf", "v", A("si", 16, 17), A("pc", 1, 2))
     ts("mask", A("mask"), A("i16"), col(1), ALU.is_equal)
     ts("ou", A("ou"), A("i16", 0, 8), 16.0, ALU.mult)
     act("rst", A("rst"), A("i16"), ACT.Sign, 0.0, 1.0)
-    for s, c in enumerate((1.0, 1.0, 6.0, 5.0)):
-        act("val", A("val", s, 64, 4), A("x5"), ACT.Identity, c, 1.0 if s else 0.0)
-    act("val", A("val", 64, 72), A("x5", 0, 8), ACT.Identity, 0.0, 0.0)
-    for s, c in enumerate((1.0, 2.0, 7.0, 6.0, 11.0, 10.0)):
-        act("val", N("val", 72 + s, 12, 6), A("x5", 0, 12), ACT.Identity, c, 1.0 if s else 0.0)
+    const("val", A("val", 0, 64, 4), 12.0)
+    for s, rows in ((1, (12, 10, 9, 37)), (2, (10, 9, 37, 0)), (3, (3, 8, 36, 0))):
+        for i, c in enumerate(rows):
+            act("val", N("val", 16 * i + s, 4, 4), A("x5", 0, 4), ACT.Identity, float(c), 0.0 if c in (0, 12) else 7.0)
     for s, c in enumerate((0.0, 1.0, 4.0, 0.0)):
-        act("val", A("val", 144 + s, 208, 4), A("i16", 0, 16), ACT.Identity, c, 1.0)
-    act("val3", A("val", 208, 272), A("val", 0, 64), ACT.Identity, 0.0, 1.0)
-    act("val3", A("val", 272, 336), A("val", 144, 208), ACT.Identity, 3.0, 4.0)
-    act("val4", N("val", 222, 3, 16), N("x5", 3, 3, 4), ACT.Identity, 5.0, 1.0)
-    for base, c in ((208, 32.0), (272, 80.0)):
-        act("val4", N("val", base + 15, 3, 16), N("i16", 3, 3, 4), ACT.Identity, c, 1.0)
-        act("val4", N("val", base + 50, 4, 4), A("i16", 12, 16), ACT.Identity, c, 1.0)
-    for s, c in ((1, 19.0), (2, 3.0)):
-        act("val4", N("val", 284 + s, 3, 16), N("i16", 3, 3, 4), ACT.Identity, c, 4.0)
-    for nm, lo, hi in (("", 0, 208), ("5", 208, 272), ("6", 272, 336)):
-        tt("vam" + nm, A("vam", lo, hi), A("val", lo, hi), A("mask", 0, hi - lo), ALU.mult)
-        scan("vas" + nm, A("vas", lo, hi), A("rst", 0, hi - lo), A("vam", lo, hi), ALU.mult, ALU.add)
-    cp("ox5", "v", A("ox3"), N("vas", 223, 4, 16))
-    cp("oz5", "v", A("oz3"), N("vas", 287, 4, 16))
-    place = N("vas", 159, 4, 16)
-    ts("oz", A("tmp", 0, 4), place, 8.0, ALU.is_ge, 20.0, ALU.mult)
+        act("val", A("val", 64 + s, 128, 4), A("x5"), ACT.Identity, c, 1.0)
+    act("val", A("val", 128, 144), A("x5"), ACT.Identity, 3.0, 4.0)
+    for a, b in SWAPS + [s[::-1] for s in SWAPS]:
+        const("val2", A("val", 128 + a, 129 + a), 4.0 * b + 3.0)
+    const("val", A("val", 144, 208, 4), 0.0)
+    for s in (1, 2, 3):
+        cp("val2", "a", A("val", 144 + s, 208, 4), A("val", 4 - s, 64, 4))
+    tt("vam", A("vam"), A("val"), A("mask", 0, 208), ALU.mult)
+    scan("vas", A("vas"), A("rst", 0, 208), A("vam"))
+    cp("om", "v", A("om", 0, 1), A("vas", 143, 144))
+    cp("oxr", "v", A("ox", 4, 8), N("vas", 159, 4, 16))
+    place = N("vas", 79, 4, 16)
     ts("oz", A("oz0"), place, 16.0, ALU.mult, 15.0, ALU.add)
     ts("oz", A("oz1"), place, 4.0, ALU.mult, 3.0, ALU.add)
-    cp("ob", "v", A("ox"), N("vas", 15, 4, 16))
-    cp("ob", "v", A("ob", 0, 2), N("vas", 15, 2, 16))
-    cp("ob", "v", A("ob", 2, 7), N("vas", 79, 5, 16))
-    cp("ob", "v", A("ob", 7, 9), N("vas", 47, 2, 16))
-    tt("oza", A("tmp", 4, 8), A("tmp", 0, 4), place, ALU.add)
-    ts("ozb", A("oza"), A("tmp", 4, 8), 4.0, ALU.mult, 3.0, ALU.add)
+    cp("oz", "v", A("ox", 0, 4), N("vas", 15, 4, 16))
     ts("cf2", A("cf", 2, 6), A("i16", 0, 4), 16.0, ALU.mult, col(1), ALU.add)
     ts("cf3", A("cf", 2, 6), A("cf", 2, 6), 256.0, ALU.add)
     const("pad", A("kl", 256, 320), LOW)
-    const("pad", A("zz", 32, 112), 0.0)
+    const("pad", col(6), -255.5)
+    act("pad", col(7), col(1), ACT.Identity, 280.0, 1.0)
+    const("pad", A("he"), 0.0)
     const("pad", A("il", 0, 80), col(5))
-    const("pad", A("oo", 144, 240), LOW)
-    const("pad", A("zz", 208, 288), 0.0)
+    const("pad", A("oo", 64, 80), LOW)
+    const("pad", A("oo", 144, 160), LOW)
     for k in range(1, 4):
         const("pad", A("il", 80 * k + 64, 80 * k + 80), col(5))
     const("pad", A("il", 335, 336), col(2))
@@ -296,8 +292,7 @@ def rank_program(g, core, T, topo):
     cp("qp", "a", A("qps"), G(A("qus"), A("ou")))
     for h in range(2):
         quant("hq%d" % h, "qtc0", "qts0", 128 * h, A("tw0", 512 * h, 512 * h + 512))
-        came = keys_and_send("h", 0, h)
-    dma("v", "s", "v", A("vb"), T.v[:], [came])
+        keys_and_send("h", 0, h)
     for h in range(2):
         cp("pa", "v", A("pa", 16 * h, 16 * h + 16), A("pi"))
     run("pb", "v", [A("pb")], [A("pa")], lambda: V.transpose(T.pb[:], T.pa[:]))
@@ -305,33 +300,29 @@ def rank_program(g, core, T, topo):
     cp("oka", "v", A("oka"), turned)
     cp("il0", "a", A("il", 3, 64, 4), turned)
     cp("si", "v", A("si", 0, 16), turned)
-    low = A("si", 17, 34)
-    ts("low", low, A("si", 0, 17), 15, ALU.bitwise_and)
-    ts("low", A("si", 34, 51), A("si", 0, 17), 4, ALU.logical_shift_right)
-    ts("sf0", A("sf", 0, 102, 6), low, 16.0, ALU.mult)
-    cp("sf0", "v", A("sf", 1, 102, 6), A("si", 34, 51))
+    low = A("si", 16, 32)
+    ts("low", low, A("si", 0, 16), 15, ALU.bitwise_and)
+    ts("low", A("si", 32, 48), A("si", 0, 16), 4, ALU.logical_shift_right)
+    ts("sf0", A("sf", 0, 96, 6), low, 16.0, ALU.mult)
+    cp("sf0", "v", A("sf", 1, 96, 6), A("si", 32, 48))
     for j, (a, b) in enumerate(SWAPS + [s[::-1] for s in SWAPS]):
-        ts("sf%d" % (1 + j // 2), A("sf", 2 + j, 102, 6), low, float(a), ALU.is_equal, 16.0 * (b - a), ALU.mult)
-    scan("sh", A("sh"), A("six"), A("sf"), ALU.mult, ALU.add)
-    ts("om", A("om", 0, 1), A("sh", 101, 102), 0.25, ALU.mult, 3.0, ALU.add)
+        ts("sf%d" % (1 + j // 2), A("sf", 2 + j, 96, 6), low, float(a), ALU.is_equal, 16.0 * (b - a), ALU.mult)
+    scan("sh", A("sh"), A("six"), A("sf"))
     cp("okb", "v", A("okb"), N("sh", 5, 16, 6))
     now[0] = 1
-    quant("qy", "qyc", "qys", 0, A("vb"))
     iota("inv", A("inv", 0, 256), [[1, 16], [16, 16]], 0, 0)
     iota("inv", A("inv", 256, 320), [[1, 64]], 256, 0)
     for a, b in SWAPS + [s[::-1] for s in SWAPS]:
         act("inv1", A("inv", 16 * a, 16 * a + 16), A("inv", 16 * a, 16 * a + 16), ACT.Identity, float(b - a), 1.0)
 
-    DN = [("zz", 40), ("oo", 45), ("zz", 216), ("oo", 253)]
-    PARTS = [[(0, 64, "ob", 0, 0), (64, 144, "ob", 4, 64)],
-             [(144, 176, "ox", 0, 160), (176, 208, "ox", 2, 192)],
-             [(208, 240, "ob", 2, 240), (240, 288, "ob", 4, 272)]]
+    def pair(buf, k, lo, count, slot):
+        return N(buf, 56 * k + 7 * (lo + 1) + slot, count, 7)
 
-    def dn(k, lo, count, slot=0):
-        return N(DN[k][0], DN[k][1] + 6 * lo + slot, count, 6)
+    def dn(k, lo, count):
+        return pair("ho", k - 1, lo, count, 5) if k % 2 else pair("he", k, lo, count, 0)
 
     def keys(k, lo, count):
-        return N("kl", 16 * lo + 15, count, 16) if k == 0 else N("oo", 163 + 4 * lo, count, 4)
+        return N("oo", 83 + 4 * lo, count, 4) if k else N("kl", 16 * lo + 15, count, 16)
 
     def ids(k, lo=0, count=16):
         return N("il", 80 * k + 4 * lo + 3, count, 4)
@@ -343,56 +334,81 @@ def rank_program(g, core, T, topo):
         for h in range(2):
             half = (128 * h, 128 * h + 128)
             tt("km%d" % h, A("km", *half), G(A("sk"), A("oka" if r == 0 else "okb", 8 * h, 8 * h + 8)), A("mask", *half), ALU.mult)
-            scan("kl%d" % h, A("kl", *half), A("rst", *half), A("km", *half), ALU.mult, ALU.add)
+            scan("kl%d" % h, A("kl", *half), A("rst", *half), A("km", *half))
         for h in range(2):
             for b in range(4):
                 mm("u%d%d" % (h, b), BANK[4 * (1 - h) + b], "qec", "qes", 128 * b, "ldc%d" % r, "lds%d" % r, 128 * h, 128)
                 cp("u%d%d" % (h, b), "a", A("dd%d" % r, 256 * b + 128 * h, 256 * b + 128 * h + 128), A(BANK[4 * (1 - h) + b], 0, 128))
         for k in range(4):
-            x, z = 40 * k, 64 * k
             if k % 2 == 0:
+                b = 56 * k
                 tt("d%da" % k, dn(k, 0, 3), keys(k, 4, 3), keys(k, 1, 3), ALU.is_gt)
                 tt("d%db" % k, dn(k, 4, 7), keys(k, 8, 7), keys(k, 5, 7), ALU.is_gt)
-                for s, (a, b) in enumerate(((4, 2), (4, 5), (5, 1), (8, 1))):
-                    tt("e%d%d" % (k, s + 1), dn(k, 0, 11, s + 1), keys(k, a, 11), keys(k, b, 11), ALU.is_gt)
-                cp("c%d" % k, "a", dn(k, 0, 11, 5), dn(k, 0, 11))
+                for s, (lo, hi) in enumerate(((4, 2), (4, 5), (5, 1), (8, 1))):
+                    for nm, at, w in (("a", 0, 3), ("b", 4, 7)) if s < 3 and k == 0 else (("", 0, 11),):
+                        tt("e%d%d%s" % (k, s + 1, nm), pair("he", k, at, w, 4 - s), keys(k, lo + at, w), keys(k, hi + at, w), ALU.is_gt)
+                cp("c%da" % k, "a", pair("he", k, 0, 3, 5), dn(k, 0, 3))
+                cp("c%db" % k, "a", pair("he", k, 4, 7, 5), dn(k, 4, 7))
+                for h, (lo, hi) in enumerate(((b + 7, b + 28), (b + 35, b + 84))):
+                    tt("D%d%s" % (k, "ab"[h]), A("hd", lo, hi), A("he", lo, hi), A("he", lo + 1, hi + 1), ALU.subtract)
+                for i, (one, two, more) in enumerate((((0, 3), None, ((0, 4, 1), (4, 5, 1))),
+                                                      ((0, 2), (1, 1), ((4, 3, 0), (4, 4, 1), (8, 5, 1))),
+                                                      ((4, 2), (5, 1), ((8, 3, 0), (8, 4, 1))))):
+                    for nm, at in (("s", one), ("S", two)):
+                        if at:
+                            scan("%s%d%d" % (nm, k, i), pair("hb", k, at[0], 3, at[1]), dn(k, 4 * i, 3), pair("hb", k, 0, 3, (5, 3, 2)[i]), ALU.max, ALU.min)
+                    for j, (lo, s, c) in enumerate(more):
+                        cp("x%d%d%d" % (k, i, j), "a", pair("hb", k, lo, 3 - c, s), pair("hb", k, one[0] + c, 3 - c, one[1]))
+                for i in range(3):
+                    lo = b + 28 * i + 7
+                    scan("H%d%d" % (k, i), A("ho", lo, lo + 21), A("hb", lo, lo + 21), A("hd", lo, lo + 21))
+            else:
+                b, slot = (0, (1, 2, 3)) if k == 1 else (64, (3, 2, 1))
+                for i in range(3):
+                    first = N("hk", b + 16 * i + 16 + slot[0], 3, 4)
+                    for j, at in enumerate((first, N("hk", b + 16 * i + slot[1], 3, 4), N("hk", b + 16 * i + 4 + slot[2], 3, 4))):
+                        if j and i < (k + 1) // 2:
+                            cp("x%d%d%d" % (k, i, j), "a", at, first)
+                        else:
+                            scan("%s%d%d" % ("sST"[j], k, i), at, dn(k, 4 * i, 3), N("hk", b + 16 * i + slot[0], 3, 4), ALU.max, ALU.min)
             if k == 0:
-                cp("z0a", "a", A("zz", 0, 32), G(A("kl"), A("oz0", 0, 2)))
-                cp("z0b", "a", A("zz", 112, 144), G(A("kl"), A("oz0", 2, 4)))
-            if k == 1:
-                cp("z1", "a", A("zz", 144, 208), G(A("oo", 0, 160), A("oza")))
-            if k == 3:
-                cp("y3", "a", A("zi", z, z + 64), G(A("il", 240, 336), A("oz3")))
-                ts("em3", A("xx", x + 32, x + 48), ids(3), 256.0, ALU.is_ge)
-            elif k or r < 2:
-                cp("y%d" % k if k else "y0s", "a", A("zi", z, z + 64), G(A("il", 80 * k, 80 * k + 80), A("oz1")))
+                path = G(A("hb", 0, 64), A("ox", 0, 4))
+                cp("z0", "a", A("zz"), G(A("kl"), A("oz0")))
+                tt("p0", A("pp", 0, 64), path, A("zz"), ALU.mult)
+                act("n0", A("nn", 0, 64), path, ACT.Identity, 1.0, -1.0)
+                scan("o0", A("oo", 0, 64), A("nn", 0, 64), A("pp", 0, 64))
+            for h in range(2 if k == 1 else 0):
+                lo, x = 64 + 32 * h, A("hk", 32 * h, 32 * h + 32)
+                tt("p1" + "ab"[h], A("pp", lo, lo + 32), G(A("oo", 0, 80), A("oz1", 2 * h, 2 * h + 2)), x, ALU.mult)
+                act("n1" + "ab"[h], A("nn", lo, lo + 32), x, ACT.Identity, 1.0, -1.0)
+                scan("o1" + "ab"[h], A("oo", lo + 16, lo + 48), A("nn", lo, lo + 32), A("pp", lo, lo + 32))
             if k == 2:
                 cp("la", "v", A("lso%d" % r, 0, 3), A("il", 3, 164, 80))
                 act("l3", A("l3", 0, 1), ids(2, 1, 1), ACT.Identity, ids(2, 4, 1), -1.0)
                 ts("lb", A("lso%d" % r, 3, 4), dn(k, 0, 1), A("l3", 0, 1), ALU.mult, ids(2, 1, 1), ALU.add)
-                send("sl", r, 2, [(A("lsi%d" % r), A("lso%d" % r))])
-                ts("em2", A("em", 0, 15), ids(2, 0, 15), 256.0, ALU.is_ge)
-                act("r2", A("il", 320, 335), A("em", 0, 15), ACT.Identity, col(4), -16.0)
-            for i in range(3):
-                scan("s%d%d" % (k, i), A("xx", x + 5 * i + 6, x + 5 * i + 9), dn(k, 4 * i, 3), A("xx", x + 5 * i + 1, x + 5 * i + 4), ALU.max, ALU.min)
+                came = send("sl", r, 2, [(A("lsi%d" % r), A("lso%d" % r))])
+                if r == 0:
+                    dma("v", "s", "v", A("vb"), T.v[:], [came])
+                if r == 1:
+                    quant("qy", "qyc", "qys", 0, A("vb"))
+                act("em2", A("em", 0, 15), ids(2, 0, 15), ACT.Sign, col(6), 1.0)
+                act("r2", A("il", 320, 335), A("em", 0, 15), ACT.Identity, col(7), -8.0)
+            if k == 1:
+                tt("j1", A("pj"), G(A("il", 80, 160), A("oz1")), A("hk", 0, 64), ALU.mult)
+                scan("i1", A("il", 160, 224), A("nn", 64, 128), A("pj"))
+                continue
+            for s, (lo, hi) in enumerate(((0, 4), (4, 1), (1, 0)) if k or r < 2 else ()):
+                tt("A%d%d" % (k, s), N("il", 80 * k + s, 16, 4) if k < 3 else A("hy", s, 64, 4), ids(k, lo), ids(k, hi), ALU.subtract)
             if k < 3:
-                for h, (lo, hi, lst, c, o) in enumerate(PARTS[k]):
-                    nm = "%d%s" % (k, "ab"[h])
-                    path = G(A("xx", x, x + 16 * h + 16), A(lst, c, c + (hi - lo) // 16))
-                    act("n" + nm, A("nn", lo, hi), path, ACT.Identity, 1.0, -1.0)
-                    tt("p" + nm, A("pp", lo, hi), path, A("zz", lo, hi), ALU.mult)
-                    scan("o" + nm, A("oo", o, o + hi - lo), A("nn", lo, hi), A("pp", lo, hi), ALU.mult, ALU.add)
-            path = G(A("xx", x, x + 48), A("ox3")) if k == 3 else G(A("xx", x, x + 32), A("ox"))
-            nx = A("nn", 144, 208)
-            if k != 1:
-                nx = A("ni", z, z + 64)
-                act("m%d" % k, nx, path, ACT.Identity, 1.0, -1.0)
-            tt("j%d" % k, A("pj", z, z + 64), path, A("zi", z, z + 64), ALU.mult)
-            o = 336 if k == 3 else 80 * k + 80
-            scan("i%d" % k, A("il", o, o + 64), nx, A("pj", z, z + 64), ALU.mult, ALU.add)
+                x = A("nn", 128 + 32 * k, 192 + 32 * k)
+                cp("m%d" % k, "a", x, G(A("hb", b, b + 64), A("ox", 4, 8)))
+                scan("i%d" % k, A("il", 80 * k + 80, 80 * k + 144), x, A("il", 80 * k, 80 * k + 64))
+            else:
+                tt("A33", A("hy", 3, 64, 4), ids(3), A("il", 320, 336), ALU.min)
+                scan("i3", A("il", 336, 400), A("hk", 64, 128), A("hy"))
         where, e = G(A("il", 336, 400), A("om", 0, 1)), ""
         if last:
-            scan("i4", A("il", 400, 464), nx, A("pj", z, z + 64), ALU.mult, ALU.add)
+            scan("i4", A("il", 400, 464), A("hk", 64, 128), A("hy"))
             twice = N("il", 339, 32, 4)
             run("turn", "v", [A("pb")], [twice], lambda: V.transpose(T.pb[:], twice[0]))
             where, e = turned, "z"

@@ -8,25 +8,26 @@ STEP = [3, 6, 4]
 LOW = -9.0e29
 SWAPS = [(3, 8), (7, 9)]
 PICK_F, PICK_V = "vvaa", ["vvaa", "vvaa"]
+COPIES = ["0b", "0c", "0d", "0e", "0f", "1e", "1f", "1g", "1h"]
 HEAD = {
     "s": "x0 u x1 p ws wc",
-    "g": "x5 pc i16 i128 hs0 hs1",
-    "v": "eb six pc1 six0 cf xz mask cf2 e1 cf3 ou hq0 qe3 vam qu qe1 vas qp hq1 pa qe0 oxr pb oz om oka si qe2",
-    "a": "val val2 rst pad qp xo hk0 hk1 xf il0",
+    "g": "pc x5 i16 i128 hs0 hs1",
+    "v": "eb pc1 xz cf six cf1 mask cf2 e1 ou six0 hq0 vam qu cf3 vas qp hq1 qe3 pa qe0 pb oz qe1 oka qe2 si om",
+    "a": "val rst xf val2 xo qp pad hk0 hk1 il0",
     "t": "hk0 hk1",
 }
 ROUND = {
     "s": "v ol oc0 oc1 os",
-    "g": "inv sl s1",
-    "v": "km0 km1 kl0 A00 kl1 d0a e01a e02a e03a d0b s00 e04 e01b e02b e03b s01 D0a S01 D0b s02 S02 H00 A01 A02 H01 "
-         "s10 p0 H02 s11 S11 T11 o0 s12 S12 T12 p1a i0 p1b o1a j1 o1b d2a i1 d2b "
-         "s20 e24 e21 e23 e22 s21 la S21 lb D2a s22 S22 D2b H20 A20 A21 A22 H21 "
-         "s30 low i2 H22 s31 A30 A31 A33 s32 S32 T32 A32 sf2 i3 i4 sf0 "
-         "a2 a0 a3 a1 g00 g01 f0 f1 q0 sf1 g11 g10 sh qy q1 t00 t00b t01 t02 t03 t10 t11 t12 t13 qt0 qt1 okb "
-         "turn zf0 zf1 za2 za0 za1 za3 zg00 zg01 ot zq0 zg11 zg10 zq1 zt00 zt00b zt01 zt02 zt03 zt10 zqt0 zt11 zt12 zt13 zqt1",
-    "a": "c0a c0b x001 x000 z0 x011 x010 x012 x020 x021 n0 m0 x102 x101 n1a n1b c2a l3 c2b em2 x200 x201 x210 x211 x212 x220 m2 x221 "
-         "u00 r2 u01 x302 u02 x301 x312 x311 u03 u10 u11 u12 u13 "
-         "g02 g03 f3 f2 g13 g12 r00 r00b r01 ilb r02 r03 r10 r11 r12 r13 inv1 k0 k1 "
+    "g": "inv sl s0 s2 s1",
+    "v": "km0 km1 kl0 A00 A01 kl1 d0a e01a e02a e03a c0a d0b s00a e04 c0b e01b e02b e03b A02 s01a D0a s01b s01c s01d D0b "
+         "s02a s02b H00 s02d p0a s02e s02c H01 s10 p0b s02g s02f o0a H02 s11 S11 T11 o0b i0 T12 S12 s12 p1a j1a p1b o1a j1b i1a o1b "
+         "d2a e21a c2a e22a i1b la e23a e24 d2b s20a e22b e21b e23b lb c2b A20 D2a s21a s21b A22 s21c s21d D2b "
+         "s22a s22b H20 s22g s22e A21 s22f s22d s22c H21 s30 T30 i2 H22 S30 s31 low S31 T31 A30 A31 A32 A33 T32 s32 S32 i3 i4 sf0 "
+         "a2 a0 a3 sf2 a1 g00 g01 f1 f0 q0 sf1 g11 g10 qy sh q1 t00 t00b t01 t02 t03 t10 t11 t12 t13 qt0 okb qt1 "
+         "turn zf0 zf1 za2 za0 za1 za3 ot zg00 zg01 zq0 zg11 zg10 zq1 zt00 zt00b zt01 zt02 zt03 zt10 zqt0 zt11 zt12 zt13 zqt1",
+    "a": "z0a x00e x00b x00f x00c z0b x01h x01e x01f n0a x01g x00d n0b x102 x101 n1a n1b l3 "
+         "x20b x20c x20f em2 x20d x21g x20e r2 x21h x21e x21f u00 u01 u02 u03 u10 u11 u12 u13 "
+         "g02 g03 f3 f2 g13 g12 r00 r00b r01 r02 r03 inv1 r10 r11 r12 r13 k0 k1 ilb "
          "zf2 zf3 zg02 zg03 zg13 zg12 o1 zr00 zr00b zr01 zr02 zr03 zr10 zr11 zr12 zr13 yp0 y0d yp1 y1d",
     "t": "u00 u01 u02 u03 u10 u11 u12 u13 r00 r01 r02 r03 r10 r11 r12 r13 k0 k1",
 }
@@ -62,14 +63,14 @@ for _n, _w, _d in [
     ("ys", 256, "float32"), ("o1", 256, "float32"),
     ("pc", 4, "int32"), ("cf", 8, "float32"), ("i16", 256, "float32"), ("i128", 128, "float32"), ("x5", 16, "float32"),
     ("mask", 256, "float32"), ("rst", 256, "float32"), ("six", 96, "float32"), ("inv", 320, "float32"),
-    ("val", 208, "float32"), ("vam", 208, "float32"), ("vas", 208, "float32"),
+    ("val", 144, "float32"), ("vam", 144, "float32"), ("vas", 144, "float32"),
     ("si", 48, "int32"), ("sf", 96, "float32"), ("sh", 96, "float32"),
-    ("oz0", 4, "uint16"), ("oz1", 4, "uint16"), ("ox", 8, "uint16"), ("ou", 8, "uint16"),
+    ("oz0", 4, "uint16"), ("oz1", 4, "uint16"), ("ox", 4, "uint16"), ("ou", 8, "uint16"),
     ("om", 6, "uint16"), ("oka", 16, "uint16"), ("okb", 16, "uint16"), ("ov", 64, "uint16"), ("ot", 16, "uint16"),
     ("pa", 32, "float32"), ("pb", 32, "float32"),
     ("sk", 256, "float32"), ("km", 256, "float32"), ("kl", 320, "float32"), ("il", 464, "float32"),
-    ("hb", 224, "float32"), ("he", 224, "float32"), ("hd", 224, "float32"), ("ho", 224, "float32"), ("hk", 128, "float32"), ("hy", 64, "float32"),
-    ("zz", 64, "float32"), ("nn", 256, "float32"), ("pp", 128, "float32"), ("oo", 160, "float32"),
+    ("hb", 224, "float32"), ("he", 224, "float32"), ("hd", 224, "float32"), ("ho", 224, "float32"), ("hk", 256, "float32"), ("hy", 64, "float32"),
+    ("zz", 64, "float32"), ("nn", 128, "float32"), ("pp", 128, "float32"), ("oo", 160, "float32"),
     ("pj", 64, "float32"), ("em", 16, "float32"), ("l3", 2, "float32"),
 ]:
     _buf(_n, _w, _d)
@@ -79,7 +80,7 @@ for _n in BANK:
 
 DMAS = ["x0", "x1", "u", "p", "wc", "ws", "v", "y0", "y1", "ol", "oc0", "oc1", "os0", "os1", "os2", "os3"]
 SEMAPHORES = (["sv", "sa", "st", "sg", "sent"] + ["m_" + n for n in DMAS]
-              + ["in%d_%d" % (r, k) for r in range(R) for k in range(3)])
+              + ["in%d_%d" % (r, k) for r in range(R) for k in range(4)])
 
 
 def order(ops):
@@ -215,10 +216,13 @@ def rank_program(g, core, T, topo):
         lo, hi = 128 * h, 128 * h + 128
         mm(nm + "k%d" % h, BANK[h], "qpc", "qps", 0, "qtc%d" % r, "qts%d" % r, lo, 128)
         cp(nm + "k%d" % h, "a", A("sk", lo, hi), A(BANK[h], 0, 128))
-        if r:
-            lo = 0
-        if h or not r:
-            send(nm + "s%d" % h, r, h, [(u8(A("ldc%d" % r, lo, hi)), u8(A("qtc%d" % r, lo, hi))), (A("lds%d" % r, lo, hi), A("qts%d" % r, lo, hi))])
+        codes = (u8(A("ldc%d" % r, lo, hi)), u8(A("qtc%d" % r, lo, hi)))
+        if not r:
+            send(nm + "s%d" % h, r, h, [codes, (A("lds%d" % r, lo, hi), A("qts%d" % r, lo, hi))])
+            return
+        if h:
+            send("s2", r, 3, [(A("lds%d" % r), A("qts%d" % r))])
+        send("s%d" % h, r, h, [codes])
 
     def col(j):
         return A("cf", j, j + 1)
@@ -238,14 +242,15 @@ def rank_program(g, core, T, topo):
     fill("xz", A("hk"), 0.0)
     for lo, step in ((12, 28), (19, 28), (25, 28), (26, 28), (30, 28), (31, 112)):
         const("xo", A("hb", lo, 224, step), 1.0)
-    for lo, hi, step in ((0, 64, 4), (1, 64, 4), (67, 128, 4), (14, 47, 16), (78, 111, 16)):
+    for lo, hi, step in ((0, 64, 4), (1, 64, 4), (67, 256, 4), (14, 47, 16), (78, 111, 16), (142, 175, 16), (206, 239, 16)):
         const("xf", A("hk", lo, hi, step), 1.0)
     fill("eb", A("eb"), 0.0)
     fill("six", A("six"), 1.0)
     fill("six0", A("six", 0, 96, 6), 0.0)
     ts("pc1", A("pc", 1, 2), A("pc", 0, 1), 15, ALU.bitwise_and)
     ts("pc1", A("pc", 2, 3), A("pc", 0, 1), 31, ALU.bitwise_and)
-    cp("cf", "v", A("cf", 0, 2), A("pc", 0, 2))
+    cp("cf", "v", A("cf", 0, 3), A("pc", 0, 3))
+    ts("cf1", A("om", 2, 3), col(1), 7.0, ALU.is_lt, col(2), ALU.add)
     cp("cf", "v", A("om", 4, 5), A("pc", 2, 3))
     ts("mask", A("mask"), A("i16"), col(1), ALU.is_equal)
     ts("ou", A("ou"), A("i16", 0, 8), 16.0, ALU.mult)
@@ -259,20 +264,17 @@ def rank_program(g, core, T, topo):
     act("val", A("val", 128, 144), A("x5"), ACT.Identity, 3.0, 4.0)
     for a, b in SWAPS + [s[::-1] for s in SWAPS]:
         const("val2", A("val", 128 + a, 129 + a), 4.0 * b + 3.0)
-    const("val", A("val", 144, 208, 4), 0.0)
-    for s in (1, 2, 3):
-        cp("val2", "a", A("val", 144 + s, 208, 4), A("val", 4 - s, 64, 4))
-    tt("vam", A("vam"), A("val"), A("mask", 0, 208), ALU.mult)
-    scan("vas", A("vas"), A("rst", 0, 208), A("vam"))
+    tt("vam", A("vam"), A("val"), A("mask", 0, 144), ALU.mult)
+    scan("vas", A("vas"), A("rst", 0, 144), A("vam"))
     cp("om", "v", A("om", 0, 1), A("vas", 143, 144))
-    cp("oxr", "v", A("ox", 4, 8), N("vas", 159, 4, 16))
     place = N("vas", 79, 4, 16)
     ts("oz", A("oz0"), place, 16.0, ALU.mult, 15.0, ALU.add)
     ts("oz", A("oz1"), place, 4.0, ALU.mult, 3.0, ALU.add)
-    cp("oz", "v", A("ox", 0, 4), N("vas", 15, 4, 16))
+    cp("oz", "v", A("ox"), N("vas", 15, 4, 16))
     ts("cf2", A("cf", 2, 6), A("i16", 0, 4), 16.0, ALU.mult, col(1), ALU.add)
     ts("cf3", A("cf", 2, 6), A("cf", 2, 6), 256.0, ALU.add)
     const("pad", A("kl", 256, 320), LOW)
+    const("pad", A("kl", 0, 16), LOW)
     const("pad", col(6), -255.5)
     act("pad", col(7), col(1), ACT.Identity, 280.0, 1.0)
     const("pad", A("he"), 0.0)
@@ -297,7 +299,7 @@ def rank_program(g, core, T, topo):
         cp("pa", "v", A("pa", 16 * h, 16 * h + 16), A("pi"))
     run("pb", "v", [A("pb")], [A("pa")], lambda: V.transpose(T.pb[:], T.pa[:]))
     turned = G(A("pb"), A("om", 4, 5))
-    cp("oka", "v", A("oka"), turned)
+    cp("oka", "v", A("oka"), G(A("pb"), A("om", 2, 3)))
     cp("il0", "a", A("il", 3, 64, 4), turned)
     cp("si", "v", A("si", 0, 16), turned)
     low = A("si", 16, 32)
@@ -308,7 +310,8 @@ def rank_program(g, core, T, topo):
     for j, (a, b) in enumerate(SWAPS + [s[::-1] for s in SWAPS]):
         ts("sf%d" % (1 + j // 2), A("sf", 2 + j, 96, 6), low, float(a), ALU.is_equal, 16.0 * (b - a), ALU.mult)
     scan("sh", A("sh"), A("six"), A("sf"))
-    cp("okb", "v", A("okb"), N("sh", 5, 16, 6))
+    cp("okb", "v", A("okb", 0, 7), N("sh", 11, 7, 6))
+    cp("okb", "v", A("okb", 8, 16), N("sh", 53, 8, 6))
     now[0] = 1
     iota("inv", A("inv", 0, 256), [[1, 16], [16, 16]], 0, 0)
     iota("inv", A("inv", 256, 320), [[1, 64]], 256, 0)
@@ -332,9 +335,9 @@ def rank_program(g, core, T, topo):
         tw, nxt, vv, ar = "tw%d" % r, "tw%d" % (r + 1), "vv%d" % r, "ar%d" % r
         last = r == R - 1
         for h in range(2):
-            half = (128 * h, 128 * h + 128)
-            tt("km%d" % h, A("km", *half), G(A("sk"), A("oka" if r == 0 else "okb", 8 * h, 8 * h + 8)), A("mask", *half), ALU.mult)
-            scan("kl%d" % h, A("kl", *half), A("rst", *half), A("km", *half))
+            lo, hi = (16, 128) if h == 0 else (128, 256)
+            tt("km%d" % h, A("km", lo, hi), G(A("sk"), A("oka" if r == 0 else "okb", 8 * h, 8 * h + 7 + h)), A("mask", lo, hi), ALU.mult)
+            scan("kl%d" % h, A("kl", lo, hi), A("rst", lo, hi), A("km", lo, hi))
         for h in range(2):
             for b in range(4):
                 mm("u%d%d" % (h, b), BANK[4 * (1 - h) + b], "qec", "qes", 128 * b, "ldc%d" % r, "lds%d" % r, 128 * h, 128)
@@ -345,20 +348,20 @@ def rank_program(g, core, T, topo):
                 tt("d%da" % k, dn(k, 0, 3), keys(k, 4, 3), keys(k, 1, 3), ALU.is_gt)
                 tt("d%db" % k, dn(k, 4, 7), keys(k, 8, 7), keys(k, 5, 7), ALU.is_gt)
                 for s, (lo, hi) in enumerate(((4, 2), (4, 5), (5, 1), (8, 1))):
-                    for nm, at, w in (("a", 0, 3), ("b", 4, 7)) if s < 3 and k == 0 else (("", 0, 11),):
+                    for nm, at, w in (("a", 0, 3), ("b", 4, 7)) if s < 3 else (("", 0, 11),):
                         tt("e%d%d%s" % (k, s + 1, nm), pair("he", k, at, w, 4 - s), keys(k, lo + at, w), keys(k, hi + at, w), ALU.is_gt)
-                cp("c%da" % k, "a", pair("he", k, 0, 3, 5), dn(k, 0, 3))
-                cp("c%db" % k, "a", pair("he", k, 4, 7, 5), dn(k, 4, 7))
+                tt("c%da" % k, pair("he", k, 0, 3, 5), keys(k, 4, 3), keys(k, 1, 3), ALU.is_gt)
+                tt("c%db" % k, pair("he", k, 4, 7, 5), keys(k, 8, 7), keys(k, 5, 7), ALU.is_gt)
                 for h, (lo, hi) in enumerate(((b + 7, b + 28), (b + 35, b + 84))):
                     tt("D%d%s" % (k, "ab"[h]), A("hd", lo, hi), A("he", lo, hi), A("he", lo + 1, hi + 1), ALU.subtract)
-                for i, (one, two, more) in enumerate((((0, 3), None, ((0, 4, 1), (4, 5, 1))),
-                                                      ((0, 2), (1, 1), ((4, 3, 0), (4, 4, 1), (8, 5, 1))),
-                                                      ((4, 2), (5, 1), ((8, 3, 0), (8, 4, 1))))):
-                    for nm, at in (("s", one), ("S", two)):
-                        if at:
-                            scan("%s%d%d" % (nm, k, i), pair("hb", k, at[0], 3, at[1]), dn(k, 4 * i, 3), pair("hb", k, 0, 3, (5, 3, 2)[i]), ALU.max, ALU.min)
-                    for j, (lo, s, c) in enumerate(more):
-                        cp("x%d%d%d" % (k, i, j), "a", pair("hb", k, lo, 3 - c, s), pair("hb", k, one[0] + c, 3 - c, one[1]))
+                for i, to in enumerate((((0, 3), (-1, 4), (3, 5)), ((0, 2), (1, 1), (4, 3), (3, 4), (7, 5)), ((4, 2), (5, 1), (8, 3), (7, 4)))):
+                    spots = [pair("hb", k, lo, 3, s) for lo, s in to] + [N("hk", 128 + 32 * k + 16 * i + c, 3, 4) for c in (19, 2, 5)]
+                    for j, at in enumerate(spots):
+                        nm = "%d%d%s" % (k, i, "abcdefgh"[j])
+                        if nm[1:] in COPIES:
+                            cp("x" + nm, "a", at, spots[0])
+                        else:
+                            scan("s" + nm, at, dn(k, 4 * i, 3), pair("hb", k, 0, 3, (5, 3, 2)[i]), ALU.max, ALU.min)
                 for i in range(3):
                     lo = b + 28 * i + 7
                     scan("H%d%d" % (k, i), A("ho", lo, lo + 21), A("hb", lo, lo + 21), A("hd", lo, lo + 21))
@@ -367,16 +370,16 @@ def rank_program(g, core, T, topo):
                 for i in range(3):
                     first = N("hk", b + 16 * i + 16 + slot[0], 3, 4)
                     for j, at in enumerate((first, N("hk", b + 16 * i + slot[1], 3, 4), N("hk", b + 16 * i + 4 + slot[2], 3, 4))):
-                        if j and i < (k + 1) // 2:
+                        if j and i == 0 and k == 1:
                             cp("x%d%d%d" % (k, i, j), "a", at, first)
                         else:
                             scan("%s%d%d" % ("sST"[j], k, i), at, dn(k, 4 * i, 3), N("hk", b + 16 * i + slot[0], 3, 4), ALU.max, ALU.min)
-            if k == 0:
-                path = G(A("hb", 0, 64), A("ox", 0, 4))
-                cp("z0", "a", A("zz"), G(A("kl"), A("oz0")))
-                tt("p0", A("pp", 0, 64), path, A("zz"), ALU.mult)
-                act("n0", A("nn", 0, 64), path, ACT.Identity, 1.0, -1.0)
-                scan("o0", A("oo", 0, 64), A("nn", 0, 64), A("pp", 0, 64))
+            for h in range(2 if k == 0 else 0):
+                lo, x = 32 * h, G(A("hb", 0, 35 + 29 * h), A("ox", 2 * h, 2 * h + 2))
+                cp("z0" + "ab"[h], "a", A("zz", lo, lo + 32), G(A("kl"), A("oz0", 2 * h, 2 * h + 2)))
+                tt("p0" + "ab"[h], A("pp", lo, lo + 32), x, A("zz", lo, lo + 32), ALU.mult)
+                act("n0" + "ab"[h], A("nn", lo, lo + 32), x, ACT.Identity, 1.0, -1.0)
+                scan("o0" + "ab"[h], A("oo", lo, lo + 32), A("nn", lo, lo + 32), A("pp", lo, lo + 32))
             for h in range(2 if k == 1 else 0):
                 lo, x = 64 + 32 * h, A("hk", 32 * h, 32 * h + 32)
                 tt("p1" + "ab"[h], A("pp", lo, lo + 32), G(A("oo", 0, 80), A("oz1", 2 * h, 2 * h + 2)), x, ALU.mult)
@@ -394,15 +397,14 @@ def rank_program(g, core, T, topo):
                 act("em2", A("em", 0, 15), ids(2, 0, 15), ACT.Sign, col(6), 1.0)
                 act("r2", A("il", 320, 335), A("em", 0, 15), ACT.Identity, col(7), -8.0)
             if k == 1:
-                tt("j1", A("pj"), G(A("il", 80, 160), A("oz1")), A("hk", 0, 64), ALU.mult)
-                scan("i1", A("il", 160, 224), A("nn", 64, 128), A("pj"))
+                for h, lo in enumerate((0, 32)):
+                    tt("j1" + "ab"[h], A("pj", lo, lo + 32), G(A("il", 80, 160), A("oz1", 2 * h, 2 * h + 2)), A("hk", lo, lo + 32), ALU.mult)
+                    scan("i1" + "ab"[h], A("il", 160 + lo, 192 + lo), A("nn", 64 + lo, 96 + lo), A("pj", lo, lo + 32))
                 continue
             for s, (lo, hi) in enumerate(((0, 4), (4, 1), (1, 0)) if k or r < 2 else ()):
                 tt("A%d%d" % (k, s), N("il", 80 * k + s, 16, 4) if k < 3 else A("hy", s, 64, 4), ids(k, lo), ids(k, hi), ALU.subtract)
             if k < 3:
-                x = A("nn", 128 + 32 * k, 192 + 32 * k)
-                cp("m%d" % k, "a", x, G(A("hb", b, b + 64), A("ox", 4, 8)))
-                scan("i%d" % k, A("il", 80 * k + 80, 80 * k + 144), x, A("il", 80 * k, 80 * k + 64))
+                scan("i%d" % k, A("il", 80 * k + 80, 80 * k + 144), A("hk", 128 + 32 * k, 192 + 32 * k), A("il", 80 * k, 80 * k + 64))
             else:
                 tt("A33", A("hy", 3, 64, 4), ids(3), A("il", 320, 336), ALU.min)
                 scan("i3", A("il", 336, 400), A("hk", 64, 128), A("hy"))

import math
from concourse.mybir import dt, AluOpType, ActivationFunctionType

ALU = AluOpType
ACT = ActivationFunctionType
R = 3
STEP = [3, 6, 4]
LOW = -9.0e29
SWAPS = [(3, 8), (7, 9)]
PICK_F, PICK_V = "vvaa", ["vvaa", "vvaa"]
COPIES = ["0b", "0c", "0d", "0e", "0f", "1e", "1f", "1g", "1h"]
HEAD = {
    "s": "x0 u x1 p ws wc",
    "g": "pc x5 i16 i128 hs0 hs1",
    "v": "eb pc1 xz cf six cf1 mask cf2 e1 ou six0 hq0 vam qu cf3 vas qp hq1 qe3 pa qe0 pb oz qe1 oka qe2 si om",
    "a": "val rst xf val2 xo qp pad hk0 hk1 il0",
    "t": "hk0 hk1",
}
ROUND = {
    "s": "v ol oc0 oc1 os",
    "g": "inv sl s0 s2 s1",
    "v": "km0 km1 kl0 A00 A01 kl1 d0a e01a e02a e03a c0a d0b s00a e04 c0b e01b e02b e03b A02 s01a D0a s01b s01c s01d D0b "
         "s02a s02b H00 s02d p0a s02e s02c H01 s10 p0b s02g s02f o0a H02 s11 S11 T11 o0b i0 T12 S12 s12 p1a j1a p1b o1a j1b i1a o1b "
         "d2a e21a c2a e22a i1b la e23a e24 d2b s20a e22b e21b e23b lb c2b A20 D2a s21a s21b A22 s21c s21d D2b "
         "s22a s22b H20 s22g s22e A21 s22f s22d s22c H21 s30 T30 i2 H22 S30 s31 low S31 T31 A30 A31 A32 A33 T32 s32 S32 i3 i4 sf0 "
         "a2 a0 a3 sf2 a1 g00 g01 f1 f0 q0 sf1 g11 g10 qy sh q1 t00 t00b t01 t02 t03 t10 t11 t12 t13 qt0 okb qt1 "
         "turn zf0 zf1 za2 za0 za1 za3 ot zg00 zg01 zq0 zg11 zg10 zq1 zt00 zt00b zt01 zt02 zt03 zt10 zqt0 zt11 zt12 zt13 zqt1",
    "a": "z0a x00e x00b x00f x00c z0b x01h x01e x01f n0a x01g x00d n0b x102 x101 n1a n1b l3 "
         "x20b x20c x20f em2 x20d x21g x20e r2 x21h x21e x21f u00 u01 u02 u03 u10 u11 u12 u13 "
         "g02 g03 f3 f2 g13 g12 r00 r00b r01 r02 r03 inv1 r10 r11 r12 r13 k0 k1 ilb "
         "zf2 zf3 zg02 zg03 zg13 zg12 o1 zr00 zr00b zr01 zr02 zr03 zr10 zr11 zr12 zr13 yp0 y0d yp1 y1d",
    "t": "u00 u01 u02 u03 u10 u11 u12 u13 r00 r01 r02 r03 r10 r11 r12 r13 k0 k1",
}

CODES = "float8_e4m3fn_x4"
SCRATCH = {}


def _buf(name, n, dtype, where="sbuf"):
    SCRATCH[name] = (where, [128, n], dtype)


for _r in range(R):
    _buf("tw%d" % _r, 1280, "bfloat16")
    _buf("vv%d" % _r, 1024, "bfloat16")
    _buf("dd%d" % _r, 1024, "bfloat16")
    _buf("qvc%d" % _r, 256, CODES)
    _buf("qvs%d" % _r, 256, "uint8")
    _buf("ldc%d" % _r, 256, CODES)
    _buf("lds%d" % _r, 256, "uint8")
    _buf("lso%d" % _r, 4, "uint16")
    _buf("lsi%d" % _r, 4, "uint16")
    _buf("ar%d" % _r, 1024, "float32")
_buf("tw3", 1024, "bfloat16")
for _r in range(R + 1):
    _buf("qtc%d" % _r, 256, CODES)
    _buf("qts%d" % _r, 256, "uint8")
for _n, _w, _d in [
    ("ub", 512, "bfloat16"), ("vb", 512, "bfloat16"), ("pi", 16, "int32"),
    ("quc", 128, CODES), ("qus", 128, "uint8"), ("qpc", 128, CODES), ("qps", 128, "uint8"),
    ("qyc", 128, CODES), ("qys", 128, "uint8"), ("wqc", 512, CODES), ("wqs", 512, "uint8"),
    ("eb", 1032, "bfloat16"), ("qec", 512, CODES), ("qes", 512, "uint8"),
    ("ys", 256, "float32"), ("o1", 256, "float32"),
    ("pc", 4, "int32"), ("cf", 8, "float32"), ("i16", 256, "float32"), ("i128", 128, "float32"), ("x5", 16, "float32"),
    ("mask", 256, "float32"), ("rst", 256, "float32"), ("six", 96, "float32"), ("inv", 320, "float32"),
    ("val", 144, "float32"), ("vam", 144, "float32"), ("vas", 144, "float32"),
    ("si", 48, "int32"), ("sf", 96, "float32"), ("sh", 96, "float32"),
    ("oz0", 4, "uint16"), ("oz1", 4, "uint16"), ("ox", 4, "uint16"), ("ou", 8, "uint16"),
    ("om", 6, "uint16"), ("oka", 16, "uint16"), ("okb", 16, "uint16"), ("ov", 64, "uint16"), ("ot", 16, "uint16"),
    ("pa", 32, "float32"), ("pb", 32, "float32"),
    ("sk", 256, "float32"), ("km", 256, "float32"), ("kl", 320, "float32"), ("il", 464, "float32"),
    ("hb", 224, "float32"), ("he", 224, "float32"), ("hd", 224, "float32"), ("ho", 224, "float32"), ("hk", 256, "float32"), ("hy", 64, "float32"),
    ("zz", 64, "float32"), ("nn", 128, "float32"), ("pp", 128, "float32"), ("oo", 160, "float32"),
    ("pj", 64, "float32"), ("em", 16, "float32"), ("l3", 2, "float32"),
]:
    _buf(_n, _w, _d)
BANK = ["ps%d" % _b for _b in range(8)]
for _n in BANK:
    _buf(_n, 512, "float32", "psum")

DMAS = ["x0", "x1", "u", "p", "wc", "ws", "v", "y0", "y1", "ol", "oc0", "oc1", "os0", "os1", "os2", "os3"]
SEMAPHORES = (["sv", "sa", "st", "sg", "sent"] + ["m_" + n for n in DMAS]
              + ["in%d_%d" % (r, k) for r in range(R) for k in range(4)])


def order(ops):
    lines = {None: [i for i, o in enumerate(ops) if not o[0]]}
    for q in HEAD:
        head, body = HEAD[q].split(), ROUND[q].split()
        mine = [i for i, o in enumerate(ops) if o[0] == q]
        lines[q] = sorted(mine, key=lambda i: (-1, head.index(ops[i][2]), i) if ops[i][2] in head else (ops[i][3], body.index(ops[i][2]), i))
    seq, done = [], set()
    while len(seq) < len(ops):
        before = len(seq)
        for line in lines.values():
            while line and done.issuperset(ops[line[0]][1]):
                done.add(line[0])
                seq.append(line.pop(0))
        assert len(seq) > before, [ops[line[0]][2:4] for line in lines.values() if line]
    return seq


def rank_program(g, core, T, topo):
    rank = T.rank_of(core)
    if rank is None:
        return
    n = len(T.cores)
    queues = {"g": g, "v": g.vector, "a": g.scalar, "t": g.tensor, "s": g.sync}
    own = {"g": "sg", "v": "sv", "a": "sa", "t": "st"}
    ops = []
    log = {}
    now = [0]

    def A(name, lo=0, hi=None, step=1):
        if hi is None:
            hi = SCRATCH[name][1][1]
        ap = T[name][:, lo:hi:step] if step > 1 else T[name][:, lo:hi]
        return (ap, [(name, 0, 512, 1) if SCRATCH[name][0] == "psum" else (name, lo, hi, step)], (hi - lo + step - 1) // step)

    def N(name, lo, count, step):
        return A(name, lo, lo + (count - 1) * step + 1, step)

    def G(win, off, words=False):
        ap = win[0].bitcast(dt.uint32) if words else win[0]
        return (ap.indirect(off[0]), win[1] + off[1], 16 * off[2])

    def regs(xs):
        return [r for x in xs if isinstance(x, tuple) for r in x[1]]

    def raw(x):
        return x[0] if isinstance(x, tuple) else x

    def note(nm, q, outs, ins, call, sem, inc, more=()):
        reads, writes, deps = regs(ins), regs(outs), set(more)
        for rs, wr in ((reads, False), (writes, True)):
            for (name, lo, hi, st) in rs:
                bank = SCRATCH[name][0] == "psum"
                for (l2, h2, s2, w2, i) in log.get(name, []):
                    if (l2 < hi and lo < h2 and (wr or w2 or bank and ops[i][0] != q)
                            and (lo - l2) % max(1, math.gcd(st * (hi - lo > 1), s2 * (h2 - l2 > 1))) == 0):
                        deps.add(i)
        for rs, wr in ((reads, False), (writes, True)):
            for (name, lo, hi, st) in rs:
                old = log.get(name, [])
                if wr:
                    old = [e for e in old if not (lo <= e[0] and e[1] <= hi and (st == 1 or (st == e[2] and (lo - e[0]) % st == 0)))]
                log[name] = old + [(lo, hi, st, wr, len(ops))]
        ops.append((q, sorted(deps), nm, now[0], call, sem, inc))
        return len(ops) - 1

    def run(nm, q, outs, ins, call):
        note(nm, q, outs, ins, lambda: call().then_inc(T.sem[own[q]], 1), own[q], 1)

    V, S = g.vector, g.scalar

    def ts(nm, out, a, s1, op0, s2=None, op1=None):
        if op1 is None:
            run(nm, "v", [out], [a, s1], lambda: V.tensor_scalar(out[0], a[0], raw(s1), None, op0))
        else:
            run(nm, "v", [out], [a, s1, s2], lambda: V.tensor_scalar(out[0], a[0], raw(s1), raw(s2), op0, op1))

    def tt(nm, out, a, b, op):
        run(nm, "v", [out], [a, b], lambda: V.tensor_tensor(out[0], a[0], b[0], op))

    def cp(nm, q, out, a):
        if q == "v":
            run(nm, "v", [out], [a], lambda: V.tensor_copy(out[0], a[0]))
        else:
            run(nm, "a", [out], [a], lambda: S.activation(out[0], a[0], ACT.Copy))

    def act(nm, out, a, func, bias, scale):
        run(nm, "a", [out], [a, bias], lambda: S.activation(out[0], a[0], func, bias=raw(bias), scale=scale))

    def scan(nm, out, d0, d1, op0=ALU.mult, op1=ALU.add):
        run(nm, "v", [out], [d0, d1], lambda: V.tensor_tensor_scan(out[0], d0[0], d1[0], 0.0, op0, op1))

    def fill(nm, out, c):
        run(nm, "v", [out], [], lambda: V.memset(out[0], c))

    def const(nm, out, c):
        act(nm, out, A("i16" if out[2] > 16 else "x5", 0, out[2]), ACT.Identity, c, 0.0)

    def quant(nm, c, s, lo, a):
        oc, osc = A(c, lo, lo + a[2] // 4), A(s, lo, lo + a[2] // 4)
        run(nm, "v", [oc, osc], [a], lambda: V.quantize_mx(oc[0], osc[0], a[0]))

    def mm(nm, bank, wc, ws, wl, c, s, lo, w):
        o, a, b, x, y = A(bank, 0, w), A(wc, wl, wl + 128), A(ws, wl, wl + 128), A(c, lo, lo + w), A(s, lo, lo + w)
        run(nm, "t", [o], [a, b, x, y], lambda: g.tensor.matmul_mx(o[0], a[0], b[0], x[0], y[0], True, True))

    def iota(nm, out, pattern, base, mult, flag=True):
        if flag:
            run(nm, "g", [out], [], lambda: g.iota(out[0], pattern, base, mult, allow_small_or_imprecise_dtypes=True))
        else:
            run(nm, "g", [out], [], lambda: g.iota(out[0], pattern, base, mult))

    def dma(nm, q, name, out, a, more=()):
        note(nm, q, [out], [a], lambda: queues[q].dma_start(raw(out), raw(a)).then_inc(T.sem["m_" + name], 16), "m_" + name, 16, more)

    def u8(x):
        return (x[0].bitcast(dt.uint8),) + x[1:]

    def u32(x):
        return (x[0].bitcast(dt.uint32),) + x[1:]

    def send(nm, r, k, pairs):
        dst = T.cores[(rank + STEP[r]) % n]
        src = T.cores[(rank - STEP[r]) % n]
        rid, pid = topo.addr(dst, core)
        sem = "in%d_%d" % (r, k)
        mine = [note(nm, "g", [], [a], lambda out=out, a=a: g.remote_dma(out[0], a[0], T.sem[sem], T.sem["sent"], pid, rid, topo.mask(core, dst)),
                     "sent", len(topo.engines(core, dst))) for out, a in pairs]
        return note(nm, None, [p[0] for p in pairs], [], None, sem, len(pairs) * len(topo.engines(src, core)), mine)

    def keys_and_send(nm, r, h):
        lo, hi = 128 * h, 128 * h + 128
        mm(nm + "k%d" % h, BANK[h], "qpc", "qps", 0, "qtc%d" % r, "qts%d" % r, lo, 128)
        cp(nm + "k%d" % h, "a", A("sk", lo, hi), A(BANK[h], 0, 128))
        codes = (u8(A("ldc%d" % r, lo, hi)), u8(A("qtc%d" % r, lo, hi)))
        if not r:
            send(nm + "s%d" % h, r, h, [codes, (A("lds%d" % r, lo, hi), A("qts%d" % r, lo, hi))])
            return
        if h:
            send("s2", r, 3, [(A("lds%d" % r), A("qts%d" % r))])
        send("s%d" % h, r, h, [codes])

    def col(j):
        return A("cf", j, j + 1)

    dma("u", "s", "u", A("ub"), T.u[:])
    dma("x0", "s", "x0", A("tw0", 0, 512), T.x[:, 0:512])
    dma("x1", "s", "x1", A("tw0", 512, 1024), T.x[:, 512:1024])
    dma("p", "s", "p", A("pi"), T.p[:])
    dma("wc", "s", "wc", u8(A("wqc")), T.wc[:])
    dma("ws", "s", "ws", A("wqs"), T.ws[:])

    iota("pc", A("pc", 0, 1), [[0, 1]], 0, 1, False)
    iota("x5", A("x5"), [[1, 16]], 0, 0)
    iota("i16", A("i16"), [[0, 16], [1, 16]], 0, 0)
    iota("i128", A("i128"), [[1, 128]], 0, 0)
    fill("xz", A("hb"), 0.0)
    fill("xz", A("hk"), 0.0)
    for lo, step in ((12, 28), (19, 28), (25, 28), (26, 28), (30, 28), (31, 112)):
        const("xo", A("hb", lo, 224, step), 1.0)
    for lo, hi, step in ((0, 64, 4), (1, 64, 4), (67, 256, 4), (14, 47, 16), (78, 111, 16), (142, 175, 16), (206, 239, 16)):
        const("xf", A("hk", lo, hi, step), 1.0)
    fill("eb", A("eb"), 0.0)
    fill("six", A("six"), 1.0)
    fill("six0", A("six", 0, 96, 6), 0.0)
    ts("pc1", A("pc", 1, 2), A("pc", 0, 1), 15, ALU.bitwise_and)
    ts("pc1", A("pc", 2, 3), A("pc", 0, 1), 31, ALU.bitwise_and)
    cp("cf", "v", A("cf", 0, 3), A("pc", 0, 3))
    ts("cf1", A("om", 2, 3), col(1), 7.0, ALU.is_lt, col(2), ALU.add)
    cp("cf", "v", A("om", 4, 5), A("pc", 2, 3))
    ts("mask", A("mask"), A("i16"), col(1), ALU.is_equal)
    ts("ou", A("ou"), A("i16", 0, 8), 16.0, ALU.mult)
    act("rst", A("rst"), A("i16"), ACT.Sign, 0.0, 1.0)
    const("val", A("val", 0, 64, 4), 12.0)
    for s, rows in ((1, (12, 10, 9, 37)), (2, (10, 9, 37, 0)), (3, (3, 8, 36, 0))):
        for i, c in enumerate(rows):
            act("val", N("val", 16 * i + s, 4, 4), A("x5", 0, 4), ACT.Identity, float(c), 0.0 if c in (0, 12) else 7.0)
    for s, c in enumerate((0.0, 1.0, 4.0, 0.0)):
        act("val", A("val", 64 + s, 128, 4), A("x5"), ACT.Identity, c, 1.0)
    act("val", A("val", 128, 144), A("x5"), ACT.Identity, 3.0, 4.0)
    for a, b in SWAPS + [s[::-1] for s in SWAPS]:
        const("val2", A("val", 128 + a, 129 + a), 4.0 * b + 3.0)
    tt("vam", A("vam"), A("val"), A("mask", 0, 144), ALU.mult)
    scan("vas", A("vas"), A("rst", 0, 144), A("vam"))
    cp("om", "v", A("om", 0, 1), A("vas", 143, 144))
    place = N("vas", 79, 4, 16)
    ts("oz", A("oz0"), place, 16.0, ALU.mult, 15.0, ALU.add)
    ts("oz", A("oz1"), place, 4.0, ALU.mult, 3.0, ALU.add)
    cp("oz", "v", A("ox"), N("vas", 15, 4, 16))
    ts("cf2", A("cf", 2, 6), A("i16", 0, 4), 16.0, ALU.mult, col(1), ALU.add)
    ts("cf3", A("cf", 2, 6), A("cf", 2, 6), 256.0, ALU.add)
    const("pad", A("kl", 256, 320), LOW)
    const("pad", A("kl", 0, 16), LOW)
    const("pad", col(6), -255.5)
    act("pad", col(7), col(1), ACT.Identity, 280.0, 1.0)
    const("pad", A("he"), 0.0)
    const("pad", A("il", 0, 80), col(5))
    const("pad", A("oo", 64, 80), LOW)
    const("pad", A("oo", 144, 160), LOW)
    for k in range(1, 4):
        const("pad", A("il", 80 * k + 64, 80 * k + 80), col(5))
    const("pad", A("il", 335, 336), col(2))
    ts("e1", A("eb", 2, 514, 4), A("i128"), col(0), ALU.is_equal)
    ts("e1", A("eb", 519, 1031, 4), A("i128"), col(0), ALU.is_equal)
    for b, o in enumerate((2, 518, 0, 516)):
        quant("qe%d" % b, "qec", "qes", 128 * b, A("eb", o, o + 512))

    quant("qu", "quc", "qus", 0, A("ub"))
    cp("qp", "v", u32(A("qpc")), G(A("quc"), A("ou"), True))
    cp("qp", "a", A("qps"), G(A("qus"), A("ou")))
    for h in range(2):
        quant("hq%d" % h, "qtc0", "qts0", 128 * h, A("tw0", 512 * h, 512 * h + 512))
        keys_and_send("h", 0, h)
    for h in range(2):
        cp("pa", "v", A("pa", 16 * h, 16 * h + 16), A("pi"))
    run("pb", "v", [A("pb")], [A("pa")], lambda: V.transpose(T.pb[:], T.pa[:]))
    turned = G(A("pb"), A("om", 4, 5))
    cp("oka", "v", A("oka"), G(A("pb"), A("om", 2, 3)))
    cp("il0", "a", A("il", 3, 64, 4), turned)
    cp("si", "v", A("si", 0, 16), turned)
    low = A("si", 16, 32)
    ts("low", low, A("si", 0, 16), 15, ALU.bitwise_and)
    ts("low", A("si", 32, 48), A("si", 0, 16), 4, ALU.logical_shift_right)
    ts("sf0", A("sf", 0, 96, 6), low, 16.0, ALU.mult)
    cp("sf0", "v", A("sf", 1, 96, 6), A("si", 32, 48))
    for j, (a, b) in enumerate(SWAPS + [s[::-1] for s in SWAPS]):
        ts("sf%d" % (1 + j // 2), A("sf", 2 + j, 96, 6), low, float(a), ALU.is_equal, 16.0 * (b - a), ALU.mult)
    scan("sh", A("sh"), A("six"), A("sf"))
    cp("okb", "v", A("okb", 0, 7), N("sh", 11, 7, 6))
    cp("okb", "v", A("okb", 8, 16), N("sh", 53, 8, 6))
    now[0] = 1
    iota("inv", A("inv", 0, 256), [[1, 16], [16, 16]], 0, 0)
    iota("inv", A("inv", 256, 320), [[1, 64]], 256, 0)
    for a, b in SWAPS + [s[::-1] for s in SWAPS]:
        act("inv1", A("inv", 16 * a, 16 * a + 16), A("inv", 16 * a, 16 * a + 16), ACT.Identity, float(b - a), 1.0)

    def pair(buf, k, lo, count, slot):
        return N(buf, 56 * k + 7 * (lo + 1) + slot, count, 7)

    def dn(k, lo, count):
        return pair("ho", k - 1, lo, count, 5) if k % 2 else pair("he", k, lo, count, 0)

    def keys(k, lo, count):
        return N("oo", 83 + 4 * lo, count, 4) if k else N("kl", 16 * lo + 15, count, 16)

    def ids(k, lo=0, count=16):
        return N("il", 80 * k + 4 * lo + 3, count, 4)

    for r in range(R):
        now[0] = r
        tw, nxt, vv, ar = "tw%d" % r, "tw%d" % (r + 1), "vv%d" % r, "ar%d" % r
        last = r == R - 1
        for h in range(2):
            lo, hi = (16, 128) if h == 0 else (128, 256)
            tt("km%d" % h, A("km", lo, hi), G(A("sk"), A("oka" if r == 0 else "okb", 8 * h, 8 * h + 7 + h)), A("mask", lo, hi), ALU.mult)
            scan("kl%d" % h, A("kl", lo, hi), A("rst", lo, hi), A("km", lo, hi))
        for h in range(2):
            for b in range(4):
                mm("u%d%d" % (h, b), BANK[4 * (1 - h) + b], "qec", "qes", 128 * b, "ldc%d" % r, "lds%d" % r, 128 * h, 128)
                cp("u%d%d" % (h, b), "a", A("dd%d" % r, 256 * b + 128 * h, 256 * b + 128 * h + 128), A(BANK[4 * (1 - h) + b], 0, 128))
        for k in range(4):
            if k % 2 == 0:
                b = 56 * k
                tt("d%da" % k, dn(k, 0, 3), keys(k, 4, 3), keys(k, 1, 3), ALU.is_gt)
                tt("d%db" % k, dn(k, 4, 7), keys(k, 8, 7), keys(k, 5, 7), ALU.is_gt)
                for s, (lo, hi) in enumerate(((4, 2), (4, 5), (5, 1), (8, 1))):
                    for nm, at, w in (("a", 0, 3), ("b", 4, 7)) if s < 3 else (("", 0, 11),):
                        tt("e%d%d%s" % (k, s + 1, nm), pair("he", k, at, w, 4 - s), keys(k, lo + at, w), keys(k, hi + at, w), ALU.is_gt)
                tt("c%da" % k, pair("he", k, 0, 3, 5), keys(k, 4, 3), keys(k, 1, 3), ALU.is_gt)
                tt("c%db" % k, pair("he", k, 4, 7, 5), keys(k, 8, 7), keys(k, 5, 7), ALU.is_gt)
                for h, (lo, hi) in enumerate(((b + 7, b + 28), (b + 35, b + 84))):
                    tt("D%d%s" % (k, "ab"[h]), A("hd", lo, hi), A("he", lo, hi), A("he", lo + 1, hi + 1), ALU.subtract)
                for i, to in enumerate((((0, 3), (-1, 4), (3, 5)), ((0, 2), (1, 1), (4, 3), (3, 4), (7, 5)), ((4, 2), (5, 1), (8, 3), (7, 4)))):
                    spots = [pair("hb", k, lo, 3, s) for lo, s in to] + [N("hk", 128 + 32 * k + 16 * i + c, 3, 4) for c in (19, 2, 5)]
                    for j, at in enumerate(spots):
                        nm = "%d%d%s" % (k, i, "abcdefgh"[j])
                        if nm[1:] in COPIES:
                            cp("x" + nm, "a", at, spots[0])
                        else:
                            scan("s" + nm, at, dn(k, 4 * i, 3), pair("hb", k, 0, 3, (5, 3, 2)[i]), ALU.max, ALU.min)
                for i in range(3):
                    lo = b + 28 * i + 7
                    scan("H%d%d" % (k, i), A("ho", lo, lo + 21), A("hb", lo, lo + 21), A("hd", lo, lo + 21))
            else:
                b, slot = (0, (1, 2, 3)) if k == 1 else (64, (3, 2, 1))
                for i in range(3):
                    first = N("hk", b + 16 * i + 16 + slot[0], 3, 4)
                    for j, at in enumerate((first, N("hk", b + 16 * i + slot[1], 3, 4), N("hk", b + 16 * i + 4 + slot[2], 3, 4))):
                        if j and i == 0 and k == 1:
                            cp("x%d%d%d" % (k, i, j), "a", at, first)
                        else:
                            scan("%s%d%d" % ("sST"[j], k, i), at, dn(k, 4 * i, 3), N("hk", b + 16 * i + slot[0], 3, 4), ALU.max, ALU.min)
            for h in range(2 if k == 0 else 0):
                lo, x = 32 * h, G(A("hb", 0, 35 + 29 * h), A("ox", 2 * h, 2 * h + 2))
                cp("z0" + "ab"[h], "a", A("zz", lo, lo + 32), G(A("kl"), A("oz0", 2 * h, 2 * h + 2)))
                tt("p0" + "ab"[h], A("pp", lo, lo + 32), x, A("zz", lo, lo + 32), ALU.mult)
                act("n0" + "ab"[h], A("nn", lo, lo + 32), x, ACT.Identity, 1.0, -1.0)
                scan("o0" + "ab"[h], A("oo", lo, lo + 32), A("nn", lo, lo + 32), A("pp", lo, lo + 32))
            for h in range(2 if k == 1 else 0):
                lo, x = 64 + 32 * h, A("hk", 32 * h, 32 * h + 32)
                tt("p1" + "ab"[h], A("pp", lo, lo + 32), G(A("oo", 0, 80), A("oz1", 2 * h, 2 * h + 2)), x, ALU.mult)
                act("n1" + "ab"[h], A("nn", lo, lo + 32), x, ACT.Identity, 1.0, -1.0)
                scan("o1" + "ab"[h], A("oo", lo + 16, lo + 48), A("nn", lo, lo + 32), A("pp", lo, lo + 32))
            if k == 2:
                cp("la", "v", A("lso%d" % r, 0, 3), A("il", 3, 164, 80))
                act("l3", A("l3", 0, 1), ids(2, 1, 1), ACT.Identity, ids(2, 4, 1), -1.0)
                ts("lb", A("lso%d" % r, 3, 4), dn(k, 0, 1), A("l3", 0, 1), ALU.mult, ids(2, 1, 1), ALU.add)
                came = send("sl", r, 2, [(A("lsi%d" % r), A("lso%d" % r))])
                if r == 0:
                    dma("v", "s", "v", A("vb"), T.v[:], [came])
                if r == 1:
                    quant("qy", "qyc", "qys", 0, A("vb"))
                act("em2", A("em", 0, 15), ids(2, 0, 15), ACT.Sign, col(6), 1.0)
                act("r2", A("il", 320, 335), A("em", 0, 15), ACT.Identity, col(7), -8.0)
            if k == 1:
                for h, lo in enumerate((0, 32)):
                    tt("j1" + "ab"[h], A("pj", lo, lo + 32), G(A("il", 80, 160), A("oz1", 2 * h, 2 * h + 2)), A("hk", lo, lo + 32), ALU.mult)
                    scan("i1" + "ab"[h], A("il", 160 + lo, 192 + lo), A("nn", 64 + lo, 96 + lo), A("pj", lo, lo + 32))
                continue
            for s, (lo, hi) in enumerate(((0, 4), (4, 1), (1, 0)) if k or r < 2 else ()):
                tt("A%d%d" % (k, s), N("il", 80 * k + s, 16, 4) if k < 3 else A("hy", s, 64, 4), ids(k, lo), ids(k, hi), ALU.subtract)
            if k < 3:
                scan("i%d" % k, A("il", 80 * k + 80, 80 * k + 144), A("hk", 128 + 32 * k, 192 + 32 * k), A("il", 80 * k, 80 * k + 64))
            else:
                tt("A33", A("hy", 3, 64, 4), ids(3), A("il", 320, 336), ALU.min)
                scan("i3", A("il", 336, 400), A("hk", 64, 128), A("hy"))
        where, e = G(A("il", 336, 400), A("om", 0, 1)), ""
        if last:
            scan("i4", A("il", 400, 464), A("hk", 64, 128), A("hy"))
            twice = N("il", 339, 32, 4)
            run("turn", "v", [A("pb")], [twice], lambda: V.transpose(T.pb[:], twice[0]))
            where, e = turned, "z"
            cp("ot", "v", A("ot"), where)
            cp("o1", "a", A("o1"), G(A("inv"), A("ot")))
            dma("ol", "s", "ol", T.ol[:], (T.o1[0:128:16, :],) + A("o1")[1:])
        for t in range(4):
            ts(e + "a%d" % t, A("ov", 16 * t, 16 * t + 16), where, 4.0, ALU.mult, float(t), ALU.add)
        if r == 0:
            cp("ilb", "a", ids(0), N("sh", 5, 16, 6))
        for b in range(4):
            cp(e + "f%d" % b, PICK_F[b], A(tw, 1024 + b, 1280, 4), G(A("dd%d" % r, 256 * b, 256 * b + 256), A("lsi%d" % r)))
        for h in range(2):
            for t in range(4):
                cp(e + "g%d%d" % (h, t), PICK_V[h][t], A(vv, 512 * h + t, 512 * h + 512, 4),
                   G(A(tw, 0, 1280 if h or last else 1024), A("ov", 8 * h + 16 * t, 8 * h + 16 * t + 8)))
            quant(e + "q%d" % h, "qvc%d" % r, "qvs%d" % r, 128 * h, A(vv, 512 * h, 512 * h + 512))
            for b in range(4):
                mm("r%d%d" % (h, b), BANK[4 * h + b], "wqc", "wqs", 128 * b, "qvc%d" % r, "qvs%d" % r, 128 * h, 128)
                for c, w in ((0, 64), (64, 64)) if h + b == 0 else ((0, 128),):
                    nm, lo, at = "%d%d" % (h, b) + "b" * (c > 0), 512 * h + 128 * b + c, 512 * h + 4 * c + b
                    act(e + "r" + nm, A(ar, lo, lo + w), A(BANK[4 * h + b], c, c + w), ACT.Relu, 0.0, 0.015625)
                    tt(e + "t" + nm, N(nxt, at, w, 4), A(ar, lo, lo + w), N(vv, at, w, 4), ALU.add)
            quant(e + "qt%d" % h, "qtc%d" % (r + 1), "qts%d" % (r + 1), 128 * h, A(nxt, 512 * h, 512 * h + 512))
        if not last:
            for h in range(2):
                keys_and_send("", r + 1, h)

    for h in range(2):
        lo, hi = 128 * h, 128 * h + 128
        dma("oc%d" % h, "s", "oc%d" % h, T.oc[:, 4 * lo:4 * hi], u8(A("qtc3", lo, hi)))
        mm("k%d" % h, BANK[h], "qyc", "qys", 0, "qtc3", "qts3", lo, 128)
        cp("yp%d" % h, "a", A("ys", lo, hi), A(BANK[h], 0, 128))
        dma("y%d" % h + "d", "a", "y%d" % h, T.y[:, lo:hi], A("ys", lo, hi))
    for k in range(4):
        dma("os", "s", "os%d" % k, T.osc[4 * k:4 * k + 4, :], (T.qts3[32 * k:32 * k + 4, :],) + A("qts3")[1:])

    known = {q: {} for q in queues}
    count, seen, token = {}, {}, {}
    for i in order(ops):
        q, deps, call, sem, inc = ops[i][0], ops[i][1], ops[i][4], ops[i][5], ops[i][6]
        if q:
            want = {}
            for d in deps:
                s, v = token[d]
                want[s] = max(want.get(s, 0), v)
            todo = [(s, v) for s, v in want.items() if known[q].get(s, 0) < v]
            for s, v in todo:
                if not any(s2 != s and seen[(s2, v2)].get(s, 0) >= v for s2, v2 in todo):
                    queues[q].wait_ge(T.sem[s], v)
                    for s2, v2 in seen[(s, v)].items():
                        known[q][s2] = max(known[q].get(s2, 0), v2)
            call()
        count[sem] = count.pop(sem, 0) + inc
        token[i] = (sem, count[sem])
        seen[token[i]] = dict(known[q]) if q else {}
        seen[token[i]][sem] = count[sem]
    for s, v in count.items():
        if all(known[q].get(s, 0) < v for q in queues):
            g.wait_ge(T.sem[s], v)
